import numpy as np, ml_dtypes
CORES = [2,3,42,43,82,83,122,123]
N = 8
BF = ml_dtypes.bfloat16
W, B, L, J, VIS, ST = 3584, 2560, 128, 1024, 4, 3
def pick(rng, share, *tail):
    v = rng.integers(0, W, (N, 8) + tail); pool = rng.integers(0, W, (N, 8, 64)); ix = rng.integers(0, 64, (N, 8) + tail)
    h = np.take_along_axis(pool, ix.reshape(N, 8, -1), 2).reshape(v.shape)
    return np.where(rng.random(v.shape) < np.reshape(share, (N, 8) + (1,) * len(tail)), h, v)
def thread(rng, par, share, out):
    ft = np.full((N, 8, J), W, np.int64); a = np.arange(N)[:, None]; g = np.arange(8)[None, :]
    order = B + np.argsort(rng.random((N, 8, J)), axis=-1)
    for s in range(J):
        n = order[:, :, s]; base = rng.integers(0, B, (N, 8)); o = rng.random((N, 8)) < out
        x = np.where(rng.random((N, 8)) < (share if s else 0.0), order[a, g, rng.integers(0, max(s, 1), (N, 8))], base)
        up = par[a, g, x]
        par[a, g, n] = np.where(o, base, up); par[a, g, x] = np.where(o, up, n); ft[a, g, n - B] = np.where(o, W, x)
        v = np.maximum(up - B, 0); cur = ft[a, g, v]
        ft[a, g, v] = np.where(~o & (up >= B) & (cur == x), n, cur)
    return ft
def parts(rng):
    sh = np.array([0.05, 0.1, 0.3, 0.5])
    x = rng.integers(0, 256, (N, 8, 16, W)); kn = np.zeros((N, 8, 16, W), np.int64)
    kn[:, :, 1:] = pick(rng, rng.choice(sh, (N, 8)), 15, W)
    par = np.zeros((N, 8, W), np.int64); par[:, :, :B] = (rng.random((N, 8, B)) * np.arange(B)).astype(np.int64)
    ft = thread(rng, par, rng.choice(np.array([0.2, 0.5, 0.8]), (N, 8)), 0.0625); kn[:, :, 0] = par
    tr = pick(rng, rng.choice(sh, (N, 8)), W); b = pick(rng, rng.choice(sh, (N, 8)), L); z = rng.integers(0, 256, (N, 8, 16, L))
    m = rng.random((N, 8, L)) < 0.08
    oj = B + L * np.arange(N)[:, None, None] + rng.integers(0, L, (N, 8, L))
    near = np.take_along_axis(x, oj[:, :, None, :], 3) + rng.integers(-9, 10, z.shape)
    b = np.where(m, oj, b); z = np.where(m[:, :, None, :], np.minimum(np.maximum(near, 0), 255), z)
    return x, kn, tr, ft, z, b
def pack(x, kn, tr, ft, z, b):
    return {"x0": np.ascontiguousarray(x.reshape(N, 128, W)).astype(np.float32).astype(BF), "kn": np.ascontiguousarray(kn.reshape(N, 128, W)).astype(np.int32), "tr": tr.astype(np.int32),
            "ft": ft.astype(np.int32), "z0": np.ascontiguousarray(z.reshape(N, 128, L)).astype(np.float32).astype(BF), "bs": b.astype(np.int32)}
def setup_inputs(rng):
    return pack(*parts(rng))
def uneven(rng, top, p, *shape):
    return np.minimum((top * rng.random(shape) ** p).astype(np.int64), top - 1)
def setup_inputs_spread(rng):
    x, kn, tr, ft, z, b = parts(rng); ps = np.array([0.25, 0.5, 1.0, 2.0, 4.0, 8.0])
    x = uneven(rng, 256, rng.choice(ps, (N, 8, 1, W)), N, 8, 16, W); z = uneven(rng, 256, rng.choice(ps, (N, 8, 1, L)), N, 8, 16, L)
    k2 = uneven(rng, W, rng.choice(ps, (N, 8, 16, 1)), N, 8, 16, W); kn[:, :, 1:] = k2[:, :, 1:]; kn[:, 1::2, 0] = k2[:, 1::2, 0]
    f2 = uneven(rng, W + 1, rng.choice(ps, (N, 8, 1)), N, 8, J); ft[:, 1::2] = f2[:, 1::2]
    tr = uneven(rng, W, rng.choice(ps, (N, 8, 1)), N, 8, W); b = uneven(rng, W, rng.choice(ps, (N, 8, 1)), N, 8, L)
    return pack(x, kn, tr, ft, z, b)
def two(rng, lo, hi, *shape):
    return np.where(rng.random(shape) < 0.5, lo, hi)
def setup_inputs_ends(rng):
    x, kn, tr, ft, z, b = parts(rng); e = np.array([0, W - 1])
    x = np.where(rng.random((N, 8, 1, W)) < 0.5, two(rng, 0, 255, N, 8, 1, W), two(rng, 0, 255, N, 8, 16, W))
    z = np.where(rng.random((N, 8, 1, L)) < 0.6, two(rng, 0, 255, N, 8, 1, L), two(rng, 0, 255, N, 8, 16, L))
    kn = np.where(rng.random((N, 8, 16, W)) < 0.72, two(rng, 0, W - 1, N, 8, 16, W), kn)
    tr = np.where(rng.random((N, 8, W)) < 0.7, two(rng, 0, W - 1, N, 8, W), tr)
    ft = np.where(rng.random((N, 8, J)) < 0.7, two(rng, 0, W, N, 8, J), ft)
    b = np.where(rng.random((N, 8, L)) < 0.7, two(rng, 0, W - 1, N, 8, L), b)
    s = int(rng.integers(0, 4))
    for q in range(N):
        for g in range(8):
            c = (q + g + s) % 4
            x[q, g, :, 0] = 255 * (c & 1); x[q, g, :, W - 1] = 255 * (c >> 1)
        v = 255 * ((q + s) & 1); w = (q >> 1) & 1
        x[q, 7, :, 0] = v; x[q, 7, :, W - 1] = v
        kn[q, 7][:, e] = two(rng, 0, W - 1, 16, 2); kn[q, 7, 14, e] = 0; kn[q, 7, 15, e] = W - 1
        z[q, 7, :, w::2] = 255 - v; z[q, 7, :, 1 - w::2] = v
        b[q, 7, :] = two(rng, 0, W - 1, L); b[q, 7, L - 2:] = W - 1
        z[q, :, :, L - 1] = np.where(np.arange(8)[:, None] % 2 == q % 2, 0, 255)
        lo = B + L * ((q - 1) % N)
        x[q, 6] = 255 * (q & 1); z[q, 6] = 255 * (q & 1); tr[q, 6] = 0
        kn[q, 6, :, 0] = rng.integers(lo, lo + L, 16); b[q, 6] = np.where(b[q, 6] == 0, W - 1, b[q, 6])
    return pack(x, kn, tr, ft, z, b)
def chain(par, fo, seq, x):
    up = int(par[x]); par[x] = seq[0]; fo[seq[0] - B] = x
    par[seq[:-1]] = seq[1:]; fo[seq[1:] - B] = seq[:-1]; par[seq[-1]] = up
def setup_inputs_corners(rng):
    x, kn, tr, ft, z, b = parts(rng); sh = int(rng.integers(0, 8)); jn = B + np.arange(J); sits = []
    kinj = B + L * rng.integers(0, N, (N, 8, 1, W)) + rng.integers(0, L, (N, 8, 15, W))
    kn[:, :, 1:] = np.where(rng.random((N, 8, 1, W)) < 0.15, kinj, kn[:, :, 1:])
    for q in range(N):
        nx = L * ((q + 1) % N)
        for g in range(8):
            c = (q + g + sh) % 8; par = kn[q, g, 0]; fo = ft[q, g]
            if c == 7: continue
            par[:] = rng.integers(0, B, W); fo[:] = W; p = rng.permutation(B)[:J]
            if c == 0:
                m = rng.random(W) < 0.1; kn[q, g][:, m] = B + L * rng.integers(0, N, (1, W))[:, m] + rng.integers(0, L, (16, W))[:, m]
            if c == 1: chain(par, fo, jn, int(rng.integers(0, B)))
            if c == 2: chain(par, fo, np.ascontiguousarray(jn.reshape(N, L).T).reshape(-1), int(rng.integers(0, B)))
            if c == 3:
                up = par[p].copy(); par[p] = jn; fo[:] = p; par[B:] = up
                if q % 2 == 0: sits.append((q, g, np.arange(L), p[nx:nx + L]))
            if c == 4:
                fo[:] = rng.integers(0, W + 1, J); par[B:] = rng.integers(0, W, J)
                i = int(rng.integers(0, L)); m = L * min(q, N - 2) + i
                fo[m] = W; par[B + m] = rng.integers(0, B); par[W - 1] = B + m
                if q > 0:
                    n = L * q + (i + 1) % (L - 1); y = int(rng.integers(1, B))
                    fo[n] = y; par[y] = B + n; par[B + n] = rng.integers(0, B)
                    fo[0] = B + n; par[B] = B + 1; fo[1] = W; x[q, g, :, B] = 255 * (np.arange(16) % 2)
            if c == 5:
                fo[:] = 0; par[0] = B + rng.integers(0, J); par[B:] = two(rng, 0, B - 1, J)
            if c == 6:
                w = np.arange(J) % 3
                fo[:] = np.where(w == 0, jn, np.where(w == 1, W, p)); par[p[w == 2]] = jn[w == 2]
                par[B:] = np.where(w == 1, jn, np.where(w == 2, B + (np.arange(J) + L) % J, par[B:]))
                ls = rng.permutation(np.nonzero(w[L * q:L * q + L] == 2)[0])[:8]; js = B + nx + ls
                fo[js - B] = js; par[js] = js; sits.append((q, g, ls, js))
    ch = rng.integers(0, 5, (N, 8, L)); ro = B + L * np.arange(N)[:, None, None] + 0 * ch
    b = np.choose(ch, [0 * ch, 0 * ch + W - 1, ro + np.arange(L), ro + rng.integers(0, L, (N, 8, L)), b])
    h = rng.integers(0, 4, (N, 8, W)); tr = np.choose(h, [rng.integers(B, W, (N, 8, W)), two(rng, 0, W - 1, N, 8, W), tr, tr])
    for q, g, i, v in sits:
        b[q, g, i] = v; z[q, g][:, i] = x[q, g][:, v]
    return pack(x, kn, tr, ft, z, b)
def setup_inputs_crowd(rng):
    x, kn, tr, ft, z, b = parts(rng); hs = np.zeros((N, 8), np.int64)
    for q in range(N):
        own = B + L * q
        kn[q, :, 0, own:own + L] = rng.integers(0, B, (8, L)); ft[q, :, L * q:L * q + L] = W
        for g in range(8):
            h = int(rng.integers(1, B - 1)); h2 = h + 1; c = (g + q) % 4; hs[q, g] = h
            if q < 2:
                b[q, g] = h; kn[q, g, :, h] = h; kn[q, g, :, h2] = h2
                if q == 1 and g % 2: b[q, g, int(rng.integers(0, L))] = h2
            elif q == N - 1:
                b[q, g] = W - 1; kn[q, g, 1:, W - 1] = rng.integers(own, own + L, 15)
                up = int(kn[q, g, 0, W - 1]); x[q, g, :, up] = x[q, g, :, W - 1]
            elif q == 2:
                s = rng.permutation(B)[:L]; b[q, g] = s; kn[q, g][:, s] = s
            else: b[q, g] = rng.choice(np.array([0, h, h2, W - 1]), L)
            if c == 0: tr[q, g] = W - 1
            if c == 1: tr[q, g] = two(rng, 0, h, W)
            if c == 2: tr[q, g] = h
    for g in range(8):
        h = int(hs[0, g]); e = (h + 3) % B; e2 = (h + 4) % B
        kn[0, g, :, e] = e2; kn[0, g, :, e2] = e2; x[0, g, :, e2] = x[0, g, :, e]; tr[N - 1, g, W - 1] = e
    for g in (3, 7):
        h = int(hs[0, g]); e = (int(hs[1, g]) + 3) % B; js = B + rng.permutation(L)[:16]
        z[0, g] = 0; x[0, g, :, h] = 0; tr[0, g, h] = e
        x[1, g, :, e] = 255; kn[1, g, :, e] = js; x[1, g][:, js] = 0; ft[1, g, js[0] - B] = W
    return pack(x, kn, tr, ft, z, b)
def setup_inputs_ties(rng):
    x, kn, tr, ft, z, b = parts(rng)
    lo = rng.integers(0, 247, (N, 8, 1, 1)); sp = np.array([1, 2, 4, 9])[(np.arange(8)[None, :] + rng.integers(0, 4, (N, 1))) % 4].reshape(N, 8, 1, 1)
    x = lo + (rng.random((N, 8, 16, W)) * sp).astype(np.int64); z = lo + (rng.random((N, 8, 16, L)) * sp).astype(np.int64)
    x[..., 1::2] = np.where(rng.random((N, 8, 1, W // 2)) < 0.5, x[..., ::2], x[..., 1::2])
    kn[:, :, 9:] = np.where(rng.random((N, 8, 7, W)) < 0.5, kn[:, :, 2:9], kn[:, :, 9:])
    return pack(x, kn, tr, ft, z, b)
def check_inputs(d):
    bad = []
    for k, lo, hi in (("x0", 0, 255), ("kn", 0, W - 1), ("tr", 0, W - 1), ("ft", 0, W), ("z0", 0, 255), ("bs", 0, W - 1)):
        a = np.asarray(d[k]).astype(np.float64)
        if not (np.min(a) >= lo and np.max(a) <= hi): bad.append("range of " + k)
        elif np.any(np.floor(a) != a): bad.append("whole numbers in " + k)
    return bad
def own(v, r):
    return (v >= B + L * r) & (v < B + L * r + L)
def lowest(key):
    return np.argmax(key[:, :, None] == key[:, None, :], axis=2) == np.arange(L)
def reference(x0, kn, tr, ft, z0, bs):
    X = x0.astype(np.float32).astype(np.int32).reshape(N, 8, 16, W); KN = kn.astype(np.int64).reshape(N, 8, 16, W)
    TR = tr.astype(np.int64); FT = ft.astype(np.int64)
    z = z0.astype(np.float32).astype(np.int32).reshape(N, 8, 16, L); b = bs.astype(np.int64); b0 = np.zeros((N, 8, L), np.int64); A = [0] * N
    g = np.arange(8)[:, None]; lane = np.arange(L)
    for t in range(VIS):
        for q in range(N):
            r = (q - t) % N; lo = B + L * r; Xq = X[q]; Kq = KN[q]; par = Kq[:, 0]; fo = FT[q]; zz = z[r].copy(); s = b[r].copy()
            n = lo + lane; y = fo[:, L * r:L * r + L].copy(); u = par[:, lo:lo + L].copy()
            live = ~own(y, r) & ~own(u, r)
            held = live & (y < W) & (par[g, np.minimum(y, W - 1)] == n)
            uj = np.maximum(u - B, 0); turn = held & (u >= B) & (fo[g, uj] == n)
            gi, li = np.nonzero(held); par[gi, y[gi, li]] = u[gi, li]
            gi, li = np.nonzero(turn); fo[gi, uj[gi, li]] = y[gi, li]
            fo[:, L * r:L * r + L] = np.where(live, W, y)
            for step in range(ST):
                c = Kq[g, :, s]
                xc = np.take_along_axis(Xq, c.reshape(8, 1, L * 16), 2).reshape(8, 16, L, 16)
                d = np.where(own(c, r), 2 ** 20, np.add.reduce(np.abs(xc - zz[:, :, :, None]), axis=1))
                k = np.argmin(d, axis=2)[:, :, None]
                best = np.take_along_axis(d, k, 2)[:, :, 0]; cand = np.take_along_axis(c, k, 2)[:, :, 0]
                here = np.add.reduce(np.abs(np.take_along_axis(Xq, s[:, None, :], 2) - zz), axis=1)
                s = np.where(best < here + (A[r] & 31), cand, s)
            may = live & ~own(s, r); seat = may & lowest(np.where(may, s, W + lane))
            xs = np.take_along_axis(Xq, s[:, None, :], 2)
            gi, li = np.nonzero(seat); m = s[gi, li]; nn = lo + li
            cols = Kq[gi, :, m]; up = cols[:, 0].copy()
            hit = (up >= B) & (fo[gi, np.maximum(up - B, 0)] == m)
            Kq[gi, :, nn] = cols; par[gi, m] = nn
            fo[gi[hit], up[hit] - B] = nn[hit]; fo[gi, nn - B] = m
            Xq[gi, :, nn] = (xs[gi, :, li] + zz[gi, :, li]) >> 1
            A[r] = int(np.sum(live & ~seat))
            z[r] = (zz + xs) >> 1; b[r] = s
        if t > 0:
            for q in range(N):
                r = (q - t) % N; o = b0[r]; gi, li = np.nonzero(lowest(o))
                TR[(q - 1) % N][gi, o[gi, li]] = b[r][gi, li]
        b0 = b.copy()
        if t < VIS - 1:
            for q in range(N):
                r = (q - t) % N; b[r] = np.take_along_axis(TR[q], b0[r], 1)
    zq = np.stack([z[(q - VIS + 1) % N] for q in range(N)])
    return {"yk": np.ascontiguousarray(KN[:, :, :, B:]).reshape(N, 128, J).astype(np.float32), "yp": np.ascontiguousarray(KN[:, :, 0, :B]).astype(np.float32), "yf": FT.astype(np.float32),
            "yt": TR.astype(np.float32), "yx": np.ascontiguousarray(X[:, :, :, B:]).reshape(N, 128, J).astype(np.float32).astype(BF), "yz": zq.reshape(N, 128, L).astype(np.float32).astype(BF)}

@@ -1,0 +1,469 @@
+from concourse.mybir import AluOpType as A, ActivationFunctionType as AF
+
+NW, NB, NJ, VIS, ST = 3584, 2560, 1024, 4, 3
+WN = 3856
+DA, DB = 3600, 3728
+WT = 2176.0
+M7, M0C = 1.5 * 2.0 ** 30, 1.5 * 2.0 ** 23
+CH = [(0, 64), (64, 96), (96, 112), (112, 128)]
+PE = {0: (0, 64), 1: (64, 96), 3: (96, 128)}
+BUFS = {
+    "float32": "KN:3856 FX:3856 TT:3856 OT:3856 ID:3584 TRF:224 ML:48 MS:48 COLF:16 CF:128 C15F:128 CGF:128 D:128 B0:128 R:8 IF:128 GI:136 "
+               "PFF:136 R0:272 RS:256 I8:8 J8:8 DUM:40 NN:64 BO:96 BSS:128 NR:1024 VF:1024 FVO:256 CFR:128 FP:16 VM:272 RR:16 FF:16 "
+               "TM:128 TS:128 TB1:8 MU:256 MS1:256 GO:128 GZ:128 UM:128 MU2:256 MS2:256 SQ2:16 NLV:16 CE:16 "
+               "CO:24 OF:32 BLF:8 ZS:128 ZQ:128 VK:256 CND:32 AQ:8 WAQ:4 OR:128",
+    "bfloat16": "X:3856 XW:3584 BT:4096 Z0:128 ZL:384 ZN:512 ZR:2048 RB:8 RB64:8 E:256 HO:256 EM:256 IB:128 ONB:128 WB:16 NU:128 PB:272 "
+                "CK:272 RSB:256 BCB:1024 DIFF:2048 AB:2048 DFB:128 ABB:128 CHB:128 CB8:8 CDE:128 CDO:128 ME:128 MH:128 MX:128 ML2:16 "
+                "EQ:1024 E2:256 H2:256 EM2:256 LA:8",
+    "int32": "KI:3584 FI:1024 BI:128 TRI:224 CI:128 C15:128 CG:128 COLI:4 NI:64 BC:768 AI:4",
+    "uint16": "CL:64 BL:320 KL:128 YL:16 LO:24 VL:8 LS:32 L8:8",
+}
+SCRATCH = {"TD": ("dram", [128, 224], "float32"), "TB": ("dram", [128, 224], "float32"), "TBL": ("dram", [128, 224], "float32"),
+           "BTD": ("dram", [16, 64, 64], "bfloat16")}
+for _d in BUFS:
+    for _b in BUFS[_d].split():
+        SCRATCH[_b.split(":")[0]] = ("sbuf", [128, int(_b.split(":")[1])], _d)
+for _i in range(8):
+    SCRATCH["ps%d" % _i] = ("psum", [128, 512], "float32")
+SEMAPHORES = ["V", "S", "P", "G", "kn0", "kn1", "kn2", "kn3", "lx", "lw", "lf", "lb", "lz", "lt", "btd", "bt", "tt", "tb", "ot", "out",
+              "aT", "aB", "aTB", "loc"] + ["a%s%d" % (k, t) for k in "CZM" for t in range(3)]
+
+
+def rank_program(g, core, T, topo):
+    rank = T.rank_of(core)
+    if rank is None:
+        return
+    cores = T.cores
+    n = len(cores)
+    Q = {"V": g.vector, "S": g.scalar, "P": g.tensor, "G": g, "Y": g.sync}
+    tot, waited, last, readers, excl = {}, {}, {}, {}, {}
+
+    def need(eng, sem, val):
+        val = tot[sem] if val is None else val
+        if waited.get((eng, sem), 0) < val:
+            Q[eng].wait_ge(T.sem[sem], val)
+            waited[(eng, sem)] = val
+
+    def before(eng, rd, wr, ps):
+        for k in rd:
+            if k in last:
+                need(eng, last[k][0], last[k][1])
+        for k in wr:
+            if k in last:
+                need(eng, last[k][0], last[k][1])
+            for s, v in readers.get(k, {}).items():
+                if s != eng:
+                    need(eng, s, v)
+        for k in ps:
+            for s, v in excl.get(k, {}).items():
+                if s != eng:
+                    need(eng, s, v)
+
+    def after(sem, val, rd, wr, ps):
+        for k in rd:
+            readers.setdefault(k, {})[sem] = val
+        for k in wr:
+            last[k] = (sem, val)
+            readers[k] = {}
+        for k in ps:
+            excl.setdefault(k, {})[sem] = val
+
+    def op(eng, fn, rd, wr, ps):
+        rd, wr, ps = rd.split(), wr.split(), ps.split()
+        before(eng, rd, wr, ps)
+        fn().then_inc(T.sem[eng], 1)
+        tot[eng] = tot.get(eng, 0) + 1
+        after(eng, tot[eng], rd, wr, ps)
+
+    def ts(out, in0, s1, op0, s2=None, op1=None, rd="", wr="", ps=""):
+        if op1 is None:
+            op("V", lambda: g.vector.tensor_scalar(out=out, in0=in0, scalar1=s1, scalar2=None, op0=op0), rd, wr, ps)
+        else:
+            op("V", lambda: g.vector.tensor_scalar(out=out, in0=in0, scalar1=s1, scalar2=s2, op0=op0, op1=op1), rd, wr, ps)
+
+    def tt(out, in0, in1, o, rd="", wr="", ps=""):
+        op("V", lambda: g.vector.tensor_tensor(out=out, in0=in0, in1=in1, op=o), rd, wr, ps)
+
+    def cp(out, in_, rd="", wr="", ps=""):
+        op("V", lambda: g.vector.tensor_copy(out=out, in_=in_), rd, wr, ps)
+
+    def scan(out, d0, d1, init, o0, o1, rd="", wr="", ps=""):
+        op("V", lambda: g.vector.tensor_tensor_scan(out=out, data0=d0, data1=d1, initial=init, op0=o0, op1=o1), rd, wr, ps)
+
+    def fill(ap, c, wr):
+        op("V", lambda: g.vector.memset(ap, c), "", wr, "")
+
+    def act(out, in_, f, rd="", wr="", ps="", **kw):
+        op("S", lambda: g.scalar.activation(out=out, in_=in_, func=f, **kw), rd, wr, ps)
+
+    def mm(out, l, r, a, z, rd="", ps=""):
+        op("P", lambda: g.tensor.matmul(out=out, lhsT=l, rhs=r, start=a, stop=z), rd, "", ps)
+
+    def iota(out, pat, base, cm, wr, flag=True):
+        if flag:
+            op("G", lambda: g.iota(out=out, pattern=pat, base=base, channel_multiplier=cm, allow_small_or_imprecise_dtypes=True), "", wr, "")
+        else:
+            op("G", lambda: g.iota(out=out, pattern=pat, base=base, channel_multiplier=cm), "", wr, "")
+
+    def dma(eng, grp, out, in_, rd="", wr=""):
+        rd, wr = rd.split(), wr.split()
+        for k in rd:
+            if k in last:
+                need(eng, last[k][0], last[k][1])
+        for k in wr:
+            if k in last and last[k][0] != grp:
+                need(eng, last[k][0], last[k][1])
+            for s, v in readers.get(k, {}).items():
+                need(eng, s, v)
+        Q[eng].dma_start(out=out, in_=in_).then_inc(T.sem[grp], 16)
+        tot[grp] = tot.get(grp, 0) + 16
+        after(grp, None, rd, wr, [])
+
+    def send(dst, out, in_, sem, rd):
+        before("G", rd.split(), [], [])
+        rid, pid, _ = topo.addr(dst)
+        m = 0
+        for e in topo.engines(core, dst)[:8]:
+            m |= 1 << e
+        g.remote_dma(out, in_, T.sem[sem], T.sem.loc, pid, rid, m)
+        tot["loc"] = tot.get("loc", 0) + 8
+
+    def arrives(sem, key):
+        tot[sem] = 8
+        last[key] = (sem, 8)
+        readers[key] = {}
+
+    nxt, prv = cores[(rank + 1) % n], cores[(rank - 1) % n]
+    lo = [NB + 128 * ((rank - t) % n) for t in range(VIS)]
+    D, RS, DP = T.D[:], T.RS, T.ps7
+    PF, P15, PG, PP, OD, EV, M0, NM0, WA0 = [T.COLF[:, i:i + 1] for i in range(9)]
+    PI, P15I, PGI, PEI = [T.COLI[:, i:i + 1] for i in range(4)]
+
+    for i in (3, 2, 0, 1):
+        dma("Y", "kn%d" % i, T.KI[:, 896 * i:896 * i + 896], T.kn[:, 896 * i:896 * i + 896], wr="KI%d" % i)
+    for p in range(16):
+        dma("S", "lf", T.FI[p::16, :], T.ft[:], wr="FI")
+    dma("S", "lt", T.TRI[:], T.tr[:], wr="TRI")
+    dma("Y", "lx", T.X[:, 0:NW], T.x0[:], wr="XL")
+    for p in range(16):
+        dma("S", "lb", T.BI[p::16, :], T.bs[:], wr="BI")
+    dma("S", "lz", T.Z0[:], T.z0[:], wr="Z0")
+    dma("Y", "lw", T.XW[:], T.x0[:], wr="XW")
+
+    iota(T.NI[0:64, :], [[1, 64]], 0, 64, "NI", False)
+    fill(T.CK[:], 0.0, "CK")
+    iota(T.CK[0:1, :], [[0, 16], [128, 17]], 0, 0, "CK")
+    iota(T.CI[:], [[1, 128]], 0, 0, "CI", False)
+    iota(PI, [[0, 1]], 0, 1, "PI", False)
+    iota(T.CF[:], [[1, 128]], 0, 0, "CF")
+    iota(PF, [[0, 1]], 0, 1, "PF")
+    iota(T.I8[:], [[16, 8]], 0, 0, "I8")
+    iota(T.GI[:], [[17, 8], [1, 17]], 0, 0, "GI")
+    fill(T.BCB[0:64, 768:1024], 0.0, "BCB")
+    for b in range(12):
+        ts(T.BC[0:64, 64 * b:64 * b + 64], T.NI[0:64, :], b, A.arith_shift_right, 1, A.bitwise_and, rd="NI", wr="BC")
+    ts(T.BCB[0:64, 0:768], T.BC[0:64, :], 2.0, A.mult, -1.0, A.add, rd="BC", wr="BCB")
+    for b in range(16):
+        dma("Y", "btd", T.BTD[b], T.BCB[0:64, 64 * b:64 * b + 64], rd="BCB", wr="BTD")
+    for i in range(8):
+        dma("Y", "bt", T.BT[16 * i:16 * i + 16, :], T.BTD[:], rd="BTD", wr="BT")
+    iota(T.FX[:, 0:NB], [[0, NB]], -1, 0, "FXa")
+    ts(P15I, PI, 15, A.bitwise_and, rd="PI", wr="P15I")
+    ts(PGI, PI, 4, A.arith_shift_right, rd="PI", wr="PGI")
+    ts(T.C15[:], T.CI[:], 15, A.bitwise_and, rd="CI", wr="C15")
+    ts(T.CG[:], T.CI[:], 4, A.arith_shift_right, rd="CI", wr="CG")
+    ts(PEI, PI, 4, A.arith_shift_right, 1, A.bitwise_and, rd="PI", wr="PEI")
+    cp(P15, P15I, "P15I", "P15")
+    cp(PG, PGI, "PGI", "PG")
+    cp(T.C15F[:], T.C15[:], "C15", "C15F")
+    cp(T.CGF[:], T.CG[:], "CG", "CGF")
+    cp(OD, PEI, "PEI", "OD")
+    ts(T.D[:], T.C15F[:], P15, A.is_equal, rd="C15F P15", wr="D")
+    ts(M0, P15, 0.0, A.is_equal, rd="P15", wr="M0")
+    ts(NM0, P15, 0.0, A.not_equal, rd="P15", wr="NM0")
+    ts(T.B0[:], T.CGF[:], PG, A.is_equal, M0, A.mult, rd="CGF PG M0", wr="B0")
+    cp(DP[:, 0:128], D, "D", "DP")
+    cp(DP[:, 128:256], D, "D", "DP")
+    fill(T.RS[:], 1.0, "RS")
+    fill(T.RS[:, 0::16], 0.0, "RS")
+    ts(T.J8[:], T.I8[:], P15, A.add, rd="I8 P15", wr="J8")
+    for i, d in enumerate((DA, DA, DB, DA, DA)):
+        ts(T.DUM[:, 8 * i:8 * i + 8], T.J8[:], float(d), A.add, rd="J8", wr="DUM")
+    for t in range(VIS):
+        ts(T.NN[:, 16 * t:16 * t + 8], T.J8[:], float(lo[t]), A.add, rd="J8", wr="NN")
+        ts(T.NN[:, 16 * t + 8:16 * t + 16], T.J8[:], float(lo[t]), A.add, rd="J8", wr="NN")
+        fill(T.BO[:, 24 * t + 16:24 * t + 24], float(lo[t] - DB), "BO")
+        fill(T.BSS[:, 32 * t + 8:32 * t + 16], float(lo[t] - DB), "BSS")
+    fill(T.FX[:, NW:WN], -1.0, "FX")
+    fill(T.KN[:, NW:WN], -1.0, "KN")
+    cp(T.FX[:, NB:NW], T.FI[:], "FI", "FX")
+    cp(T.TRF[:], T.TRI[:], "TRI", "TRF")
+    ts(T.IF[:], T.CF[:], PF, A.is_equal, rd="CF PF", wr="IF")
+    ts(T.R[:], T.CGF[:, 0::16], PG, A.is_equal, rd="CGF PG", wr="R")
+    cp(T.RB[:], T.R[:], "R", "RB")
+    ts(T.RB64[:], T.R[:], 64.0, A.mult, rd="R", wr="RB64")
+    fill(T.RSB[:], 1.0, "RSB")
+    fill(T.RSB[:, 0::16], 0.0, "RSB")
+    ts(T.WB[:, 0:8], T.R[:], WT, A.mult, rd="R", wr="WB")
+    ts(T.WB[:, 8:16], T.R[:], WT, A.mult, rd="R", wr="WB")
+    fill(T.ONB[:], 1.0, "ONB")
+    tt(PP, PF, PG, A.add, "PF PG", "PP0")
+    ts(PP, PP, 1.0, A.add, rd="PP0", wr="PP")
+    ts(T.PB[:, 0:136], T.GI[:], PP, A.is_equal, 1.0 / 64, A.mult, rd="GI PP", wr="PB")
+    ts(T.PB[:, 136:272], T.GI[:], PP, A.is_equal, -1.0, A.mult, rd="GI PP", wr="PB")
+    ts(T.PFF[:], T.GI[:], PP, A.is_equal, rd="GI PP", wr="PFF")
+    fill(T.CK[32:33, 0:136], -161.0, "CK")
+    fill(T.CK[32:33, 136:272], 8192.0, "CK")
+    fill(T.CK[64:65, 136:272], 32.0, "CK")
+    fill(T.CK[32:33, 0::17], 0.0, "CK")
+    fill(T.CK[64:65, 0::17], 0.0, "CK")
+    fill(T.R0[:], -1.0e9, "R0")
+    fill(T.R0[:, 0::17], 1.0e9, "R0")
+    fill(T.E[:], 0.0, "E")
+    fill(WA0, 0.0, "WA0")
+    send(nxt, T.TD[:], T.TRF[:], "aT", "TRF")
+    arrives("aT", "TD")
+    last["XWp"] = last["XW"]
+
+    def constants3(part):
+        if part == 0:
+            iota(T.ID[:], [[1, NW]], 0, 0, "ID")
+            ts(T.IB[:], T.CF[:], PF, A.is_equal, rd="CF PF", wr="IB")
+            ts(EV, OD, 0.0, A.is_equal, rd="OD", wr="EV")
+            ts(T.NU[:], T.CF[:], PF, A.is_le, -32.0, A.mult, rd="CF PF", wr="NU")
+        elif part == 1:
+            fill(T.ME[:], 0.0, "ME")
+            fill(T.E2[:], 0.0, "E2")
+            fill(T.ML2[:], 1.0, "ML2")
+            fill(T.NR[:], 0.0, "NR")
+            fill(T.MS[:], 0.0, "MS")
+            fill(T.X[:, NW:WN], 0.0, "XL")
+            fill(T.TT[:, NW:WN], 0.0, "TT")
+        else:
+            for t in range(VIS):
+                ts(T.NR[:, 256 * t:256 * t + 128], T.CF[:], float(lo[t]), A.add, M0, A.mult, rd="CF M0", wr="NR")
+                ts(T.VF[:, 256 * t + 128:256 * t + 256], T.CF[:], float(lo[t]), A.add, rd="CF", wr="VFr")
+            for p in range(16):
+                dma("Y", "tt", T.TT[p::16, 0:NW], T.TD[:], rd="TD", wr="TTd")
+
+    def kwin():
+        return T.KN[:, 0:WN]
+
+    def convert(*ii):
+        for i in ii:
+            cp(T.KN[:, 896 * i:896 * i + 896], T.KI[:, 896 * i:896 * i + 896], "KI%d" % i, "KN")
+
+    def out(t, mid, mid2=None):
+        a, z = lo[t], lo[t] + 128
+        mm(T.ps2[:, 0:128], T.B0[:], T.KN[:, a:z], True, True, "B0 KN", "ps2")
+        tt(T.MU[:, 0:128], T.FX[:, a:z], DP[:, 0:128], A.mult, "FX DP", "MUa")
+        act(T.FVO[:, 0:128], T.FX[:, a:z], AF.Copy, "FX", "FVO")
+        act(T.UM[:], T.KN[:, a:z], AF.Copy, "KN M0", "UM", scale=M0)
+        mid()
+        tt(T.MU[:, 128:256], T.ps2[:, 0:128], D, A.mult, "D", "MUb", "ps2")
+        scan(T.MS1[:], RS[:], T.MU[:], 0.0, A.mult, A.add, "RS MUa MUb", "MS1")
+        cp(T.YL[:], T.MS1[:, 15::16], "MS1", "YL")
+        if mid2:
+            mid2()
+        act(T.GO[:], kwin().indirect(T.YL[:, 0:8]), AF.Copy, "KN YL", "GO")
+        mm(T.ps2[:, 0:128], T.B0[:], T.GO[:], True, True, "B0 GO", "ps2")
+        act(T.SQ2[:], T.MS1[:, 15::16], AF.Square, "MS1", "SQ2", bias=-a - 63.5)
+        act(T.GZ[:], T.GO[:], AF.Copy, "GO NM0", "GZ", scale=NM0)
+        tt(T.MU2[:, 128:256], T.FX[:, 0:WN].indirect(T.YL[:, 8:16]), D, A.mult, "FX FXa YL D", "MU2b")
+        tt(T.BO[:, 24 * t:24 * t + 16], T.MS1[:, 15::16], T.DUM[:, 0:16], A.subtract, "MS1 DUM", "BO")
+        ts(T.NLV[:], T.SQ2[:], 4096.0, A.is_ge, rd="SQ2", wr="NLV")
+        tt(T.CO[:, 16:24], T.NLV[:, 0:8], T.NLV[:, 8:16], A.mult, "NLV", "COc")
+        tt(T.MU2[:, 0:128], T.ps2[:, 0:128], D, A.mult, "D", "MU2a", "ps2")
+        scan(T.MS2[:], RS[:], T.MU2[:], 0.0, A.mult, A.add, "RS MU2a MU2b", "MS2")
+        tt(T.CE[:], T.MS2[:, 15::16], T.NN[:, 16 * t:16 * t + 16], A.is_equal, "MS2 NN", "CE")
+        tt(T.CO[:, 0:8], T.CE[:, 0:8], T.CO[:, 16:24], A.mult, "CE COc", "COa")
+        tt(T.CO[:, 8:16], T.CE[:, 8:16], T.CO[:, 0:8], A.mult, "CE COa", "COb")
+        tt(T.OF[:, 0:24], T.CO[:], T.BO[:, 24 * t:24 * t + 24], A.mult, "COa COb COc BO", "OF")
+        tt(T.OF[:, 0:24], T.OF[:, 0:24], T.DUM[:, 0:24], A.add, "OF DUM", "OF")
+        cp(T.LO[:], T.OF[:, 0:24], "OF", "LO")
+        tt(kwin().indirect(T.LO[:, 0:8]), T.GZ[:], T.UM[:], A.add, "LO GZ UM", "KN")
+
+    def start(t, rows, rkey):
+        tt(T.TM[:], rows, D, A.mult, rkey + " D", "TM")
+        scan(T.TS[:], RS[:, 0:128], T.TM[:], 0.0, A.mult, A.add, "RS TM", "TS")
+        cp(T.BL[:, 64 * t:64 * t + 8], T.TS[:, 15::16], "TS", "BL%d" % (4 * t))
+        mm(T.ps6[:, 0:8], T.TM[:], T.R[:], True, True, "TM R", "ps6")
+        act(T.CB8[:], T.ps6[:, 0:8], AF.Identity, "", "CB8", "ps6", bias=8224.5)
+
+    def zrep(zz, key):
+        for k in range(16):
+            act(T.ZR[:, k::16], zz, AF.Copy, key, "ZR")
+
+    def step(t, s, zz, zkey, wa, wkey, gap):
+        q = 4 * t + s
+        bl, bk = T.BL[:, 16 * q:16 * q + 8], "BL%d" % q
+        vb, vk = (T.ps0, "ps0") if q % 2 == 0 else (T.ps1, "ps1")
+
+        def stay(f, k):
+            act(T.FP[:], f, AF.Identity, k + wkey, "FP", bias=wa)
+            mm(vb[:, 0:272:17], T.IF[:], T.FP[:], False, False, "IF FP", vk)
+
+        mm(vb[:, 0:272], T.ONB[:], T.CK[:], True, False, "ONB CK", vk)
+        cp(T.KL[:], kwin().indirect(bl), "KN " + bk, "KL")
+        act(T.CFR[:], kwin().indirect(bl), AF.Copy, "KN " + bk, "CFR")
+        act(T.CHB[:], T.CFR[:], AF.Identity, "CFR", "CHB", bias=8224.5)
+        mm(vb[:, 136:272], T.CFR[:], T.PFF[:], False, False, "CFR PFF", vk)
+        if s:
+            stay(T.E[:, 0::16], "E ")
+        for c, (a, z) in enumerate(CH):
+            tt(T.DIFF[:, 16 * a:16 * z], T.XW[:].indirect(T.KL[:, a:z]), T.ZR[:, 16 * a:16 * z], A.subtract, "XW XWp KL ZR", "DF%d" % c)
+            act(T.AB[:, 16 * a:16 * z], T.DIFF[:, 16 * a:16 * z], AF.Abs, "DF%d" % c, "AB%d" % c)
+            if c in PE:
+                a, z = PE[c]
+                for k in range(16):
+                    mm(vb[a:z, k + 1:272:17], T.AB[:, 16 * a + k:16 * z:16], T.WB[:], False, False, "AB%d AB%d WB" % (c, c - (c == 3)), vk)
+        tt(T.DFB[:], T.X[:, 0:NW].indirect(bl), zz, A.subtract, "X XL " + bk + " " + zkey, "DFB")
+        act(T.ABB[:], T.DFB[:], AF.Abs, "DFB", "ABB")
+        if s == 0:
+            tt(T.TB1[:], T.ps6[:, 0:8], T.CB8[:], A.subtract, "CB8", "TB1", "ps6")
+            act(T.FF[:, 0:8], T.CB8[:], AF.Identity, "CB8", "FF", scale=1.0 / 64, bias=-161.0)
+            act(T.FF[:, 8:16], T.TB1[:], AF.Identity, "TB1", "FF", bias=8224.0)
+        gap()
+        mm(vb[:, 0:272:17], T.ABB[:], T.WB[:], False, False, "ABB WB", vk)
+        if s == 0:
+            stay(T.FF[:], "FF ")
+        mm(vb[:, 0:272], T.CHB[:], T.PB[:], False, True, "CHB PB", vk)
+        scan(T.VM[:], T.R0[:], vb[:, 0:272], 1.0e9, A.max, A.min, "R0", "VM", vk)
+        ts(T.RR[:], T.VM[:, 16::17], M7, A.add, M7, A.subtract, rd="VM", wr="RR")
+        tt(T.E[:, 0::16], T.VM[:, 16::17], T.RR[:], A.subtract, "VM RR", "E")
+        scan(T.HO[:], T.RSB[:], T.E[:], 0.0, A.mult, A.add, "RSB E", "HO")
+        tt(T.EM[:], T.HO[:], DP[:, 0:256], A.mult, "HO DP", "EM")
+        mm(T.ps6[:, 0:8], T.EM[:, 0:128], T.RB64[:], True, False, "EM RB64", "ps6")
+        mm(T.ps6[:, 0:8], T.EM[:, 128:256], T.RB[:], False, True, "EM RB", "ps6")
+        ts(T.BL[:, 16 * q + 16:16 * q + 24], T.ps6[:, 0:8], 2080.0, A.add, wr="BL%d" % (q + 1), ps="ps6")
+
+    def seat(t, zz, zkey):
+        fin = t == VIS - 1
+        a = lo[t]
+        q = 4 * t + 3
+        bl, bk = T.BL[:, 16 * q:16 * q + 8], "BL%d" % q
+        zn, znk = T.ZN[:, 128 * t:128 * t + 128], "ZN%d" % t
+        vf = T.VF[:, 256 * t:256 * t + 256]
+        if fin:
+            send(prv, T.CL[:, 48:56], bl, "aB", bk)
+        else:
+            send(nxt, T.CL[:, 16 * t:16 * t + 8], bl, "aC%d" % t, bk)
+        act(T.VK[:, 128:256], kwin().indirect(bl), AF.Copy, "KN " + bk, "VKb")
+        mm(T.ps2[:, 0:128], T.B0[:], T.VK[:, 128:256], True, True, "B0 VKb", "ps2")
+        act(T.CDE[:], T.BT[:].indirect(bl), AF.Copy, "BT EV " + bk, "CDE", scale=EV)
+        act(T.CDO[:], T.BT[:].indirect(bl), AF.Copy, "BT OD " + bk, "CDO", scale=OD)
+        ts(T.BLF[:], T.ps6[:, 0:8], 2080.0, A.add, wr="BLF", ps="ps6")
+        act(T.SQ2[:, 0:8], T.BLF[:], AF.Square, "BLF", "SQ2", bias=-a - 63.5)
+        for h in range(2):
+            ps, pk = (T.ps3, "ps3") if h == 0 else (T.ps4, "ps4")
+            for i in range(4):
+                gr = 4 * h + i
+                r = 32 * (gr // 2)
+                cd, ck = (T.CDE, "CDE") if gr % 2 == 0 else (T.CDO, "CDO")
+                mm(ps[:, 128 * i:128 * i + 128], T.IB[:], T.NU[:], True, False, "IB NU", pk)
+                if i == 2:
+                    need("P", "P", tot["P"])
+                mm(ps[:, 128 * i:128 * i + 128], cd[r:r + 32, :], cd[r:r + 32, :], False, True, ck, pk)
+            act(T.EQ[:, 512 * h:512 * h + 512], ps[:], AF.Relu, "", "EQ%d" % h, pk, bias=-11.0)
+        tt(T.ZS[:], T.X[:, 0:NW].indirect(bl), zz, A.add, "X XL " + bk + " " + zkey, "ZS")
+        ts(T.ZQ[:], T.ZS[:], 0.4999, A.mult, M0C, A.add, rd="ZS", wr="ZQ")
+        ts(zn, T.ZQ[:], -M0C, A.add, rd="ZQ", wr=znk)
+        if not fin:
+            send(nxt, T.ZL[:, 128 * t:128 * t + 128], zn, "aZ%d" % t, znk)
+        tt(T.MU[:, 0:128], T.ps2[:, 0:128], D, A.mult, "D", "MUa", "ps2")
+        scan(T.MS1[:, 0:128], RS[:, 0:128], T.MU[:, 0:128], 0.0, A.mult, A.add, "RS MUa", "MS1")
+        ts(T.NLV[:, 0:8], T.SQ2[:, 0:8], 4096.0, A.is_ge, rd="SQ2", wr="NLV")
+        cp(T.VL[:], T.MS1[:, 15:128:16], "MS1", "VL")
+        tt(T.ME[:, 0::16], T.NLV[:, 0:8], T.CO[:, 16:24], A.mult, "NLV COc", "ME")
+        scan(T.MH[:], T.RSB[:, 0:128], T.ME[:], 0.0, A.mult, A.add, "RSB ME", "MH")
+        tt(T.MU2[:, 0:128], T.FX[:, 0:WN].indirect(T.VL[:]), D, A.mult, "FX FXa VL D", "MU2a")
+        tt(T.MX[:], T.MH[:], DP[:, 0:128], A.mult, "MH DP", "MX")
+        mm(T.ps5[:, 0:8], T.MX[:], T.RB[:], True, True, "MX RB", "ps5")
+        scan(T.MS2[:, 0:128], RS[:, 0:128], T.MU2[:, 0:128], 0.0, A.mult, A.add, "RS MU2a", "MS2")
+        cp(T.ML2[:, 0:8], T.ps5[:, 0:8], "", "ML2", "ps5")
+        act(vf[:, 0:128], T.ID[:].indirect(bl), AF.Copy, "ID " + bk, "VF%d" % t)
+        act(T.VK[:, 0:128], T.VK[:, 128:256], AF.Copy, "VKb NM0", "VKa", scale=NM0)
+        for gr in range(8):
+            mm(T.ps5[:, 16 + gr:32:8], T.EQ[:, 128 * gr:128 * gr + 128], T.ML2[:, gr::8], True, True, "EQ%d ML2" % (gr // 4), "ps5")
+        tt(T.CE[:, 0:8], T.MS2[:, 15:128:16], T.BLF[:], A.is_equal, "MS2 BLF", "CE")
+        b0 = 32 * t
+        tt(T.BSS[:, b0:b0 + 8], T.BLF[:], T.DUM[:, 0:8], A.subtract, "BLF DUM", "BSS")
+        tt(T.BSS[:, b0 + 16:b0 + 24], T.MS1[:, 15:128:16], T.DUM[:, 0:8], A.subtract, "MS1 DUM", "BSS")
+        tt(T.BSS[:, b0 + 24:b0 + 32], T.BLF[:], T.DUM[:, 0:8], A.subtract, "BLF DUM", "BSS")
+        if t in (1, 2):
+            cp(T.L8[:], T.ML[:, 16 * (t - 1):16 * (t - 1) + 8], "M%d" % (t - 1), "L8")
+            cp(T.TT[:].indirect(T.L8[:]), vf[:, 0:128], "L8 VF%d" % t, "TT TTd")
+        ts(T.E2[:, 0::16], T.ps5[:, 16:32], 0.0, A.is_equal, rd="", wr="E2", ps="ps5")
+        scan(T.H2[:], T.RSB[:], T.E2[:], 0.0, A.mult, A.add, "RSB E2", "H2")
+        tt(T.EM2[:], T.H2[:], DP[:, 0:256], A.mult, "H2 DP", "EM2")
+        mm(T.ps5[:, 32:40], T.EM2[:, 0:128], T.RB[:], True, True, "EM2 RB", "ps5")
+        mm(T.ps5[:, 40:48], T.EM2[:, 128:256], T.RB[:], True, True, "EM2 RB", "ps5")
+        tt(T.CND[:, 0:8], T.ps5[:, 32:40], T.ME[:, 0::16], A.mult, "ME", "CN0", "ps5")
+        tt(T.CND[:, 8:16], T.ps5[:, 32:40], T.ME[:, 0::16], A.mult, "ME", "CN1", "ps5")
+        cp(T.CND[:, 24:32], T.ps5[:, 40:48], "", "CN3", "ps5")
+        tt(T.CND[:, 16:24], T.CE[:, 0:8], T.CND[:, 0:8], A.mult, "CE CN0", "CN2")
+        if not fin:
+            tt(T.LA[:], T.CO[:, 16:24], T.CND[:, 0:8], A.subtract, "COc CN0", "LA")
+            mm(T.ps5[:, 48:56], T.ONB[:], T.LA[:], True, True, "ONB LA", "ps5")
+        tt(T.OF[:], T.CND[:], T.BSS[:, b0:b0 + 32], A.mult, "CN0 CN1 CN2 CN3 BSS", "OF")
+        tt(T.OF[:], T.OF[:], T.DUM[:, 8:40], A.add, "OF DUM", "OF")
+        cp(T.LS[:], T.OF[:], "OF", "LS")
+        if not fin:
+            m0 = 16 * t
+            cp(T.MS[:, m0:m0 + 8], T.OF[:, 24:32], "OF", "MS")
+            act(T.AQ[:], T.ps5[:, 48:56], AF.Copy, "", "AQ MSa", "ps5", accum_out=T.MS[:, m0 + 8:m0 + 9])
+            send(nxt, T.ML[:, m0:m0 + 16], T.MS[:, m0:m0 + 16], "aM%d" % t, "MS MSa")
+            if t == 2:
+                cp(T.L8[:], T.OF[:, 24:32], "OF", "L8")
+            arrives("aC%d" % t, "CL%d" % t)
+            arrives("aZ%d" % t, "ZL%d" % t)
+            arrives("aM%d" % t, "M%d" % t)
+            zrep(T.ZL[:, 128 * t:128 * t + 128], "ZL%d" % t)
+        tt(kwin().indirect(T.LS[:, 0:16]), T.VK[:], T.NR[:, 256 * t:256 * t + 256], A.add, "LS VKa VKb NR", "KN")
+        cp(T.FX[:, 0:WN].indirect(T.LS[:, 8:24]), vf, "LS VF%d VFr" % t, "FX")
+        cp(T.X[:].indirect(T.LS[:, 8:16]), zn, "LS " + znk, "X XL")
+        if not fin:
+            act(T.XW[:, a:a + 128], T.X[:, a:a + 128], AF.Copy, "X", "XW")
+
+    def gap(t, s):
+        if t == 0:
+            constants3(s)
+        elif s == 0:
+            cp(T.AI[:, 0:1], T.ML[:, 16 * t - 8:16 * t - 7], "M%d" % (t - 1), "AI0")
+            ts(T.AI[:, 1:2], T.AI[:, 0:1], 31, A.bitwise_and, rd="AI0", wr="AI1")
+            ts(T.WAQ[:, 0:1], T.AI[:, 1:2], WT, A.mult, rd="AI1", wr="WA")
+        if s == 0:
+            cp(T.FX[:, 0:WN].indirect(T.LO[:, 8:24]), T.FVO[:], "LO FVO FVOr", "FX")
+
+    fill(T.FVO[:, 128:256], float(NW), "FVOr")
+    zrep(T.Z0[:], "Z0")
+    convert(3, 2)
+    out(0, lambda: start(0, T.BI[:], "BI"), lambda: convert(0, 1))
+    fill(T.XW[:, lo[0]:lo[0] + 128], 4096.0, "XWp")
+    for t in range(VIS):
+        if t == 0:
+            zz, zkey, wa, wkey = T.Z0[:], "Z0", WA0, "WA0"
+        else:
+            zz, zkey, wa, wkey = T.ZL[:, 128 * t - 128:128 * t], "ZL%d" % (t - 1), T.WAQ[:, 0:1], "WA"
+        for s in range(ST):
+            step(t, s, zz, zkey, wa, wkey, lambda: gap(t, s))
+        seat(t, zz, zkey)
+        if t == 2:
+            dma("Y", "tb", T.TB[:], T.TT[0::16, 0:NW], rd="TT", wr="TB")
+            send(prv, T.TBL[:], T.TB[:], "aTB", "TB")
+            arrives("aTB", "TBL")
+            dma("Y", "ot", T.OT[0::16, 0:NW], T.TBL[:], rd="TBL", wr="OT")
+        if t < VIS - 1:
+            fill(T.XW[:, lo[t + 1]:lo[t + 1] + 128], 4096.0, "XWp")
+            out(t + 1, lambda: start(t + 1, T.TT[:].indirect(T.CL[:, 16 * t:16 * t + 8]), "TT TTd CL%d" % t))
+    arrives("aB", "CLB")
+    act(T.OR[:], T.ID[:].indirect(T.CL[:, 48:56]), AF.Copy, "ID CLB", "OR")
+    dma("Y", "out", T.yz[:], T.ZN[:, 384:512], rd="ZN3")
+    dma("S", "out", T.yk[:], T.KN[:, NB:NW], rd="KN")
+    dma("Y", "out", T.yp[:], T.KN[0::16, 0:NB], rd="KN")
+    dma("S", "out", T.yf[:], T.FX[0::16, NB:NW], rd="FX")
+    dma("Y", "out", T.yx[:], T.X[:, NB:NW], rd="X")
+    cp(T.OT[:].indirect(T.L8[:]), T.OR[:], "L8 OR", "OT")
+    dma("Y", "out", T.yt[:], T.OT[0::16, 0:NW], rd="OT")
+    for s in list(tot):
+        need("G", s, tot[s])

@@ -3,30 +3,40 @@ from concourse.mybir import AluOpType as A, ActivationFunctionType as AF
 NW, NB, NJ, VIS, ST = 3584, 2560, 1024, 4, 3
 WN = 3856
 DA, DB = 3600, 3728
-WT = 2176.0
-M7, M0C = 1.5 * 2.0 ** 30, 1.5 * 2.0 ** 23
-CH = [(0, 64), (64, 96), (96, 112), (112, 128)]
-PE = {0: (0, 64), 1: (64, 96), 3: (96, 128)}
+WT, SL = 131072.0, 4096
+BIG = 4096.0
+OFS = 1792.0
+M0C = 1.5 * 2.0 ** 23
+EPS = 2.0 ** -20
+CUTS = (0, 28, 40, 52, 64)
+LISTS = "y1 po1 por sq1 sqr squ pnu ne pe pen d1 s1 nc0 oy0 nch oy dead bov m1 e3 m2 ofv bou held h1 e1 h2 ofu dum dumo sq3".split()
 BUFS = {
-    "float32": "KN:3856 FX:3856 TT:3856 OT:3856 ID:3584 TRF:224 ML:48 MS:48 COLF:16 CF:128 C15F:128 CGF:128 D:128 B0:128 R:8 IF:128 GI:136 "
-               "PFF:136 R0:272 RS:256 I8:8 J8:8 DUM:40 NN:64 BO:96 BSS:128 NR:1024 VF:1024 FVO:256 CFR:128 FP:16 VM:272 RR:16 FF:16 "
-               "TM:128 TS:128 TB1:8 MU:256 MS1:256 GO:128 GZ:128 UM:128 MU2:256 MS2:256 SQ2:16 NLV:16 CE:16 "
-               "CO:24 OF:32 BLF:8 ZS:128 ZQ:128 VK:256 CND:32 AQ:8 WAQ:4 OR:128",
-    "bfloat16": "X:3856 XW:3584 BT:4096 Z0:128 ZL:384 ZN:512 ZR:2048 RB:8 RB64:8 E:256 HO:256 EM:256 IB:128 ONB:128 WB:16 NU:128 PB:272 "
-                "CK:272 RSB:256 BCB:1024 DIFF:2048 AB:2048 DFB:128 ABB:128 CHB:128 CB8:8 CDE:128 CDO:128 ME:128 MH:128 MX:128 ML2:16 "
-                "EQ:1024 E2:256 H2:256 EM2:256 LA:8",
-    "int32": "KI:3584 FI:1024 BI:128 TRI:224 CI:128 C15:128 CG:128 COLI:4 NI:64 BC:768 AI:4",
-    "uint16": "CL:64 BL:320 KL:128 YL:16 LO:24 VL:8 LS:32 L8:8",
+    "float32": "KN:3856 FX:3856 TT:3856 OT:3856 ID:3584 TRF:224 ML:48 MS:48 COLF:16 CF:160 C15F:128 CGF:128 D:128 B0:128 IF:128 RG8:128 "
+               "R0:68 RS:128 I8:8 J8:8 NN:32 NR:1024 VF:1024 FVO:128 TM:128 TS:128 MU:128 MS1:128 GZ:128 UM:128 "
+               "MU2:128 MS2:128 MS3:128 MV:128 SM:256 AQ:8 OR:128 VM:136 GG:136 BB:136 SC:136 ZQ:128 "
+               "SND:408 LND:408 BF8:128 RPI:128 CMP:16 MUL:16 E2:16 T2:32 S2:16 OO:16",
+    "bfloat16": "X:3856 XW:3584 BT:4096 Z0:128 ZN:128 ZR:2048 IB:128 NIB:128 ONB:128 BON:128 SW:144 CK:204 CW:4 CA:4 BCB:1024 DIFF:2048 "
+                "XB:128 CDE:128 CDO:128 LIVE:16 LX:128 SN:8 NL:8 PO:8 NUA:512 NUB:128 RG:512 RP:128",
+    "float16": "C16:128 C2:256 IE:160 IO:160 RH8:128 F16:1024",
+    "int32": "KI:3584 FI:1024 BI:128 TRI:224 CI:128 C15:128 CG:128 COLI:4 NI:64 BC:768 AI:8 C8I:8",
+    "uint16": "CL:16 BL:256 KL:128 YL:16 LO:16 VL:8 LS:16 LN:16 L8:8 C8:8",
 }
 SCRATCH = {"TD": ("dram", [128, 224], "float32"), "TB": ("dram", [128, 224], "float32"), "TBL": ("dram", [128, 224], "float32"),
-           "BTD": ("dram", [16, 64, 64], "bfloat16")}
+           "BTD": ("dram", [16, 64, 64], "bfloat16"),
+           "AB": ("sbuf", [128, 128, 17], "bfloat16"), "EQ": ("sbuf", [128, 8, 128], "bfloat16"), "CT": ("sbuf", [128, 4, 32], "float16"),
+           "CT2": ("sbuf", [128, 8, 32], "float16"), "VK": ("sbuf", [128, 2, 128], "float32"), "BN": ("sbuf", [128, 2, 16], "float32"),
+           "OF": ("sbuf", [128, 2, 16], "float32"), "DUM": ("sbuf", [128, 2, 16], "float32")}
 for _d in BUFS:
     for _b in BUFS[_d].split():
         SCRATCH[_b.split(":")[0]] = ("sbuf", [128, int(_b.split(":")[1])], _d)
-for _i in range(8):
-    SCRATCH["ps%d" % _i] = ("psum", [128, 512], "float32")
-SEMAPHORES = ["V", "S", "P", "G", "kn0", "kn1", "kn2", "kn3", "lx", "lw", "lf", "lb", "lz", "lt", "btd", "bt", "tt", "tb", "ot", "out",
-              "aT", "aB", "aTB", "loc"] + ["a%s%d" % (k, t) for k in "CZM" for t in range(3)]
+SCRATCH["dz"] = ("psum", [128, 512], "float32")
+SCRATCH["eA"] = ("psum", [128, 4, 128], "float32")
+for _i in range(4):
+    SCRATCH["e%d" % _i] = ("psum", [128, 16, 32], "float32")
+for _i in range(2):
+    SCRATCH["k%d" % _i] = ("psum", [128, 4, 128], "float32")
+SEMAPHORES = ["V", "S", "P", "G", "kn0", "kn1", "kn2", "kn3", "lx", "lw", "lf", "lb", "lz", "lt", "btd", "bt", "tt", "tb", "ot", "out", "early",
+              "aT", "aB", "aTB", "loc"] + ["a%s%d" % (k, t) for k in "ZM" for t in range(3)]
 
 
 def rank_program(g, core, T, topo):
@@ -48,8 +58,9 @@ def rank_program(g, core, T, topo):
         for k in rd:
             if k in last:
                 need(eng, last[k][0], last[k][1])
-        for k in wr:
-            if k in last:
+        for w in wr:
+            k = w.lstrip("+")
+            if k in last and (k == w or last[k][0] != eng):
                 need(eng, last[k][0], last[k][1])
             for s, v in readers.get(k, {}).items():
                 if s != eng:
@@ -62,9 +73,9 @@ def rank_program(g, core, T, topo):
     def after(sem, val, rd, wr, ps):
         for k in rd:
             readers.setdefault(k, {})[sem] = val
-        for k in wr:
-            last[k] = (sem, val)
-            readers[k] = {}
+        for w in wr:
+            last[w.lstrip("+")] = (sem, val)
+            readers[w.lstrip("+")] = {}
         for k in ps:
             excl.setdefault(k, {})[sem] = val
 
@@ -90,6 +101,9 @@ def rank_program(g, core, T, topo):
     def scan(out, d0, d1, init, o0, o1, rd="", wr="", ps=""):
         op("V", lambda: g.vector.tensor_tensor_scan(out=out, data0=d0, data1=d1, initial=init, op0=o0, op1=o1), rd, wr, ps)
 
+    def turn32(out, in_, rd, wr):
+        op("V", lambda: g.vector.transpose(out=out, in_=in_), rd, wr, "")
+
     def fill(ap, c, wr):
         op("V", lambda: g.vector.memset(ap, c), "", wr, "")
 
@@ -104,6 +118,9 @@ def rank_program(g, core, T, topo):
             op("G", lambda: g.iota(out=out, pattern=pat, base=base, channel_multiplier=cm, allow_small_or_imprecise_dtypes=True), "", wr, "")
         else:
             op("G", lambda: g.iota(out=out, pattern=pat, base=base, channel_multiplier=cm), "", wr, "")
+
+    def keep(ap, pat, base, cm, key):
+        op("G", lambda: g.affine_select(out=ap, in_=ap, pattern=pat, compare_op=A.is_ge, fill=0.0, base=base, channel_multiplier=cm), key, key, "")
 
     def dma(eng, grp, out, in_, rd="", wr=""):
         rd, wr = rd.split(), wr.split()
@@ -135,335 +152,557 @@ def rank_program(g, core, T, topo):
 
     nxt, prv = cores[(rank + 1) % n], cores[(rank - 1) % n]
     lo = [NB + 128 * ((rank - t) % n) for t in range(VIS)]
-    D, RS, DP = T.D[:], T.RS, T.ps7
-    PF, P15, PG, PP, OD, EV, M0, NM0, WA0 = [T.COLF[:, i:i + 1] for i in range(9)]
+    D, RS, dz, eA = T.D[:], T.RS[:], T.dz, T.eA
+    eq, kk = [T["e%d" % i] for i in range(4)], [T.k0, T.k1]
+    PF, P15, PG, OD, EV, M0, NM0, PW, P16, AS = [T.COLF[:, i:i + 1] for i in range(10)]
     PI, P15I, PGI, PEI = [T.COLI[:, i:i + 1] for i in range(4)]
+    L = {k: T.SM[:, 8 * i:8 * i + 8] for i, k in enumerate(LISTS)}
+    KCH = [(2560, 3584), (0, 1024), (1024, 2048), (2048, 2560)]
 
-    for i in (3, 2, 0, 1):
-        dma("Y", "kn%d" % i, T.KI[:, 896 * i:896 * i + 896], T.kn[:, 896 * i:896 * i + 896], wr="KI%d" % i)
-    for p in range(16):
-        dma("S", "lf", T.FI[p::16, :], T.ft[:], wr="FI")
-    dma("S", "lt", T.TRI[:], T.tr[:], wr="TRI")
-    dma("Y", "lx", T.X[:, 0:NW], T.x0[:], wr="XL")
-    for p in range(16):
-        dma("S", "lb", T.BI[p::16, :], T.bs[:], wr="BI")
+    def t3(out, a, o, b):
+        tt(L[out], L[a], L[b], o, a + " " + b, out)
+
+    dma("S", "lf", T.FI[0:8, :], T.ft[:], wr="FI")
+    dma("S", "lb", T.BI[0:8, :], T.bs[:], wr="BI")
     dma("S", "lz", T.Z0[:], T.z0[:], wr="Z0")
+    dma("S", "lt", T.TRI[:], T.tr[:], wr="TRI")
+    for i, (a, z) in enumerate(KCH):
+        dma("Y", "kn%d" % i, T.KI[:, a:z], T.kn[:, a:z], wr="KI%d" % i)
     dma("Y", "lw", T.XW[:], T.x0[:], wr="XW")
+    dma("Y", "lx", T.X[:, 0:NW], T.x0[:], wr="XL")
 
-    iota(T.NI[0:64, :], [[1, 64]], 0, 64, "NI", False)
-    fill(T.CK[:], 0.0, "CK")
-    iota(T.CK[0:1, :], [[0, 16], [128, 17]], 0, 0, "CK")
-    iota(T.CI[:], [[1, 128]], 0, 0, "CI", False)
     iota(PI, [[0, 1]], 0, 1, "PI", False)
-    iota(T.CF[:], [[1, 128]], 0, 0, "CF")
+    iota(T.CI[:], [[1, 128]], 0, 0, "CI", False)
     iota(PF, [[0, 1]], 0, 1, "PF")
+    iota(T.CF[:], [[1, 160]], 0, 0, "CF")
+    iota(T.NI[0:64, :], [[1, 64]], 0, 64, "NI", False)
     iota(T.I8[:], [[16, 8]], 0, 0, "I8")
-    iota(T.GI[:], [[17, 8], [1, 17]], 0, 0, "GI")
+    iota(T.C8I[:], [[1, 8]], 0, 0, "C8I", False)
+    fill(T.CK[:], 0.0, "CK")
+    fill(RS, 1.0, "RS")
+    fill(T.R0[:], -1.0e9, "R0")
+    fill(T.KN[:, NW:WN], -1.0, "KN")
+    fill(T.ONB[:], 1.0, "ONB")
+    fill(T.LIVE[:], 0.0, "LIVE")
+    fill(T.T2[:], 1.0e9, "T2")
     fill(T.BCB[0:64, 768:1024], 0.0, "BCB")
+    fill(T.CK[0:1, 68:204], OFS, "CK")
+    fill(T.RS[:, 0::16], 0.0, "RS")
+    fill(T.R0[:, 0::17], 1.0e9, "R0")
+    fill(L["pen"], BIG + OFS, "pen")
+    fill(T.CK[0:1, 68:204:17], 0.0, "CK")
+    iota(T.CK[0:1, 0:68], [[0, 4], [SL, 17]], 0, 0, "CK")
+    ts(P15I, PI, 15, A.bitwise_and, rd="PI", wr="P15I")
+    ts(PGI, PI, 4, A.arith_shift_right, rd="PI", wr="PGI")
+    ts(PEI, PI, 4, A.arith_shift_right, 1, A.bitwise_and, rd="PI", wr="PEI")
+    ts(T.CG[:], T.CI[:], 4, A.arith_shift_right, rd="CI", wr="CG")
+    ts(T.C15[:], T.CI[:], 15, A.bitwise_and, rd="CI", wr="C15")
+    cp(P15, P15I, "P15I", "P15")
+    cp(PG, PGI, "PGI", "PG")
+    cp(OD, PEI, "PEI", "OD")
+    cp(T.CGF[:], T.CG[:], "CG", "CGF")
+    cp(T.C15F[:], T.C15[:], "C15", "C15F")
+    ts(P16, PF, 16.0, A.add, rd="PF", wr="P16")
+    ts(T.RH8[:], T.CGF[:], PF, A.is_equal, rd="CGF PF", wr="RH8")
+    ts(T.RG8[:], T.CGF[:], PF, A.is_equal, rd="CGF PF", wr="RG8")
+    ts(M0, P15, 0.0, A.is_equal, rd="P15", wr="M0")
+    ts(NM0, P15, 0.0, A.not_equal, rd="P15", wr="NM0")
+    ts(EV, OD, 0.0, A.is_equal, rd="OD", wr="EV")
+    ts(PW, PG, 16.0, A.mult, 15.0, A.add, rd="PG", wr="PW")
+    ts(T.J8[:], T.I8[:], P15, A.add, rd="I8 P15", wr="J8")
+    ts(D, T.C15F[:], P15, A.is_equal, rd="C15F P15", wr="D")
+    ts(T.F16[0:8, :], T.FI[0:8, :], -OFS, A.add, rd="FI", wr="F16")
+    cp(T.BF8[0:8, :], T.BI[0:8, :], "BI", "BF8")
+    cp(T.TRF[:], T.TRI[:], "TRI", "TRF")
+    send(nxt, T.TD[:], T.TRF[:], "aT", "TRF")
+    arrives("aT", "TD")
+    for h, (ps, pk) in enumerate(((eA[:], "eA"), (eq[3][:], "e3"))):
+        mm(ps, T.RH8[0:8, :], T.F16[0:8, 512 * h:512 * h + 512], True, True, "RH8 F16", pk)
+        act(T.FX[:, NB + 512 * h:NB + 512 * h + 512], ps, AF.Identity, "", "+FX", pk, bias=OFS)
+    mm(eq[2][:, 4:8, :], T.RG8[0:8, :], T.BF8[0:8, :], True, True, "RG8 BF8", "e2")
+    ts(T.IE[:], T.CF[:], P16, A.is_equal, EV, A.mult, rd="CF P16 EV", wr="IE")
+    ts(T.IO[:], T.CF[:], P16, A.is_equal, OD, A.mult, rd="CF P16 OD", wr="IO")
+    ts(T.IF[:], T.CF[:, 0:128], PF, A.is_equal, rd="CF PF", wr="IF")
+    ts(T.IB[:], T.CF[:, 0:128], PF, A.is_equal, rd="CF PF", wr="IB")
+    ts(T.NIB[:], T.CF[:, 0:128], PF, A.is_equal, -1.0, A.mult, rd="CF PF", wr="NIB")
+    ts(T.SW[:], T.CF[:, 0:144], PW, A.is_equal, WT, A.mult, rd="CF PW", wr="SW")
+    cp(T.C8[:], T.C8I[:], "C8I", "C8")
     for b in range(12):
-        ts(T.BC[0:64, 64 * b:64 * b + 64], T.NI[0:64, :], b, A.arith_shift_right, 1, A.bitwise_and, rd="NI", wr="BC")
-    ts(T.BCB[0:64, 0:768], T.BC[0:64, :], 2.0, A.mult, -1.0, A.add, rd="BC", wr="BCB")
+        ts(T.BC[0:64, 64 * b:64 * b + 64], T.NI[0:64, :], b, A.arith_shift_right, 1, A.bitwise_and, rd="NI", wr="+BC")
+    for out, d, key in ((L["dum"], DA, "dum"), (L["dumo"], DA - OFS, "dumo"), (T.MUL[:, 8:16], DA, "MULb"), (T.S2[:, 1::2], DA, "S2b"),
+                        (T.DUM[:, :, 0:4], DA, "DUM"), (T.DUM[:, :, 4:8], DB, "+DUM"), (T.DUM[:, :, 8:12], DA, "+DUM")):
+        act(out, T.J8[:], AF.Identity, "J8", key, bias=float(d))
+    for t in range(VIS):
+        act(T.NN[:, 8 * t:8 * t + 8], T.J8[:], AF.Identity, "J8", "+NN", bias=float(lo[t]))
+    ts(T.BCB[0:64, 0:768], T.BC[0:64, :], 2.0, A.mult, -1.0, A.add, rd="BC", wr="+BCB")
     for b in range(16):
         dma("Y", "btd", T.BTD[b], T.BCB[0:64, 64 * b:64 * b + 64], rd="BCB", wr="BTD")
     for i in range(8):
         dma("Y", "bt", T.BT[16 * i:16 * i + 16, :], T.BTD[:], rd="BTD", wr="BT")
+    for p in range(16):
+        dma("Y", "tt", T.TT[p::16, 0:NW], T.TD[:], rd="TD", wr="TTd")
     iota(T.FX[:, 0:NB], [[0, NB]], -1, 0, "FXa")
-    ts(P15I, PI, 15, A.bitwise_and, rd="PI", wr="P15I")
-    ts(PGI, PI, 4, A.arith_shift_right, rd="PI", wr="PGI")
-    ts(T.C15[:], T.CI[:], 15, A.bitwise_and, rd="CI", wr="C15")
-    ts(T.CG[:], T.CI[:], 4, A.arith_shift_right, rd="CI", wr="CG")
-    ts(PEI, PI, 4, A.arith_shift_right, 1, A.bitwise_and, rd="PI", wr="PEI")
-    cp(P15, P15I, "P15I", "P15")
-    cp(PG, PGI, "PGI", "PG")
-    cp(T.C15F[:], T.C15[:], "C15", "C15F")
-    cp(T.CGF[:], T.CG[:], "CG", "CGF")
-    cp(OD, PEI, "PEI", "OD")
-    ts(T.D[:], T.C15F[:], P15, A.is_equal, rd="C15F P15", wr="D")
-    ts(M0, P15, 0.0, A.is_equal, rd="P15", wr="M0")
-    ts(NM0, P15, 0.0, A.not_equal, rd="P15", wr="NM0")
-    ts(T.B0[:], T.CGF[:], PG, A.is_equal, M0, A.mult, rd="CGF PG M0", wr="B0")
-    cp(DP[:, 0:128], D, "D", "DP")
-    cp(DP[:, 128:256], D, "D", "DP")
-    fill(T.RS[:], 1.0, "RS")
-    fill(T.RS[:, 0::16], 0.0, "RS")
-    ts(T.J8[:], T.I8[:], P15, A.add, rd="I8 P15", wr="J8")
-    for i, d in enumerate((DA, DA, DB, DA, DA)):
-        ts(T.DUM[:, 8 * i:8 * i + 8], T.J8[:], float(d), A.add, rd="J8", wr="DUM")
-    for t in range(VIS):
-        ts(T.NN[:, 16 * t:16 * t + 8], T.J8[:], float(lo[t]), A.add, rd="J8", wr="NN")
-        ts(T.NN[:, 16 * t + 8:16 * t + 16], T.J8[:], float(lo[t]), A.add, rd="J8", wr="NN")
-        fill(T.BO[:, 24 * t + 16:24 * t + 24], float(lo[t] - DB), "BO")
-        fill(T.BSS[:, 32 * t + 8:32 * t + 16], float(lo[t] - DB), "BSS")
-    fill(T.FX[:, NW:WN], -1.0, "FX")
-    fill(T.KN[:, NW:WN], -1.0, "KN")
-    cp(T.FX[:, NB:NW], T.FI[:], "FI", "FX")
-    cp(T.TRF[:], T.TRI[:], "TRI", "TRF")
-    ts(T.IF[:], T.CF[:], PF, A.is_equal, rd="CF PF", wr="IF")
-    ts(T.R[:], T.CGF[:, 0::16], PG, A.is_equal, rd="CGF PG", wr="R")
-    cp(T.RB[:], T.R[:], "R", "RB")
-    ts(T.RB64[:], T.R[:], 64.0, A.mult, rd="R", wr="RB64")
-    fill(T.RSB[:], 1.0, "RSB")
-    fill(T.RSB[:, 0::16], 0.0, "RSB")
-    ts(T.WB[:, 0:8], T.R[:], WT, A.mult, rd="R", wr="WB")
-    ts(T.WB[:, 8:16], T.R[:], WT, A.mult, rd="R", wr="WB")
-    fill(T.ONB[:], 1.0, "ONB")
-    tt(PP, PF, PG, A.add, "PF PG", "PP0")
-    ts(PP, PP, 1.0, A.add, rd="PP0", wr="PP")
-    ts(T.PB[:, 0:136], T.GI[:], PP, A.is_equal, 1.0 / 64, A.mult, rd="GI PP", wr="PB")
-    ts(T.PB[:, 136:272], T.GI[:], PP, A.is_equal, -1.0, A.mult, rd="GI PP", wr="PB")
-    ts(T.PFF[:], T.GI[:], PP, A.is_equal, rd="GI PP", wr="PFF")
-    fill(T.CK[32:33, 0:136], -161.0, "CK")
-    fill(T.CK[32:33, 136:272], 8192.0, "CK")
-    fill(T.CK[64:65, 136:272], 32.0, "CK")
-    fill(T.CK[32:33, 0::17], 0.0, "CK")
-    fill(T.CK[64:65, 0::17], 0.0, "CK")
-    fill(T.R0[:], -1.0e9, "R0")
-    fill(T.R0[:, 0::17], 1.0e9, "R0")
-    fill(T.E[:], 0.0, "E")
-    fill(WA0, 0.0, "WA0")
-    send(nxt, T.TD[:], T.TRF[:], "aT", "TRF")
-    arrives("aT", "TD")
+    iota(T.RPI[:], [[0, 4], [1, 2], [0, 16]], 0, 0, "RPI")
+    iota(T.NUA[:], [[0, 512]], -32, 0, "NUA")
+    iota(T.NUB[:], [[0, 128]], -32, 0, "NUB")
+    iota(T.RG[:], [[0, 512]], 1, 0, "RG")
+    keep(T.NUA[:], [[-16, 4], [0, 8], [-1, 16]], 0, 1, "NUA")
+    keep(T.RG[:], [[0, 4], [-16, 8], [0, 16]], 0, 1, "RG")
+    keep(T.NUB[:], [[-16, 4], [0, 2], [-1, 16]], -64, 1, "NUB")
+    keep(T.RG[:], [[0, 4], [16, 8], [0, 16]], 15, -1, "RG")
+    iota(T.ID[:], [[1, NW]], 0, 0, "ID")
     last["XWp"] = last["XW"]
-
-    def constants3(part):
-        if part == 0:
-            iota(T.ID[:], [[1, NW]], 0, 0, "ID")
-            ts(T.IB[:], T.CF[:], PF, A.is_equal, rd="CF PF", wr="IB")
-            ts(EV, OD, 0.0, A.is_equal, rd="OD", wr="EV")
-            ts(T.NU[:], T.CF[:], PF, A.is_le, -32.0, A.mult, rd="CF PF", wr="NU")
-        elif part == 1:
-            fill(T.ME[:], 0.0, "ME")
-            fill(T.E2[:], 0.0, "E2")
-            fill(T.ML2[:], 1.0, "ML2")
-            fill(T.NR[:], 0.0, "NR")
-            fill(T.MS[:], 0.0, "MS")
-            fill(T.X[:, NW:WN], 0.0, "XL")
-            fill(T.TT[:, NW:WN], 0.0, "TT")
-        else:
-            for t in range(VIS):
-                ts(T.NR[:, 256 * t:256 * t + 128], T.CF[:], float(lo[t]), A.add, M0, A.mult, rd="CF M0", wr="NR")
-                ts(T.VF[:, 256 * t + 128:256 * t + 256], T.CF[:], float(lo[t]), A.add, rd="CF", wr="VFr")
-            for p in range(16):
-                dma("Y", "tt", T.TT[p::16, 0:NW], T.TD[:], rd="TD", wr="TTd")
 
     def kwin():
         return T.KN[:, 0:WN]
 
-    def convert(*ii):
-        for i in ii:
-            cp(T.KN[:, 896 * i:896 * i + 896], T.KI[:, 896 * i:896 * i + 896], "KI%d" % i, "KN")
+    def fwin():
+        return T.FX[:, 0:WN]
 
-    def out(t, mid, mid2=None):
-        a, z = lo[t], lo[t] + 128
-        mm(T.ps2[:, 0:128], T.B0[:], T.KN[:, a:z], True, True, "B0 KN", "ps2")
-        tt(T.MU[:, 0:128], T.FX[:, a:z], DP[:, 0:128], A.mult, "FX DP", "MUa")
-        act(T.FVO[:, 0:128], T.FX[:, a:z], AF.Copy, "FX", "FVO")
-        act(T.UM[:], T.KN[:, a:z], AF.Copy, "KN M0", "UM", scale=M0)
-        mid()
-        tt(T.MU[:, 128:256], T.ps2[:, 0:128], D, A.mult, "D", "MUb", "ps2")
-        scan(T.MS1[:], RS[:], T.MU[:], 0.0, A.mult, A.add, "RS MUa MUb", "MS1")
-        cp(T.YL[:], T.MS1[:, 15::16], "MS1", "YL")
-        if mid2:
-            mid2()
-        act(T.GO[:], kwin().indirect(T.YL[:, 0:8]), AF.Copy, "KN YL", "GO")
-        mm(T.ps2[:, 0:128], T.B0[:], T.GO[:], True, True, "B0 GO", "ps2")
-        act(T.SQ2[:], T.MS1[:, 15::16], AF.Square, "MS1", "SQ2", bias=-a - 63.5)
-        act(T.GZ[:], T.GO[:], AF.Copy, "GO NM0", "GZ", scale=NM0)
-        tt(T.MU2[:, 128:256], T.FX[:, 0:WN].indirect(T.YL[:, 8:16]), D, A.mult, "FX FXa YL D", "MU2b")
-        tt(T.BO[:, 24 * t:24 * t + 16], T.MS1[:, 15::16], T.DUM[:, 0:16], A.subtract, "MS1 DUM", "BO")
-        ts(T.NLV[:], T.SQ2[:], 4096.0, A.is_ge, rd="SQ2", wr="NLV")
-        tt(T.CO[:, 16:24], T.NLV[:, 0:8], T.NLV[:, 8:16], A.mult, "NLV", "COc")
-        tt(T.MU2[:, 0:128], T.ps2[:, 0:128], D, A.mult, "D", "MU2a", "ps2")
-        scan(T.MS2[:], RS[:], T.MU2[:], 0.0, A.mult, A.add, "RS MU2a MU2b", "MS2")
-        tt(T.CE[:], T.MS2[:, 15::16], T.NN[:, 16 * t:16 * t + 16], A.is_equal, "MS2 NN", "CE")
-        tt(T.CO[:, 0:8], T.CE[:, 0:8], T.CO[:, 16:24], A.mult, "CE COc", "COa")
-        tt(T.CO[:, 8:16], T.CE[:, 8:16], T.CO[:, 0:8], A.mult, "CE COa", "COb")
-        tt(T.OF[:, 0:24], T.CO[:], T.BO[:, 24 * t:24 * t + 24], A.mult, "COa COb COc BO", "OF")
-        tt(T.OF[:, 0:24], T.OF[:, 0:24], T.DUM[:, 0:24], A.add, "OF DUM", "OF")
-        cp(T.LO[:], T.OF[:, 0:24], "OF", "LO")
-        tt(kwin().indirect(T.LO[:, 0:8]), T.GZ[:], T.UM[:], A.add, "LO GZ UM", "KN")
+    lines = []
 
-    def start(t, rows, rkey):
-        tt(T.TM[:], rows, D, A.mult, rkey + " D", "TM")
-        scan(T.TS[:], RS[:, 0:128], T.TM[:], 0.0, A.mult, A.add, "RS TM", "TS")
-        cp(T.BL[:, 64 * t:64 * t + 8], T.TS[:, 15::16], "TS", "BL%d" % (4 * t))
-        mm(T.ps6[:, 0:8], T.TM[:], T.R[:], True, True, "TM R", "ps6")
-        act(T.CB8[:], T.ps6[:, 0:8], AF.Identity, "", "CB8", "ps6", bias=8224.5)
+    def pull():
+        for line in lines:
+            while line and next(line[0], "end") == "end":
+                line.pop(0)
 
-    def zrep(zz, key):
-        for k in range(16):
-            act(T.ZR[:, k::16], zz, AF.Copy, key, "ZR")
+    def drain():
+        while any(lines):
+            pull()
 
-    def step(t, s, zz, zkey, wa, wkey, gap):
-        q = 4 * t + s
-        bl, bk = T.BL[:, 16 * q:16 * q + 8], "BL%d" % q
-        vb, vk = (T.ps0, "ps0") if q % 2 == 0 else (T.ps1, "ps1")
+    def late():
+        ts(T.BON[:], T.CGF[:], PG, A.is_equal, float(NW), A.mult, rd="CGF PG", wr="BON")
+        yield
+        fill(T.FX[:, NW:WN], -1.0, "+FX")
+        yield
+        ts(T.B0[:], T.CGF[:], PG, A.is_equal, M0, A.mult, rd="CGF PG M0", wr="B0")
+        yield
+        ts(T.RP[:], T.RPI[:], OD, A.is_equal, rd="RPI OD", wr="RP")
+        yield
+        fill(T.EQ[64:128, 0:4, :], 0.0, "EQz")
+        yield
+        fill(T.CW[:, 0:2], BIG, "CW")
+        fill(T.CW[:, 2:4], BIG / EPS, "+CW")
+        yield
+        fill(T.X[:, NW:WN], 0.0, "XL")
+        fill(T.MS[:], 0.0, "MS")
+        yield
+        fill(T.TT[:, NW:WN], 0.0, "TT")
+        yield
 
-        def stay(f, k):
-            act(T.FP[:], f, AF.Identity, k + wkey, "FP", bias=wa)
-            mm(vb[:, 0:272:17], T.IF[:], T.FP[:], False, False, "IF FP", vk)
-
-        mm(vb[:, 0:272], T.ONB[:], T.CK[:], True, False, "ONB CK", vk)
-        cp(T.KL[:], kwin().indirect(bl), "KN " + bk, "KL")
-        act(T.CFR[:], kwin().indirect(bl), AF.Copy, "KN " + bk, "CFR")
-        act(T.CHB[:], T.CFR[:], AF.Identity, "CFR", "CHB", bias=8224.5)
-        mm(vb[:, 136:272], T.CFR[:], T.PFF[:], False, False, "CFR PFF", vk)
-        if s:
-            stay(T.E[:, 0::16], "E ")
-        for c, (a, z) in enumerate(CH):
-            tt(T.DIFF[:, 16 * a:16 * z], T.XW[:].indirect(T.KL[:, a:z]), T.ZR[:, 16 * a:16 * z], A.subtract, "XW XWp KL ZR", "DF%d" % c)
-            act(T.AB[:, 16 * a:16 * z], T.DIFF[:, 16 * a:16 * z], AF.Abs, "DF%d" % c, "AB%d" % c)
-            if c in PE:
-                a, z = PE[c]
-                for k in range(16):
-                    mm(vb[a:z, k + 1:272:17], T.AB[:, 16 * a + k:16 * z:16], T.WB[:], False, False, "AB%d AB%d WB" % (c, c - (c == 3)), vk)
-        tt(T.DFB[:], T.X[:, 0:NW].indirect(bl), zz, A.subtract, "X XL " + bk + " " + zkey, "DFB")
-        act(T.ABB[:], T.DFB[:], AF.Abs, "DFB", "ABB")
-        if s == 0:
-            tt(T.TB1[:], T.ps6[:, 0:8], T.CB8[:], A.subtract, "CB8", "TB1", "ps6")
-            act(T.FF[:, 0:8], T.CB8[:], AF.Identity, "CB8", "FF", scale=1.0 / 64, bias=-161.0)
-            act(T.FF[:, 8:16], T.TB1[:], AF.Identity, "TB1", "FF", bias=8224.0)
-        gap()
-        mm(vb[:, 0:272:17], T.ABB[:], T.WB[:], False, False, "ABB WB", vk)
-        if s == 0:
-            stay(T.FF[:], "FF ")
-        mm(vb[:, 0:272], T.CHB[:], T.PB[:], False, True, "CHB PB", vk)
-        scan(T.VM[:], T.R0[:], vb[:, 0:272], 1.0e9, A.max, A.min, "R0", "VM", vk)
-        ts(T.RR[:], T.VM[:, 16::17], M7, A.add, M7, A.subtract, rd="VM", wr="RR")
-        tt(T.E[:, 0::16], T.VM[:, 16::17], T.RR[:], A.subtract, "VM RR", "E")
-        scan(T.HO[:], T.RSB[:], T.E[:], 0.0, A.mult, A.add, "RSB E", "HO")
-        tt(T.EM[:], T.HO[:], DP[:, 0:256], A.mult, "HO DP", "EM")
-        mm(T.ps6[:, 0:8], T.EM[:, 0:128], T.RB64[:], True, False, "EM RB64", "ps6")
-        mm(T.ps6[:, 0:8], T.EM[:, 128:256], T.RB[:], False, True, "EM RB", "ps6")
-        ts(T.BL[:, 16 * q + 16:16 * q + 24], T.ps6[:, 0:8], 2080.0, A.add, wr="BL%d" % (q + 1), ps="ps6")
-
-    def seat(t, zz, zkey):
-        fin = t == VIS - 1
-        a = lo[t]
-        q = 4 * t + 3
-        bl, bk = T.BL[:, 16 * q:16 * q + 8], "BL%d" % q
-        zn, znk = T.ZN[:, 128 * t:128 * t + 128], "ZN%d" % t
-        vf = T.VF[:, 256 * t:256 * t + 256]
-        if fin:
-            send(prv, T.CL[:, 48:56], bl, "aB", bk)
-        else:
-            send(nxt, T.CL[:, 16 * t:16 * t + 8], bl, "aC%d" % t, bk)
-        act(T.VK[:, 128:256], kwin().indirect(bl), AF.Copy, "KN " + bk, "VKb")
-        mm(T.ps2[:, 0:128], T.B0[:], T.VK[:, 128:256], True, True, "B0 VKb", "ps2")
-        act(T.CDE[:], T.BT[:].indirect(bl), AF.Copy, "BT EV " + bk, "CDE", scale=EV)
-        act(T.CDO[:], T.BT[:].indirect(bl), AF.Copy, "BT OD " + bk, "CDO", scale=OD)
-        ts(T.BLF[:], T.ps6[:, 0:8], 2080.0, A.add, wr="BLF", ps="ps6")
-        act(T.SQ2[:, 0:8], T.BLF[:], AF.Square, "BLF", "SQ2", bias=-a - 63.5)
+    def rows(t):
+        act(T.VF[:, 256 * t + 128:256 * t + 256], T.CF[:, 0:128], AF.Identity, "CF", "VFr", bias=float(lo[t]))
         for h in range(2):
-            ps, pk = (T.ps3, "ps3") if h == 0 else (T.ps4, "ps4")
-            for i in range(4):
-                gr = 4 * h + i
-                r = 32 * (gr // 2)
-                cd, ck = (T.CDE, "CDE") if gr % 2 == 0 else (T.CDO, "CDO")
-                mm(ps[:, 128 * i:128 * i + 128], T.IB[:], T.NU[:], True, False, "IB NU", pk)
-                if i == 2:
-                    need("P", "P", tot["P"])
-                mm(ps[:, 128 * i:128 * i + 128], cd[r:r + 32, :], cd[r:r + 32, :], False, True, ck, pk)
-            act(T.EQ[:, 512 * h:512 * h + 512], ps[:], AF.Relu, "", "EQ%d" % h, pk, bias=-11.0)
-        tt(T.ZS[:], T.X[:, 0:NW].indirect(bl), zz, A.add, "X XL " + bk + " " + zkey, "ZS")
-        ts(T.ZQ[:], T.ZS[:], 0.4999, A.mult, M0C, A.add, rd="ZS", wr="ZQ")
-        ts(zn, T.ZQ[:], -M0C, A.add, rd="ZQ", wr=znk)
-        if not fin:
-            send(nxt, T.ZL[:, 128 * t:128 * t + 128], zn, "aZ%d" % t, znk)
-        tt(T.MU[:, 0:128], T.ps2[:, 0:128], D, A.mult, "D", "MUa", "ps2")
-        scan(T.MS1[:, 0:128], RS[:, 0:128], T.MU[:, 0:128], 0.0, A.mult, A.add, "RS MUa", "MS1")
-        ts(T.NLV[:, 0:8], T.SQ2[:, 0:8], 4096.0, A.is_ge, rd="SQ2", wr="NLV")
-        cp(T.VL[:], T.MS1[:, 15:128:16], "MS1", "VL")
-        tt(T.ME[:, 0::16], T.NLV[:, 0:8], T.CO[:, 16:24], A.mult, "NLV COc", "ME")
-        scan(T.MH[:], T.RSB[:, 0:128], T.ME[:], 0.0, A.mult, A.add, "RSB ME", "MH")
-        tt(T.MU2[:, 0:128], T.FX[:, 0:WN].indirect(T.VL[:]), D, A.mult, "FX FXa VL D", "MU2a")
-        tt(T.MX[:], T.MH[:], DP[:, 0:128], A.mult, "MH DP", "MX")
-        mm(T.ps5[:, 0:8], T.MX[:], T.RB[:], True, True, "MX RB", "ps5")
-        scan(T.MS2[:, 0:128], RS[:, 0:128], T.MU2[:, 0:128], 0.0, A.mult, A.add, "RS MU2a", "MS2")
-        cp(T.ML2[:, 0:8], T.ps5[:, 0:8], "", "ML2", "ps5")
-        act(vf[:, 0:128], T.ID[:].indirect(bl), AF.Copy, "ID " + bk, "VF%d" % t)
-        act(T.VK[:, 0:128], T.VK[:, 128:256], AF.Copy, "VKb NM0", "VKa", scale=NM0)
+            a = 256 * t + 128 * h
+            act(T.NR[:, a + 64:a + 128], T.CF[:, 0:64], AF.Copy, "CF", "+NR", scale=0.0)
+            act(T.NR[:, a:a + 64], T.VF[:, 256 * t + 128 + 64 * h:256 * t + 192 + 64 * h], AF.Copy, "VFr M0", "+NR", scale=M0)
+
+    def to_list(out, b0, b1, pk):
+        for c, (m, mk) in enumerate(((T.IE, "IE"), (T.IO, "IO"))):
+            for gp in range(2):
+                w = 16 + 16 * (c - gp)
+                mm(out[:, 2 * b0 + c:2 * b1:2], m[:, w:w + 128], T.CT2[:, b0:b1, 16 * gp], gp == 0, gp == 1, mk + " CT2", pk)
+
+    def mine(out, sq, x, a, rd, ps="", off=0.0):
+        act(L[sq], x, AF.Square, rd, sq, ps, bias=off - a - 63.5)
+        act(out[0], L[sq], AF.Relu, sq, out[1], scale=-64.0, bias=262144.0)
+
+    def out_before(t):
+        a, z = lo[t], lo[t] + 128
+        y0, pl = T.MS1[:, 15::16], dz[:, 400:416]
+        tt(T.MU[:], T.FX[:, a:z], D, A.mult, "FX D", "MU")
+        yield
+        ts(T.C2[:, 128:256], T.KN[:, a:z], -OFS, A.add, rd="KN", wr="C2b")
+        yield
+        scan(T.MS1[:], RS, T.MU[:], 0.0, A.mult, A.add, "RS MU", "MS1")
+        act(T.CMP[:, 0:8], T.J8[:], AF.Identity, "J8", "CMPa", bias=a - OFS)
+        mine((L["po1"], "po1"), "sq1", y0, a, "MS1")
+        if t:
+            mine((L["por"], "por"), "sqr", y0, lo[t - 1], "MS1")
+        yield
+        cp(T.YL[:, 0:8], y0, "MS1", "YLa")
+        yield
+        if t:
+            ts(T.C2[:, 0:128], kwin().indirect(T.YL[:, 0:8]), -OFS, A.add, rd="KN YLa", wr="C2a")
+            yield
+        b0 = 0 if t else 4
+        turn32(T.CT2[:, b0:8, :], T.C2[:, 32 * b0:256], "C2a C2b", "CT2")
+        to_list(pl, b0, 8, "dz")
+        act(L["squ"], pl[:, 8:16], AF.Square, "", "squ", "dz", bias=OFS - a - 63.5)
+        act(L["pnu"], L["squ"], AF.Relu, "squ", "pnu", scale=64.0, bias=-262144.0)
+        yield
+        tt(L["y1"], y0, L["po1"], A.add, "MS1 po1", "y1")
+        yield
+        if t:
+            tt(L["ne"], pl[:, 0:8], T.CMP[:, 0:8], A.not_equal, "CMPa", "ne", "dz")
+            yield
+        tt(L["d1"], L["y1"], T.CMP[:, 0:8], A.subtract, "y1 CMPa", "d1")
+        yield
+        if t:
+            ts(L["pe"], L["ne"], BIG, A.mult, OFS, A.add, rd="ne", wr="pe")
+            yield
+        tt(T.CMP[:, 8:16], pl[:, 8:16], L["pnu"], A.subtract, "pnu", "CMPb", "dz")
+        yield
+        if t:
+            t3("pen", "pe", A.add, "por")
+            yield
+        tt(T.MUL[:, 0:8], L["d1"], L["pen"], A.subtract, "d1 pen", "MULa")
+        yield
+
+    def out(t):
+        a, z = lo[t], lo[t] + 128
+        pl = eq[0][:, 4, 0:16]
+        ts(T.C2[:, 0:128], kwin().indirect(T.YL[:, 0:8]), -OFS, A.add, rd="KN YLa", wr="C2a")
+        ts(T.C2[:, 128:256], T.KN[:, a:z], -OFS, A.add, rd="KN", wr="C2b")
+        act(T.GZ[:], kwin().indirect(T.YL[:, 0:8]), AF.Copy, "KN YLa NM0", "GZ", scale=NM0)
+        act(T.UM[:], T.KN[:, a:z], AF.Copy, "KN M0", "UM", scale=M0)
+        yield
+        turn32(T.CT2[:], T.C2[:], "C2a C2b", "CT2")
+        to_list(pl, 0, 8, "e0")
+        yield
+        tt(T.E2[:], pl, T.CMP[:], A.is_equal, "CMPa CMPb", "E2", "e0")
+        tt(L["s1"], pl[:, 0:8], L["pen"], A.add, "pen", "s1", "e0")
+        yield
+        tt(T.T2[:, 1::2], T.E2[:], T.MUL[:], A.mult, "E2 MULa MULb", "T2")
+        yield
+        tt(T.S2[:, 0::2], L["s1"], T.T2[:, 1:16:2], A.add, "s1 T2", "S2a")
+        yield
+        scan(T.OO[:], T.T2[:, 16:32], T.S2[:], 0.0, A.max, A.min, "T2 S2a S2b", "OO")
+        yield
+        cp(T.LO[:, 0:8], T.OO[:, 1::2], "OO", "LOa")
+        yield
+        tt(kwin().indirect(T.LO[:, 0:8]), T.GZ[:], T.UM[:], A.add, "LOa GZ UM", "KN")
+        yield
+
+    def live(t):
+        act(L["nc0"], L["pen"], AF.Sign, "pen", "nc0", bias=-OFS)
+        act(L["oy0"], L["po1"], AF.Sign, "po1", "oy0")
+        if t:
+            cp(T.AI[:, 0:4], T.ML[:, 16 * t - 8:16 * t - 4], "M%d" % (t - 1), "AI0")
+            yield
+            ts(T.AI[:, 4:8], T.AI[:, 0:4], 31, A.bitwise_and, rd="AI0", wr="AI1")
+            yield
+            ts(T.CA[:], T.AI[:, 4:8], WT, A.mult, rd="AI1", wr="CA")
+            yield
+        tt(L["nch"], T.E2[:, 0:8], L["nc0"], A.max, "E2 nc0", "nch")
+        yield
+        t3("oy", "nch", A.mult, "oy0")
+        yield
+        tt(L["dead"], L["oy"], T.E2[:, 8:16], A.max, "oy E2", "dead")
+        act(T.LIVE[:, 0:8], L["dead"], AF.Identity, "dead", "LIVE", scale=-1.0, bias=1.0)
+        act(T.NL[:], L["dead"], AF.Copy, "dead", "NL", scale=BIG)
+        yield
+        yield
+        tt(T.LX[:], T.LIVE[:].indirect(T.C8[:]), D, A.mult, "LIVE C8 D", "LX")
+        mm(dz[:, 256:384], T.BON[:], T.LX[:], True, True, "BON LX", "dz")
+        yield
+
+    def out_feet(t):
+        a, z = lo[t], lo[t] + 128
+        pl = eq[0][:, 4, 0:16]
+        act(T.FVO[:], T.FX[:, a:z], AF.Copy, "FX", "FVO")
+        ts(T.YL[:, 8:16], pl[:, 8:16], OFS, A.add, wr="YLb", ps="e0")
+        tt(L["bou"], pl[:, 8:16], L["dumo"], A.subtract, "dumo", "bou", "e0")
+        yield
+        tt(T.MU2[:], fwin().indirect(T.YL[:, 8:16]), D, A.mult, "FX FXa YLb D", "MU2")
+        ts(L["held"], T.OO[:, 1::2], float(NW), A.is_lt, rd="OO", wr="held")
+        yield
+        scan(T.MS2[:], RS, T.MU2[:], 0.0, A.mult, A.add, "RS MU2", "MS2")
+        t3("h1", "held", A.mult, "bou")
+        yield
+        tt(L["e1"], T.MS2[:, 15::16], T.NN[:, 8 * t:8 * t + 8], A.is_equal, "MS2 NN", "e1")
+        yield
+        t3("h2", "e1", A.mult, "h1")
+        yield
+        t3("ofu", "h2", A.add, "dum")
+        yield
+        cp(T.LO[:, 8:16], L["ofu"], "ofu", "LOb")
+        yield
+        cp(fwin().indirect(T.LO[:, 8:16]), T.FVO[:], "LOb FVO", "FX")
+        yield
+        tt(T.FX[:, a:z], dz[:, 256:384], T.FX[:, a:z], A.max, "FX", "FX", "dz")
+        yield
+
+    def seat_begin(part):
+        if part == 0:
+            mm(eA[0:64], T.IB[:, 0:64], T.NUA[:], True, False, "IB NUA", "eA")
+            mm(eA[0:64], T.LX[:, 0:64], T.RG[:], False, False, "LX RG", "eA")
+        else:
+            for q in (2 * part - 2, 2 * part - 1):
+                mm(eq[q][:, 0:4, :], T.IB[:], T.NUB[:], True, False, "IB NUB", "e%d" % q)
+                mm(eq[q][:, 0:4, :], T.LX[32 * q:32 * q + 32, :], T.RP[32 * q:32 * q + 32, :], False, False, "LX RP", "e%d" % q)
+
+    def start(t):
+        if t == 0:
+            tt(T.TM[:], eq[2][:, 4:8, :], D, A.mult, "D", "TM", "e2")
+        else:
+            cp(T.CL[:, 0:8], T.LND[:, 136 * t - 8:136 * t], "Z%d" % (t - 1), "CL")
+            yield
+            tt(T.TM[:], T.TT[:].indirect(T.CL[:, 0:8]), D, A.mult, "TT TTd CL D", "TM")
+        yield
+        scan(T.TS[:], RS, T.TM[:], 0.0, A.mult, A.add, "RS TM", "TS")
+        yield
+        cp(T.BL[:, 64 * t:64 * t + 8], T.TS[:, 15::16], "TS", "BL%d0 BL%d1" % (4 * t, 4 * t))
+        yield
+
+    def zrep(t, h):
+        zz, key = (T.Z0, "Z0") if t == 0 else (T.LND[:, 136 * t - 136:136 * t - 8], "Z%d" % (t - 1))
+        for k in range(16):
+            act(T.ZR[:, 1024 * h + k:1024 * h + 1024:16], zz[:, 64 * h:64 * h + 64], AF.Copy, key, "+ZR%d" % h)
+
+    def far(t):
+        act(T.XW[:, lo[t]:lo[t] + 128], T.ONB[:], AF.Copy, "ONB", "XWp", scale=4096.0)
+
+    def sums(t, s, h, other):
+        q, a, k, pk = 4 * t + s, 64 * h, kk[h], "k%d" % h
+        bl, bk = T.BL[:, 16 * q + 4 * h:16 * q + 4 * h + 4], "BL%d%d" % (q, h)
+        bf, fk = (T.TS[:, a + 15:a + 64:16], "TS") if s == 0 else (T.SC[:, 68 * h + 16:68 * h + 68:17], "SC%d" % h)
+
+        def gather(c):
+            u, z = a + CUTS[c], a + CUTS[c + 1]
+            tt(T.DIFF[:, 16 * u:16 * z], T.XW[:].indirect(T.KL[:, u:z]), T.ZR[:, 16 * u:16 * z], A.subtract,
+               "XW XWp KL%d ZR%d" % (h, h), "DF%d%d" % (h, c))
+            if c != 1:
+                u = a + CUTS[c - (c == 2)]
+                act(T.AB[:, u:z, 1:17], T.DIFF[:, 16 * u:16 * z], AF.Abs, "DF%d%d DF%d%d" % (h, c, h, c - (c == 2)), "AB%d%d" % (h, c))
+            if next(other, "end") == "end":
+                pull()
+
+        cp(T.KL[:, a:a + 64], kwin().indirect(bl), "KN " + bk, "KL%d" % h)
+        act(T.XB[:, a:a + 64], T.X[:, 0:NW].indirect(bl), AF.Copy, "X XL " + bk, "XB%d" % h)
+        mm(dz[:, a:a + 64], T.IB[:], T.XB[:, a:a + 64], True, False, "IB XB%d" % h, "dz")
+        mm(dz[:, a:a + 64], T.NIB[:], T.ZR[:, 16 * a:16 * a + 1024:16], False, True, "NIB ZR%d" % h, "dz")
+        mm(k[:, 0:3, 0:68], T.ONB[:], T.CK[:], True, False, "ONB CK", pk)
+        mm(k[:, 1:3, 0:34:17], T.IF[:], bf, False, False, "IF " + fk, pk)
+        pull()
+        gather(0)
+        act(T.AB[:, a:a + 64, 0], dz[:, a:a + 64], AF.Abs, "", "AB%ds" % h, "dz")
+        ts(T.C16[:, a:a + 64], T.KL[:, a:a + 64], -OFS, A.add, rd="KL%d" % h, wr="C16%d" % h)
+        gather(1)
+        turn32(T.CT[:, 2 * h:2 * h + 2, :], T.C16[:, a:a + 64], "C16%d" % h, "CT%d" % h)
+        for c, (m, mk) in enumerate(((T.IE, "IE"), (T.IO, "IO"))):
+            for gp in range(2):
+                w = 16 + 16 * (c - gp)
+                mm(k[:, 1:3, 17 * c + 1:17 * c + 17], m[:, w:w + 128], T.CT[:, 2 * h:2 * h + 2, 16 * gp:16 * gp + 16], False, False,
+                   mk + " CT%d" % h, pk)
+        gather(2)
+        pull()
+        gather(3)
+        if t:
+            mm(k[:, 0, 0:68:17], T.IB[:], T.CA[:], False, False, "IB CA", pk)
+        for j in range(16):
+            mm(k[:, 0, 0:68], T.SW[:, 15 - j:143 - j], T.AB[:, a + j:a + 64:16, :], False, j == 15,
+               "SW AB%d0 AB%d2 AB%d3 AB%ds" % (h, h, h, h), pk)
+        pull()
+        next(other, "end")
+        pull()
+
+    def least(t, s, h):
+        q, k, pk, a = 4 * t + s + 1, kk[h], "k%d" % h, 68 * h
+        scan(T.VM[:, a:a + 68], T.R0[:], k[:, 0, 0:68], 1.0e9, A.max, A.min, "R0", "VM%d" % h, pk)
+        yield
+        tt(T.GG[:, a:a + 68], k[:, 0, 0:68], T.VM[:, a:a + 68], A.subtract, "VM%d" % h, "GG%d" % h, pk)
+        yield
+        tt(T.BB[:, a:a + 68], k[:, 1:3, 0:34], T.GG[:, a:a + 68], A.subtract, "GG%d" % h, "BB%d" % h, pk)
+        yield
+        scan(T.SC[:, a:a + 68], T.GG[:, a:a + 68], T.BB[:, a:a + 68], 0.0, A.min, A.max, "GG%d BB%d" % (h, h), "SC%d" % h)
+        yield
+        cp(T.BL[:, 16 * q + 4 * h:16 * q + 4 * h + 4], T.SC[:, a + 16:a + 68:17], "SC%d" % h, "BL%d%d" % (q, h))
+        yield
+
+    def seat_sums(t, h):
+        q, a = 4 * t + 3, 64 * h
+        bl, bk = T.BL[:, 16 * q + 4 * h:16 * q + 4 * h + 4], "BL%d%d" % (q, h)
+        bf, fk = T.SC[:, 68 * h + 16:68 * h + 68:17], "SC%d" % h
+        cnt, pk, c4 = kk[h][:, 3, 0:12], "k%d" % h, slice(4 * h, 4 * h + 4)
+        if h == 0:
+            act(T.CDE[:, 0:64], T.BT[:].indirect(bl), AF.Copy, "BT EV " + bk, "CDE0", scale=EV)
+        else:
+            ts(T.CDE[:, 64:128], T.BT[:].indirect(bl), EV, A.mult, rd="BT EV " + bk, wr="CDE1")
+        act(T.CDO[:, a:a + 64], T.BT[:].indirect(bl), AF.Copy, "BT OD " + bk, "CDO%d" % h, scale=OD)
+        act(L["sq3"][:, c4], bf, AF.Square, fk, "sq3%d" % h, bias=-lo[t] - 63.5)
+        for i in (0, 8):
+            act(T.BN[:, h, i:i + 4], bf, AF.Copy, fk, "+BN%d" % h)
+        act(T.PO[:, c4], L["sq3"][:, c4], AF.Relu, "sq3%d" % h, "PO%d" % h, scale=-64.0, bias=262144.0)
+        act(T.XB[:, a:a + 64], T.X[:, 0:NW].indirect(bl), AF.Copy, "X XL " + bk, "XB%d" % h)
+        act(T.VK[:, h, 64:128], kwin().indirect(bl), AF.Copy, "KN " + bk, "VKb%d" % h)
+        act(T.VK[:, h, 0:64], kwin().indirect(bl), AF.Copy, "KN NM0 " + bk, "VKa%d" % h, scale=NM0)
         for gr in range(8):
-            mm(T.ps5[:, 16 + gr:32:8], T.EQ[:, 128 * gr:128 * gr + 128], T.ML2[:, gr::8], True, True, "EQ%d ML2" % (gr // 4), "ps5")
-        tt(T.CE[:, 0:8], T.MS2[:, 15:128:16], T.BLF[:], A.is_equal, "MS2 BLF", "CE")
-        b0 = 32 * t
-        tt(T.BSS[:, b0:b0 + 8], T.BLF[:], T.DUM[:, 0:8], A.subtract, "BLF DUM", "BSS")
-        tt(T.BSS[:, b0 + 16:b0 + 24], T.MS1[:, 15:128:16], T.DUM[:, 0:8], A.subtract, "MS1 DUM", "BSS")
-        tt(T.BSS[:, b0 + 24:b0 + 32], T.BLF[:], T.DUM[:, 0:8], A.subtract, "BLF DUM", "BSS")
-        if t in (1, 2):
-            cp(T.L8[:], T.ML[:, 16 * (t - 1):16 * (t - 1) + 8], "M%d" % (t - 1), "L8")
-            cp(T.TT[:].indirect(T.L8[:]), vf[:, 0:128], "L8 VF%d" % t, "TT TTd")
-        ts(T.E2[:, 0::16], T.ps5[:, 16:32], 0.0, A.is_equal, rd="", wr="E2", ps="ps5")
-        scan(T.H2[:], T.RSB[:], T.E2[:], 0.0, A.mult, A.add, "RSB E2", "H2")
-        tt(T.EM2[:], T.H2[:], DP[:, 0:256], A.mult, "H2 DP", "EM2")
-        mm(T.ps5[:, 32:40], T.EM2[:, 0:128], T.RB[:], True, True, "EM2 RB", "ps5")
-        mm(T.ps5[:, 40:48], T.EM2[:, 128:256], T.RB[:], True, True, "EM2 RB", "ps5")
-        tt(T.CND[:, 0:8], T.ps5[:, 32:40], T.ME[:, 0::16], A.mult, "ME", "CN0", "ps5")
-        tt(T.CND[:, 8:16], T.ps5[:, 32:40], T.ME[:, 0::16], A.mult, "ME", "CN1", "ps5")
-        cp(T.CND[:, 24:32], T.ps5[:, 40:48], "", "CN3", "ps5")
-        tt(T.CND[:, 16:24], T.CE[:, 0:8], T.CND[:, 0:8], A.mult, "CE CN0", "CN2")
+            r = 32 * (gr // 2)
+            cd, ck = (T.CDE, "CDE") if gr % 2 == 0 else (T.CDO, "CDO")
+            if h == 0:
+                if gr in (2, 4, 6):
+                    need("P", "P", tot["P"])
+                mm(eA[0:64, :, 16 * gr:16 * gr + 16], cd[r:r + 32, 0:64], cd[r:r + 32, 0:64], False, gr == 7, ck + "0", "eA")
+            else:
+                o = 16 * (gr % 2)
+                mm(eq[gr // 2][:, 0:4, o:o + 16], cd[r:r + 32, :], cd[r:r + 32, 64:128], False, gr % 2 == 1, "%s0 %s1" % (ck, ck), "e%d" % (gr // 2))
+        mm(cnt, T.IF[:], T.BN[:, h, 0:12], True, False, "IF BN%d" % h, pk)
+        for i in (0, 4):
+            mm(cnt[:, i:i + 4], T.IB[:], T.NL[:, c4], False, False, "IB NL", pk)
+            mm(cnt[:, i:i + 4], T.IB[:], T.PO[:, c4], False, False, "IB PO%d" % h, pk)
+        if h == 0:
+            act(T.VF[:, 256 * t:256 * t + 64], T.ID[:].indirect(bl), AF.Copy, "ID " + bk, "VF0")
+            act(T.EQ[0:64, 0:4, :], eA[0:64], AF.Relu, "", "EQA", "eA", bias=-12.0 + EPS)
+        else:
+            for i in (2, 3):
+                act(T.EQ[:, 4:8, 32 * i:32 * i + 32], eq[i][:, 0:4, :], AF.Relu, "", "EQ%d" % i, "e%d" % i, bias=-12.0 + EPS)
+
+    def seat_count(h):
+        for c in range(4):
+            mm(kk[h][:, 3, c:12:4], T.EQ[:, 4 * h + c, :], T.CW[:, 0:3], False, c == 3, "CW EQ0 EQ1 EQ2 EQ3" if h else "CW EQA EQz", "k%d" % h)
+
+    def seat_kin(t, h):
+        tt(T.OF[:, h, 0:12], kk[h][:, 3, 0:12], T.DUM[:, h, 0:12], A.min, "DUM", "OF%d" % h, "k%d" % h)
+        yield
+        cp(T.LS[:, 8 * h:8 * h + 8], T.OF[:, h, 0:8], "OF%d" % h, "LS%d" % h)
+        yield
+        tt(kwin().indirect(T.LS[:, 8 * h:8 * h + 8]), T.VK[:, h, :], T.NR[:, 256 * t + 128 * h:256 * t + 128 * h + 128], A.add,
+           "LS%d VKa%d VKb%d NR" % (h, h, h), "KN")
+        yield
+
+    def seat_feet(t):
+        v = T.MS3[:, 15::16]
+        tt(T.MV[:], dz[:, 128:256], D, A.mult, "D", "MV", "dz")
+        yield
+        scan(T.MS3[:], RS, T.MV[:], 0.0, A.mult, A.add, "RS MV", "MS3")
+        yield
+        cp(T.VL[:], v, "MS3", "VL")
+        tt(L["bov"], v, L["dum"], A.subtract, "MS3 dum", "bov")
+        yield
+        tt(T.MU2[:], fwin().indirect(T.VL[:]), D, A.mult, "FX FXa VL D", "MU2")
+        tt(L["m1"], L["bov"], T.SN[:], A.mult, "bov SN", "m1")
+        yield
+        scan(T.MS2[:], RS, T.MU2[:], 0.0, A.mult, A.add, "RS MU2", "MS2")
+        yield
+        tt(L["e3"], T.MS2[:, 15::16], T.BN[:, :, 0:4], A.is_equal, "MS2 BN0 BN1", "e3")
+        yield
+        t3("m2", "m1", A.mult, "e3")
+        yield
+        t3("ofv", "dum", A.subtract, "m2")
+        yield
+        cp(T.LN[:, 8:16], L["ofv"], "ofv", "LNb")
+        yield
+        cp(fwin().indirect(T.LN[:]), T.VF[:, 256 * t:256 * t + 256], "LNa LNb VFr VF0 VF1", "FX")
+        yield
+
+    def seat_z(t):
+        fin = t == VIS - 1
+        zn, znk = (T.ZN[:], "ZN") if fin else (T.SND[:, 136 * t:136 * t + 128], "SND%d" % t)
+        mm(dz[:, 0:128], T.IB[:], T.XB[:], True, False, "IB XB0 XB1", "dz")
+        mm(dz[:, 0:128], T.IB[:], T.ZR[:, 0::16], False, True, "IB ZR0 ZR1", "dz")
+        act(T.ZQ[:], dz[:, 0:128], AF.Identity, "", "ZQ", "dz", scale=0.4999, bias=M0C)
         if not fin:
-            tt(T.LA[:], T.CO[:, 16:24], T.CND[:, 0:8], A.subtract, "COc CN0", "LA")
-            mm(T.ps5[:, 48:56], T.ONB[:], T.LA[:], True, True, "ONB LA", "ps5")
-        tt(T.OF[:], T.CND[:], T.BSS[:, b0:b0 + 32], A.mult, "CN0 CN1 CN2 CN3 BSS", "OF")
-        tt(T.OF[:], T.OF[:], T.DUM[:, 8:40], A.add, "OF DUM", "OF")
-        cp(T.LS[:], T.OF[:], "OF", "LS")
+            act(T.SND[:, 136 * t + 128:136 * t + 136], T.SC[:, 16::17], AF.Copy, "SC0 SC1", "SNb%d" % t)
+        act(zn, T.ZQ[:], AF.Identity, "ZQ", znk, bias=-M0C)
         if not fin:
-            m0 = 16 * t
-            cp(T.MS[:, m0:m0 + 8], T.OF[:, 24:32], "OF", "MS")
-            act(T.AQ[:], T.ps5[:, 48:56], AF.Copy, "", "AQ MSa", "ps5", accum_out=T.MS[:, m0 + 8:m0 + 9])
+            send(nxt, T.LND[:, 136 * t:136 * t + 136], T.SND[:, 136 * t:136 * t + 136], "aZ%d" % t, "%s SNb%d" % (znk, t))
+            arrives("aZ%d" % t, "Z%d" % t)
+        act(T.VF[:, 256 * t + 64:256 * t + 128], T.ID[:].indirect(T.BL[:, 64 * t + 52:64 * t + 56]), AF.Copy, "ID BL%d1" % (4 * t + 3), "VF1")
+        mm(dz[:, 128:256], T.B0[:], T.VK[:, :, 64:128], True, True, "B0 VKb0 VKb1", "dz")
+
+    def seat_rest(t):
+        fin = t == VIS - 1
+        a, m0 = lo[t], 16 * t
+        zn, znk = (T.ZN[:], "ZN") if fin else (T.SND[:, 136 * t:136 * t + 128], "SND%d" % t)
+        ts(T.SN[:], T.OF[:, :, 0:4], float(NW), A.is_lt, -1.0, A.mult, rd="OF0 OF1", wr="SN")
+        cp(T.LN[:, 0:8], T.OF[:, :, 4:8], "OF0 OF1", "LNa")
+        if not fin:
+            mm(dz[:, 384:392], T.ONB[:], T.LIVE[:, 0:8], True, False, "ONB LIVE", "dz")
+            mm(dz[:, 384:392], T.ONB[:], T.SN[:], False, True, "ONB SN", "dz")
+            act(T.MS[:, m0:m0 + 8], T.OF[:, :, 8:12], AF.Copy, "OF0 OF1", "MS")
+            act(T.AQ[:], dz[:, 384:392], AF.Copy, "", "AQ AS", "dz", accum_out=AS)
+            act(T.MS[:, m0 + 8:m0 + 12], T.ONB[:, 0:4], AF.Copy, "ONB AS", "MSa", scale=AS)
             send(nxt, T.ML[:, m0:m0 + 16], T.MS[:, m0:m0 + 16], "aM%d" % t, "MS MSa")
-            if t == 2:
-                cp(T.L8[:], T.OF[:, 24:32], "OF", "L8")
-            arrives("aC%d" % t, "CL%d" % t)
-            arrives("aZ%d" % t, "ZL%d" % t)
             arrives("aM%d" % t, "M%d" % t)
-            zrep(T.ZL[:, 128 * t:128 * t + 128], "ZL%d" % t)
-        tt(kwin().indirect(T.LS[:, 0:16]), T.VK[:], T.NR[:, 256 * t:256 * t + 256], A.add, "LS VKa VKb NR", "KN")
-        cp(T.FX[:, 0:WN].indirect(T.LS[:, 8:24]), vf, "LS VF%d VFr" % t, "FX")
-        cp(T.X[:].indirect(T.LS[:, 8:16]), zn, "LS " + znk, "X XL")
+        yield
+        if t in (1, 2):
+            cp(T.TT[:].indirect(T.L8[:]), T.VF[:, 256 * t:256 * t + 128], "L8 VF0 VF1", "TT TTd")
+            yield
+        cp(T.X[:].indirect(T.LN[:, 0:8]), zn, "LNa " + znk, "X XL")
         if not fin:
             act(T.XW[:, a:a + 128], T.X[:, a:a + 128], AF.Copy, "X", "XW")
+            zrep(t + 1, 0)
+            zrep(t + 1, 1)
+        yield
+        if not fin:
+            for _ in start(t + 1):
+                yield
+            if t == 2:
+                cp(T.L8[:], T.OF[:, :, 8:12], "OF0 OF1", "L8")
 
-    def gap(t, s):
-        if t == 0:
-            constants3(s)
-        elif s == 0:
-            cp(T.AI[:, 0:1], T.ML[:, 16 * t - 8:16 * t - 7], "M%d" % (t - 1), "AI0")
-            ts(T.AI[:, 1:2], T.AI[:, 0:1], 31, A.bitwise_and, rd="AI0", wr="AI1")
-            ts(T.WAQ[:, 0:1], T.AI[:, 1:2], WT, A.mult, rd="AI1", wr="WA")
-        if s == 0:
-            cp(T.FX[:, 0:WN].indirect(T.LO[:, 8:24]), T.FVO[:], "LO FVO FVOr", "FX")
+    def convert(i):
+        a, z = KCH[i]
+        cp(T.KN[:, a:z], T.KI[:, a:z], "KI%d" % i, "+KN")
 
-    fill(T.FVO[:, 128:256], float(NW), "FVOr")
-    zrep(T.Z0[:], "Z0")
-    convert(3, 2)
-    out(0, lambda: start(0, T.BI[:], "BI"), lambda: convert(0, 1))
-    fill(T.XW[:, lo[0]:lo[0] + 128], 4096.0, "XWp")
+    zrep(0, 0)
+    far(0)
+    convert(0)
+    lines[:] = [[out_before(0)], [start(0)]]
+    drain()
+    zrep(0, 1)
+    for i in (1, 2, 3):
+        convert(i)
+    lines[:] = [[out(0)], [late()]]
+    drain()
     for t in range(VIS):
-        if t == 0:
-            zz, zkey, wa, wkey = T.Z0[:], "Z0", WA0, "WA0"
+        fin = t == VIS - 1
+        if fin:
+            dma("Y", "early", T.yk[:], T.KN[:, NB:NW], rd="KN", wr="yk")
+            dma("Y", "early", T.yx[:], T.X[:, NB:NW], rd="X", wr="yx")
+        lines[:] = [([seat_feet(t - 1)] if t else []) + [out_feet(t)] + ([] if fin else [out_before(t + 1)]), [live(t)]]
+        other = iter(())
+        for i in range(2 * ST):
+            sums(t, i // 2, i % 2, other)
+            other = least(t, i // 2, i % 2)
+            if i == 1:
+                rows(t)
+                for h in range(2):
+                    act(T.BN[:, h, 4:8], T.J8[:, 4 * h:4 * h + 4], AF.Identity, "J8", "+BN%d" % h, bias=float(lo[t]))
+            if i in (2, 3, 4):
+                seat_begin(i - 2)
+        seat_sums(t, 0)
+        seat_count(0)
+        if t in (1, 2):
+            cp(T.L8[:], T.ML[:, 16 * (t - 1):16 * (t - 1) + 8], "M%d" % (t - 1), "L8")
+        for _ in range(3):
+            pull()
+        for _ in other:
+            pull()
+        if fin:
+            send(prv, T.CL[:, 8:16], T.BL[:, 64 * t + 48:64 * t + 56], "aB", "BL%d0 BL%d1" % (4 * t + 3, 4 * t + 3))
         else:
-            zz, zkey, wa, wkey = T.ZL[:, 128 * t - 128:128 * t], "ZL%d" % (t - 1), T.WAQ[:, 0:1], "WA"
-        for s in range(ST):
-            step(t, s, zz, zkey, wa, wkey, lambda: gap(t, s))
-        seat(t, zz, zkey)
+            far(t + 1)
+        seat_sums(t, 1)
+        first, second = seat_kin(t, 0), seat_kin(t, 1)
+        next(first)
+        drain()
+        next(first)
+        for i in (0, 1):
+            ts(T.EQ[:, 4:8, 32 * i:32 * i + 32], eq[i][:, 0:4, :], -12.0 + EPS, A.add, 0.0, A.max, wr="EQ%d" % i, ps="e%d" % i)
+        seat_count(1)
+        seat_z(t)
+        next(first)
+        next(second)
+        lines[:] = [[second] + ([] if fin else [out(t + 1)]), [seat_rest(t)] + ([seat_feet(t)] if fin else [])]
+        drain()
         if t == 2:
             dma("Y", "tb", T.TB[:], T.TT[0::16, 0:NW], rd="TT", wr="TB")
             send(prv, T.TBL[:], T.TB[:], "aTB", "TB")
             arrives("aTB", "TBL")
             dma("Y", "ot", T.OT[0::16, 0:NW], T.TBL[:], rd="TBL", wr="OT")
-        if t < VIS - 1:
-            fill(T.XW[:, lo[t + 1]:lo[t + 1] + 128], 4096.0, "XWp")
-            out(t + 1, lambda: start(t + 1, T.TT[:].indirect(T.CL[:, 16 * t:16 * t + 8]), "TT TTd CL%d" % t))
+    a = lo[VIS - 1]
     arrives("aB", "CLB")
-    act(T.OR[:], T.ID[:].indirect(T.CL[:, 48:56]), AF.Copy, "ID CLB", "OR")
-    dma("Y", "out", T.yz[:], T.ZN[:, 384:512], rd="ZN3")
-    dma("S", "out", T.yk[:], T.KN[:, NB:NW], rd="KN")
+    act(T.OR[:], T.ID[:].indirect(T.CL[:, 8:16]), AF.Copy, "ID CLB", "OR")
+    dma("Y", "out", T.yz[:], T.ZN[:], rd="ZN")
     dma("Y", "out", T.yp[:], T.KN[0::16, 0:NB], rd="KN")
-    dma("S", "out", T.yf[:], T.FX[0::16, NB:NW], rd="FX")
-    dma("Y", "out", T.yx[:], T.X[:, NB:NW], rd="X")
+    dma("S", "out", T.yk[:, a - NB:a - NB + 128], T.KN[:, a:a + 128], rd="KN", wr="yk")
+    for u, z in ((NB, a), (a + 128, NW)):
+        if z > u:
+            dma("Y", "out", T.yk[0::16, u - NB:z - NB], T.KN[0::16, u:z], rd="KN", wr="yk")
+    dma("Y", "out", T.yx[:, a - NB:a - NB + 128], T.X[:, a:a + 128], rd="X", wr="yx")
     cp(T.OT[:].indirect(T.L8[:]), T.OR[:], "L8 OR", "OT")
-    dma("Y", "out", T.yt[:], T.OT[0::16, 0:NW], rd="OT")
+    dma("S", "out", T.yf[:], T.FX[0::16, NB:NW], rd="FX")
+    dma("S", "out", T.yt[:], T.OT[0::16, 0:NW], rd="OT")
     for s in list(tot):
         need("G", s, tot[s])

@@ -9,17 +9,17 @@ OFS = 1792.0
 M0C = 1.5 * 2.0 ** 23
 EPS = 2.0 ** -20
 CUTS = (0, 28, 40, 52, 64)
-LISTS = "y1 po1 por sq1 sqr squ pnu ne pe pen d1 s1 nc0 oy0 nch oy dead bov m1 e3 m2 ofv bou held h1 e1 h2 ofu dum dumo sq3".split()
+LISTS = "y1 po1 por sq1 sqr ne pe pen d1 nc0 oy0 nch oy dead bov bou held dum dumo sq3 aq".split()
 BUFS = {
     "float32": "KN:3856 FX:3856 TT:3856 OT:3856 ID:3584 TRF:224 ML:48 MS:48 COLF:16 CF:160 C15F:128 CGF:128 D:128 B0:128 IF:128 RG8:128 "
                "R0:68 RS:128 I8:8 J8:8 NN:32 NR:1024 VF:1024 FVO:128 TM:128 TS:128 MU:128 MS1:128 GZ:128 UM:128 "
-               "MU2:128 MS2:128 MS3:128 MV:128 SM:256 AQ:8 OR:128 VM:136 GG:136 BB:136 SC:136 ZQ:128 "
-               "SND:408 LND:408 BF8:128 RPI:128 CMP:16 MUL:16 E2:16 T2:32 S2:16 OO:16",
-    "bfloat16": "X:3856 XW:3584 BT:4096 Z0:128 ZN:128 ZR:2048 IB:128 NIB:128 ONB:128 BON:128 SW:144 CK:204 CW:4 CA:4 BCB:1024 DIFF:2048 "
+               "MU2:128 MS2:128 MS3:128 MV:128 SM:192 OR:128 VM:136 GG:136 BB:136 SC:136 ZQ:128 "
+               "BF8:128 RPI:128 CMP:16 E2:48 A1:24 AO:24 B1:24 OO:24 PK0:16 PK1:16 PKO:16",
+    "bfloat16": "X:3856 XW:3584 BT:4096 ZL:512 ZN:512 ZR:2048 IB:128 NIB:128 ONB:128 BON:128 SW:144 CK:204 CW:4 CA:4 BCB:1024 DIFF:2048 "
                 "XB:128 CDE:128 CDO:128 LIVE:16 LX:128 SN:8 NL:8 PO:8 NUA:512 NUB:128 RG:512 RP:128",
     "float16": "C16:128 C2:256 IE:160 IO:160 RH8:128 F16:1024",
     "int32": "KI:3584 FI:1024 BI:128 TRI:224 CI:128 C15:128 CG:128 COLI:4 NI:64 BC:768 AI:8 C8I:8",
-    "uint16": "CL:16 BL:256 KL:128 YL:16 LO:16 VL:8 LS:16 LN:16 L8:8 C8:8",
+    "uint16": "CL:32 BL:256 KL:128 YL:16 LO:16 VL:8 LS:16 LN:16 L8:8 C8:8",
 }
 SCRATCH = {"TD": ("dram", [128, 224], "float32"), "TB": ("dram", [128, 224], "float32"), "TBL": ("dram", [128, 224], "float32"),
            "BTD": ("dram", [16, 64, 64], "bfloat16"),
@@ -35,8 +35,9 @@ for _i in range(4):
     SCRATCH["e%d" % _i] = ("psum", [128, 16, 32], "float32")
 for _i in range(2):
     SCRATCH["k%d" % _i] = ("psum", [128, 4, 128], "float32")
-SEMAPHORES = ["V", "S", "P", "G", "kn0", "kn1", "kn2", "kn3", "lx", "lw", "lf", "lb", "lz", "lt", "btd", "bt", "tt", "tb", "ot", "out", "early",
-              "aT", "aB", "aTB", "loc"] + ["a%s%d" % (k, t) for k in "ZM" for t in range(3)]
+KCH = [(a % NW, a % NW + 512) for a in range(NB, NB + NW, 512)]
+SEMAPHORES = (["V", "S", "P", "G", "lx", "lw", "lf", "lb", "lz", "lt", "btd", "bt", "tt", "tb", "ot", "out", "early", "aT", "aB", "aTB", "loc"]
+              + ["kn%d" % i for i in range(len(KCH))] + ["a%s%d" % (k, t) for k in ("C", "Z0", "Z1", "M") for t in range(3)])
 
 
 def rank_program(g, core, T, topo):
@@ -157,14 +158,13 @@ def rank_program(g, core, T, topo):
     PF, P15, PG, OD, EV, M0, NM0, PW, P16, AS = [T.COLF[:, i:i + 1] for i in range(10)]
     PI, P15I, PGI, PEI = [T.COLI[:, i:i + 1] for i in range(4)]
     L = {k: T.SM[:, 8 * i:8 * i + 8] for i, k in enumerate(LISTS)}
-    KCH = [(2560, 3584), (0, 1024), (1024, 2048), (2048, 2560)]
 
     def t3(out, a, o, b):
         tt(L[out], L[a], L[b], o, a + " " + b, out)
 
     dma("S", "lf", T.FI[0:8, :], T.ft[:], wr="FI")
     dma("S", "lb", T.BI[0:8, :], T.bs[:], wr="BI")
-    dma("S", "lz", T.Z0[:], T.z0[:], wr="Z0")
+    dma("S", "lz", T.ZL[:, 0:128], T.z0[:], wr="Z00 Z01")
     dma("S", "lt", T.TRI[:], T.tr[:], wr="TRI")
     for i, (a, z) in enumerate(KCH):
         dma("Y", "kn%d" % i, T.KI[:, a:z], T.kn[:, a:z], wr="KI%d" % i)
@@ -181,17 +181,16 @@ def rank_program(g, core, T, topo):
     fill(T.CK[:], 0.0, "CK")
     fill(RS, 1.0, "RS")
     fill(T.R0[:], -1.0e9, "R0")
-    fill(T.KN[:, NW:WN], -1.0, "KN")
     fill(T.ONB[:], 1.0, "ONB")
-    fill(T.LIVE[:], 0.0, "LIVE")
-    fill(T.T2[:], 1.0e9, "T2")
-    fill(T.BCB[0:64, 768:1024], 0.0, "BCB")
+    fill(T.B1[:], 1.0e9, "B1")
+    fill(T.E2[:], 0.0, "E2")
     fill(T.CK[0:1, 68:204], OFS, "CK")
     fill(T.RS[:, 0::16], 0.0, "RS")
     fill(T.R0[:, 0::17], 1.0e9, "R0")
     fill(L["pen"], BIG + OFS, "pen")
     fill(T.CK[0:1, 68:204:17], 0.0, "CK")
     iota(T.CK[0:1, 0:68], [[0, 4], [SL, 17]], 0, 0, "CK")
+    iota(T.KN[:, NW:WN], [[0, WN - NW]], -1, 0, "KNt")
     ts(P15I, PI, 15, A.bitwise_and, rd="PI", wr="P15I")
     ts(PGI, PI, 4, A.arith_shift_right, rd="PI", wr="PGI")
     ts(PEI, PI, 4, A.arith_shift_right, 1, A.bitwise_and, rd="PI", wr="PEI")
@@ -209,49 +208,45 @@ def rank_program(g, core, T, topo):
     ts(NM0, P15, 0.0, A.not_equal, rd="P15", wr="NM0")
     ts(EV, OD, 0.0, A.is_equal, rd="OD", wr="EV")
     ts(PW, PG, 16.0, A.mult, 15.0, A.add, rd="PG", wr="PW")
-    ts(T.J8[:], T.I8[:], P15, A.add, rd="I8 P15", wr="J8")
+    act(T.J8[:], T.I8[:], AF.Identity, "I8 P15", "J8", bias=P15)
     ts(D, T.C15F[:], P15, A.is_equal, rd="C15F P15", wr="D")
-    ts(T.F16[0:8, :], T.FI[0:8, :], -OFS, A.add, rd="FI", wr="F16")
     cp(T.BF8[0:8, :], T.BI[0:8, :], "BI", "BF8")
-    cp(T.TRF[:], T.TRI[:], "TRI", "TRF")
-    send(nxt, T.TD[:], T.TRF[:], "aT", "TRF")
-    arrives("aT", "TD")
-    for h, (ps, pk) in enumerate(((eA[:], "eA"), (eq[3][:], "e3"))):
-        mm(ps, T.RH8[0:8, :], T.F16[0:8, 512 * h:512 * h + 512], True, True, "RH8 F16", pk)
-        act(T.FX[:, NB + 512 * h:NB + 512 * h + 512], ps, AF.Identity, "", "+FX", pk, bias=OFS)
     mm(eq[2][:, 4:8, :], T.RG8[0:8, :], T.BF8[0:8, :], True, True, "RG8 BF8", "e2")
+
+    def feet(h):
+        ps, pk = (eA[:], "eA") if h else (eq[3][:], "e3")
+        ts(T.F16[0:8, 512 * h:512 * h + 512], T.FI[0:8, 512 * h:512 * h + 512], -OFS, A.add, rd="FI", wr="F16%d" % h)
+        mm(ps, T.RH8[0:8, :], T.F16[0:8, 512 * h:512 * h + 512], True, True, "RH8 F16%d" % h, pk)
+        act(T.FX[:, NB + 512 * h:NB + 512 * h + 512], ps, AF.Identity, "", "+FX", pk, bias=OFS)
+
+    feet(rank // 4)
     ts(T.IE[:], T.CF[:], P16, A.is_equal, EV, A.mult, rd="CF P16 EV", wr="IE")
     ts(T.IO[:], T.CF[:], P16, A.is_equal, OD, A.mult, rd="CF P16 OD", wr="IO")
     ts(T.IF[:], T.CF[:, 0:128], PF, A.is_equal, rd="CF PF", wr="IF")
-    ts(T.IB[:], T.CF[:, 0:128], PF, A.is_equal, rd="CF PF", wr="IB")
-    ts(T.NIB[:], T.CF[:, 0:128], PF, A.is_equal, -1.0, A.mult, rd="CF PF", wr="NIB")
     ts(T.SW[:], T.CF[:, 0:144], PW, A.is_equal, WT, A.mult, rd="CF PW", wr="SW")
-    cp(T.C8[:], T.C8I[:], "C8I", "C8")
-    for b in range(12):
-        ts(T.BC[0:64, 64 * b:64 * b + 64], T.NI[0:64, :], b, A.arith_shift_right, 1, A.bitwise_and, rd="NI", wr="+BC")
-    for out, d, key in ((L["dum"], DA, "dum"), (L["dumo"], DA - OFS, "dumo"), (T.MUL[:, 8:16], DA, "MULb"), (T.S2[:, 1::2], DA, "S2b"),
+    for out, d, key in ((L["dum"], DA, "dum"), (L["dumo"], DA - OFS, "dumo"), (T.A1[:, 2::3], DA, "A1c"), (T.PK1[:, 1::2], DA, "PK1b"),
                         (T.DUM[:, :, 0:4], DA, "DUM"), (T.DUM[:, :, 4:8], DB, "+DUM"), (T.DUM[:, :, 8:12], DA, "+DUM")):
         act(out, T.J8[:], AF.Identity, "J8", key, bias=float(d))
     for t in range(VIS):
         act(T.NN[:, 8 * t:8 * t + 8], T.J8[:], AF.Identity, "J8", "+NN", bias=float(lo[t]))
-    ts(T.BCB[0:64, 0:768], T.BC[0:64, :], 2.0, A.mult, -1.0, A.add, rd="BC", wr="+BCB")
-    for b in range(16):
-        dma("Y", "btd", T.BTD[b], T.BCB[0:64, 64 * b:64 * b + 64], rd="BCB", wr="BTD")
-    for i in range(8):
-        dma("Y", "bt", T.BT[16 * i:16 * i + 16, :], T.BTD[:], rd="BTD", wr="BT")
-    for p in range(16):
-        dma("Y", "tt", T.TT[p::16, 0:NW], T.TD[:], rd="TD", wr="TTd")
-    iota(T.FX[:, 0:NB], [[0, NB]], -1, 0, "FXa")
-    iota(T.RPI[:], [[0, 4], [1, 2], [0, 16]], 0, 0, "RPI")
-    iota(T.NUA[:], [[0, 512]], -32, 0, "NUA")
-    iota(T.NUB[:], [[0, 128]], -32, 0, "NUB")
-    iota(T.RG[:], [[0, 512]], 1, 0, "RG")
-    keep(T.NUA[:], [[-16, 4], [0, 8], [-1, 16]], 0, 1, "NUA")
-    keep(T.RG[:], [[0, 4], [-16, 8], [0, 16]], 0, 1, "RG")
-    keep(T.NUB[:], [[-16, 4], [0, 2], [-1, 16]], -64, 1, "NUB")
-    keep(T.RG[:], [[0, 4], [16, 8], [0, 16]], 15, -1, "RG")
-    iota(T.ID[:], [[1, NW]], 0, 0, "ID")
+    act(T.IB[:], T.IF[:], AF.Copy, "IF", "IB")
+    act(T.NIB[:], T.IF[:], AF.Copy, "IF", "NIB", scale=-1.0)
     last["XWp"] = last["XW"]
+
+    iota(T.RPI[:], [[0, 4], [1, 2], [0, 16]], 0, 0, "RPI")
+    iota(T.FX[:, 0:NB], [[0, NB]], -1, 0, "FXa")
+
+    def constants_g():
+        iota(T.NUA[:], [[0, 512]], -32, 0, "NUA")
+        iota(T.NUB[:], [[0, 128]], -32, 0, "NUB")
+        iota(T.RG[:], [[0, 512]], 1, 0, "RG")
+        keep(T.NUA[:], [[-16, 4], [0, 8], [-1, 16]], 0, 1, "NUA")
+        keep(T.RG[:], [[0, 4], [-16, 8], [0, 16]], 0, 1, "RG")
+        keep(T.NUB[:], [[-16, 4], [0, 2], [-1, 16]], -64, 1, "NUB")
+        keep(T.RG[:], [[0, 4], [16, 8], [0, 16]], 15, -1, "RG")
+        iota(T.FX[:, NW:WN], [[0, WN - NW]], -1, 0, "FXb")
+        iota(T.TT[:, NW:WN], [[0, WN - NW]], 0, 0, "TT")
+        iota(T.ID[:], [[1, NW]], 0, 0, "ID")
 
     def kwin():
         return T.KN[:, 0:WN]
@@ -259,10 +254,10 @@ def rank_program(g, core, T, topo):
     def fwin():
         return T.FX[:, 0:WN]
 
-    lines = []
+    lines, read, seated = [], [], [-1]
 
-    def pull():
-        for line in lines:
+    def pull(first=0):
+        for line in lines[first:]:
             while line and next(line[0], "end") == "end":
                 line.pop(0)
 
@@ -271,23 +266,46 @@ def rank_program(g, core, T, topo):
             pull()
 
     def late():
+        cp(T.TRF[:], T.TRI[:], "TRI", "TRF")
+        send(nxt, T.TD[:], T.TRF[:], "aT", "TRF")
+        arrives("aT", "TD")
+        constants_g()
+        yield
+        fill(T.BCB[0:64, 768:1024], 0.0, "BCB")
+        yield
+        for b in range(12):
+            ts(T.BC[0:64, 64 * b:64 * b + 64], T.NI[0:64, :], b, A.arith_shift_right, 1, A.bitwise_and, rd="NI", wr="+BC")
+            if b % 3 == 2:
+                yield
+        for i in range(3):
+            ts(T.BCB[0:64, 256 * i:256 * i + 256], T.BC[0:64, 256 * i:256 * i + 256], 2.0, A.mult, -1.0, A.add, rd="BC", wr="+BCB")
+            yield
+        for b in range(16):
+            dma("Y", "btd", T.BTD[b], T.BCB[0:64, 64 * b:64 * b + 64], rd="BCB", wr="BTD")
+        for i in range(8):
+            dma("Y", "bt", T.BT[16 * i:16 * i + 16, :], T.BTD[:], rd="BTD", wr="BT")
+        for p in range(16):
+            dma("Y", "tt", T.TT[p::16, 0:NW], T.TD[:], rd="TD", wr="TTd")
+        fill(T.LIVE[:], 0.0, "LIVE")
+        cp(T.C8[:], T.C8I[:], "C8I", "C8")
+        fill(T.PK0[:], 0.0, "PK0")
+        yield
         ts(T.BON[:], T.CGF[:], PG, A.is_equal, float(NW), A.mult, rd="CGF PG", wr="BON")
         yield
-        fill(T.FX[:, NW:WN], -1.0, "+FX")
+
+    def later():
+        feet(1 - rank // 4)
         yield
         ts(T.B0[:], T.CGF[:], PG, A.is_equal, M0, A.mult, rd="CGF PG M0", wr="B0")
-        yield
         ts(T.RP[:], T.RPI[:], OD, A.is_equal, rd="RPI OD", wr="RP")
         yield
         fill(T.EQ[64:128, 0:4, :], 0.0, "EQz")
         yield
         fill(T.CW[:, 0:2], BIG, "CW")
         fill(T.CW[:, 2:4], BIG / EPS, "+CW")
-        yield
-        fill(T.X[:, NW:WN], 0.0, "XL")
         fill(T.MS[:], 0.0, "MS")
         yield
-        fill(T.TT[:, NW:WN], 0.0, "TT")
+        fill(T.X[:, NW:WN], 0.0, "Xt")
         yield
 
     def rows(t):
@@ -303,124 +321,128 @@ def rank_program(g, core, T, topo):
                 w = 16 + 16 * (c - gp)
                 mm(out[:, 2 * b0 + c:2 * b1:2], m[:, w:w + 128], T.CT2[:, b0:b1, 16 * gp], gp == 0, gp == 1, mk + " CT2", pk)
 
-    def mine(out, sq, x, a, rd, ps="", off=0.0):
-        act(L[sq], x, AF.Square, rd, sq, ps, bias=off - a - 63.5)
-        act(out[0], L[sq], AF.Relu, sq, out[1], scale=-64.0, bias=262144.0)
+    def mine(out, sq):
+        act(L[out], L[sq], AF.Relu, sq, out, scale=-64.0, bias=262144.0)
 
     def out_before(t):
         a, z = lo[t], lo[t] + 128
         y0, pl = T.MS1[:, 15::16], dz[:, 400:416]
         tt(T.MU[:], T.FX[:, a:z], D, A.mult, "FX D", "MU")
-        yield
-        ts(T.C2[:, 128:256], T.KN[:, a:z], -OFS, A.add, rd="KN", wr="C2b")
+        act(T.CMP[:, 0:8], T.J8[:], AF.Identity, "J8", "CMPa", bias=a - OFS)
         yield
         scan(T.MS1[:], RS, T.MU[:], 0.0, A.mult, A.add, "RS MU", "MS1")
-        act(T.CMP[:, 0:8], T.J8[:], AF.Identity, "J8", "CMPa", bias=a - OFS)
-        mine((L["po1"], "po1"), "sq1", y0, a, "MS1")
-        if t:
-            mine((L["por"], "por"), "sqr", y0, lo[t - 1], "MS1")
+        ts(T.C2[:, 128:256], T.KN[:, a:z], -OFS, A.add, rd="KN", wr="C2b")
         yield
         cp(T.YL[:, 0:8], y0, "MS1", "YLa")
-        yield
+        act(L["sq1"], y0, AF.Square, "MS1", "sq1", bias=-a - 63.5)
         if t:
-            ts(T.C2[:, 0:128], kwin().indirect(T.YL[:, 0:8]), -OFS, A.add, rd="KN YLa", wr="C2a")
+            act(L["sqr"], y0, AF.Square, "MS1", "sqr", bias=-lo[t - 1] - 63.5)
+        mine("po1", "sq1")
+        if t:
+            mine("por", "sqr")
+            read.append(-t)
             yield
+            ts(T.C2[:, 0:128], kwin().indirect(T.YL[:, 0:8]), -OFS, A.add, rd="KN YLa", wr="C2a")
+            read.append(t)
+        yield
         b0 = 0 if t else 4
         turn32(T.CT2[:, b0:8, :], T.C2[:, 32 * b0:256], "C2a C2b", "CT2")
         to_list(pl, b0, 8, "dz")
-        act(L["squ"], pl[:, 8:16], AF.Square, "", "squ", "dz", bias=OFS - a - 63.5)
-        act(L["pnu"], L["squ"], AF.Relu, "squ", "pnu", scale=64.0, bias=-262144.0)
         yield
-        tt(L["y1"], y0, L["po1"], A.add, "MS1 po1", "y1")
         yield
         if t:
             tt(L["ne"], pl[:, 0:8], T.CMP[:, 0:8], A.not_equal, "CMPa", "ne", "dz")
-            yield
-        tt(L["d1"], L["y1"], T.CMP[:, 0:8], A.subtract, "y1 CMPa", "d1")
+        ts(T.CMP[:, 8:16], pl[:, 8:16], a - OFS - 0.5, A.max, z - OFS - 0.5, A.min, wr="CMPb", ps="dz")
         yield
+        tt(L["y1"], y0, L["po1"], A.add, "MS1 po1", "y1")
         if t:
             ts(L["pe"], L["ne"], BIG, A.mult, OFS, A.add, rd="ne", wr="pe")
-            yield
-        tt(T.CMP[:, 8:16], pl[:, 8:16], L["pnu"], A.subtract, "pnu", "CMPb", "dz")
         yield
+        tt(L["d1"], L["y1"], T.CMP[:, 0:8], A.subtract, "y1 CMPa", "d1")
         if t:
             t3("pen", "pe", A.add, "por")
-            yield
-        tt(T.MUL[:, 0:8], L["d1"], L["pen"], A.subtract, "d1 pen", "MULa")
+        yield
+        tt(T.A1[:, 0::3], L["d1"], L["pen"], A.subtract, "d1 pen", "A1a")
         yield
 
     def out(t):
         a, z = lo[t], lo[t] + 128
         pl = eq[0][:, 4, 0:16]
-        ts(T.C2[:, 0:128], kwin().indirect(T.YL[:, 0:8]), -OFS, A.add, rd="KN YLa", wr="C2a")
+        while t and lines[0]:
+            yield
+        ts(T.C2[:, 0:128], kwin().indirect(T.YL[:, 0:8]), -OFS, A.add, rd="KN KNt YLa", wr="C2a")
         ts(T.C2[:, 128:256], T.KN[:, a:z], -OFS, A.add, rd="KN", wr="C2b")
-        act(T.GZ[:], kwin().indirect(T.YL[:, 0:8]), AF.Copy, "KN YLa NM0", "GZ", scale=NM0)
+        act(T.GZ[:], kwin().indirect(T.YL[:, 0:8]), AF.Copy, "KN KNt YLa NM0", "GZ", scale=NM0)
         act(T.UM[:], T.KN[:, a:z], AF.Copy, "KN M0", "UM", scale=M0)
         yield
         turn32(T.CT2[:], T.C2[:], "C2a C2b", "CT2")
         to_list(pl, 0, 8, "e0")
         yield
-        tt(T.E2[:], pl, T.CMP[:], A.is_equal, "CMPa CMPb", "E2", "e0")
-        tt(L["s1"], pl[:, 0:8], L["pen"], A.add, "pen", "s1", "e0")
         yield
-        tt(T.T2[:, 1::2], T.E2[:], T.MUL[:], A.mult, "E2 MULa MULb", "T2")
+        tt(T.E2[:, 1::3], pl, T.CMP[:], A.is_equal, "CMPa CMPb", "E2", "e0")
+        tt(T.A1[:, 1::3], pl[:, 0:8], L["pen"], A.add, "pen", "A1b", "e0")
         yield
-        tt(T.S2[:, 0::2], L["s1"], T.T2[:, 1:16:2], A.add, "s1 T2", "S2a")
+        tt(T.B1[:, 2::3], T.E2[:, 25::3], L["dum"], A.mult, "E2 dum", "B1")
+        scan(T.AO[:], T.E2[:, 0:24], T.A1[:], 0.0, A.mult, A.add, "E2 A1a A1b A1c", "AO")
         yield
-        scan(T.OO[:], T.T2[:, 16:32], T.S2[:], 0.0, A.max, A.min, "T2 S2a S2b", "OO")
+        scan(T.OO[:], T.B1[:], T.AO[:], 0.0, A.max, A.min, "B1 AO", "OO")
         yield
-        cp(T.LO[:, 0:8], T.OO[:, 1::2], "OO", "LOa")
+        cp(T.LO[:, 0:8], T.OO[:, 2::3], "OO", "LOa")
         yield
         tt(kwin().indirect(T.LO[:, 0:8]), T.GZ[:], T.UM[:], A.add, "LOa GZ UM", "KN")
         yield
 
     def live(t):
+        pl = eq[0][:, 4, 0:16]
         act(L["nc0"], L["pen"], AF.Sign, "pen", "nc0", bias=-OFS)
         act(L["oy0"], L["po1"], AF.Sign, "po1", "oy0")
+        ts(T.YL[:, 8:16], pl[:, 8:16], OFS, A.add, wr="YLb", ps="e0")
+        yield
         if t:
             cp(T.AI[:, 0:4], T.ML[:, 16 * t - 8:16 * t - 4], "M%d" % (t - 1), "AI0")
-            yield
-            ts(T.AI[:, 4:8], T.AI[:, 0:4], 31, A.bitwise_and, rd="AI0", wr="AI1")
-            yield
-            ts(T.CA[:], T.AI[:, 4:8], WT, A.mult, rd="AI1", wr="CA")
-            yield
-        tt(L["nch"], T.E2[:, 0:8], L["nc0"], A.max, "E2 nc0", "nch")
+        tt(L["nch"], T.E2[:, 1:24:3], L["nc0"], A.max, "E2 nc0", "nch")
         yield
+        if t:
+            ts(T.AI[:, 4:8], T.AI[:, 0:4], 31, A.bitwise_and, rd="AI0", wr="AI1")
         t3("oy", "nch", A.mult, "oy0")
         yield
-        tt(L["dead"], L["oy"], T.E2[:, 8:16], A.max, "oy E2", "dead")
+        if t:
+            ts(T.CA[:], T.AI[:, 4:8], WT, A.mult, rd="AI1", wr="CA")
+        tt(L["dead"], L["oy"], T.E2[:, 25::3], A.max, "oy E2", "dead")
+        yield
         act(T.LIVE[:, 0:8], L["dead"], AF.Identity, "dead", "LIVE", scale=-1.0, bias=1.0)
         act(T.NL[:], L["dead"], AF.Copy, "dead", "NL", scale=BIG)
+        tt(L["bou"], pl[:, 8:16], L["dumo"], A.subtract, "dumo", "bou", "e0")
         yield
+        ts(L["held"], T.OO[:, 2::3], float(NW), A.is_lt, rd="OO", wr="held")
         yield
         tt(T.LX[:], T.LIVE[:].indirect(T.C8[:]), D, A.mult, "LIVE C8 D", "LX")
-        mm(dz[:, 256:384], T.BON[:], T.LX[:], True, True, "BON LX", "dz")
+        mm(eq[3][:, 4:8, :], T.BON[:], T.LX[:], True, True, "BON LX", "e3")
+        yield
+
+    def place(met, rd, out, key):
+        tt(T.PK0[:, 1::2], T.MS2[:, 15::16], met, A.is_equal, "MS2 " + rd, "PK0")
+        yield
+        scan(T.PKO[:], T.PK0[:], T.PK1[:], 0.0, A.mult, A.add, "PK0 PK1a PK1b", "PKO")
+        yield
+        cp(out, T.PKO[:, 1::2], "PKO", key)
         yield
 
     def out_feet(t):
         a, z = lo[t], lo[t] + 128
-        pl = eq[0][:, 4, 0:16]
+        while lines[1]:
+            yield
+        tt(T.MU2[:], fwin().indirect(T.YL[:, 8:16]), D, A.mult, "FX FXa FXb YLb D", "MU2")
         act(T.FVO[:], T.FX[:, a:z], AF.Copy, "FX", "FVO")
-        ts(T.YL[:, 8:16], pl[:, 8:16], OFS, A.add, wr="YLb", ps="e0")
-        tt(L["bou"], pl[:, 8:16], L["dumo"], A.subtract, "dumo", "bou", "e0")
-        yield
-        tt(T.MU2[:], fwin().indirect(T.YL[:, 8:16]), D, A.mult, "FX FXa YLb D", "MU2")
-        ts(L["held"], T.OO[:, 1::2], float(NW), A.is_lt, rd="OO", wr="held")
         yield
         scan(T.MS2[:], RS, T.MU2[:], 0.0, A.mult, A.add, "RS MU2", "MS2")
-        t3("h1", "held", A.mult, "bou")
+        tt(T.PK1[:, 0::2], L["held"], L["bou"], A.mult, "held bou", "PK1a")
         yield
-        tt(L["e1"], T.MS2[:, 15::16], T.NN[:, 8 * t:8 * t + 8], A.is_equal, "MS2 NN", "e1")
-        yield
-        t3("h2", "e1", A.mult, "h1")
-        yield
-        t3("ofu", "h2", A.add, "dum")
-        yield
-        cp(T.LO[:, 8:16], L["ofu"], "ofu", "LOb")
-        yield
+        tt(T.FX[:, a:z], eq[3][:, 4:8, :], T.FX[:, a:z], A.max, "FX", "FX", "e3")
+        read.append("none%d" % t)
+        for _ in place(T.NN[:, 8 * t:8 * t + 8], "NN", T.LO[:, 8:16], "LOb"):
+            yield
         cp(fwin().indirect(T.LO[:, 8:16]), T.FVO[:], "LOb FVO", "FX")
-        yield
-        tt(T.FX[:, a:z], dz[:, 256:384], T.FX[:, a:z], A.max, "FX", "FX", "dz")
         yield
 
     def seat_begin(part):
@@ -436,9 +458,7 @@ def rank_program(g, core, T, topo):
         if t == 0:
             tt(T.TM[:], eq[2][:, 4:8, :], D, A.mult, "D", "TM", "e2")
         else:
-            cp(T.CL[:, 0:8], T.LND[:, 136 * t - 8:136 * t], "Z%d" % (t - 1), "CL")
-            yield
-            tt(T.TM[:], T.TT[:].indirect(T.CL[:, 0:8]), D, A.mult, "TT TTd CL D", "TM")
+            tt(T.TM[:], T.TT[:].indirect(T.CL[:, 8 * t - 8:8 * t]), D, A.mult, "TT TTd D C%d" % t, "TM")
         yield
         scan(T.TS[:], RS, T.TM[:], 0.0, A.mult, A.add, "RS TM", "TS")
         yield
@@ -446,9 +466,9 @@ def rank_program(g, core, T, topo):
         yield
 
     def zrep(t, h):
-        zz, key = (T.Z0, "Z0") if t == 0 else (T.LND[:, 136 * t - 136:136 * t - 8], "Z%d" % (t - 1))
+        a = 128 * t + 64 * h
         for k in range(16):
-            act(T.ZR[:, 1024 * h + k:1024 * h + 1024:16], zz[:, 64 * h:64 * h + 64], AF.Copy, key, "+ZR%d" % h)
+            act(T.ZR[:, 1024 * h + k:1024 * h + 1024:16], T.ZL[:, a:a + 64], AF.Copy, "Z%d%d" % (t, h), "+ZR%d" % h)
 
     def far(t):
         act(T.XW[:, lo[t]:lo[t] + 128], T.ONB[:], AF.Copy, "ONB", "XWp", scale=4096.0)
@@ -466,16 +486,22 @@ def rank_program(g, core, T, topo):
                 u = a + CUTS[c - (c == 2)]
                 act(T.AB[:, u:z, 1:17], T.DIFF[:, 16 * u:16 * z], AF.Abs, "DF%d%d DF%d%d" % (h, c, h, c - (c == 2)), "AB%d%d" % (h, c))
             if next(other, "end") == "end":
-                pull()
+                pull(1)
 
         cp(T.KL[:, a:a + 64], kwin().indirect(bl), "KN " + bk, "KL%d" % h)
-        act(T.XB[:, a:a + 64], T.X[:, 0:NW].indirect(bl), AF.Copy, "X XL " + bk, "XB%d" % h)
-        mm(dz[:, a:a + 64], T.IB[:], T.XB[:, a:a + 64], True, False, "IB XB%d" % h, "dz")
-        mm(dz[:, a:a + 64], T.NIB[:], T.ZR[:, 16 * a:16 * a + 1024:16], False, True, "NIB ZR%d" % h, "dz")
+        def here():
+            act(T.XB[:, a:a + 64], T.X[:, 0:NW].indirect(bl), AF.Copy, "X XL " + bk, "XB%d" % h)
+            mm(dz[:, a:a + 64], T.IB[:], T.XB[:, a:a + 64], True, False, "IB XB%d" % h, "dz")
+            mm(dz[:, a:a + 64], T.NIB[:], T.ZR[:, 16 * a:16 * a + 1024:16], False, True, "NIB ZR%d" % h, "dz")
+
+        if q or h:
+            here()
         mm(k[:, 0:3, 0:68], T.ONB[:], T.CK[:], True, False, "ONB CK", pk)
         mm(k[:, 1:3, 0:34:17], T.IF[:], bf, False, False, "IF " + fk, pk)
         pull()
         gather(0)
+        if not (q or h):
+            here()
         act(T.AB[:, a:a + 64, 0], dz[:, a:a + 64], AF.Abs, "", "AB%ds" % h, "dz")
         ts(T.C16[:, a:a + 64], T.KL[:, a:a + 64], -OFS, A.add, rd="KL%d" % h, wr="C16%d" % h)
         gather(1)
@@ -486,16 +512,16 @@ def rank_program(g, core, T, topo):
                 mm(k[:, 1:3, 17 * c + 1:17 * c + 17], m[:, w:w + 128], T.CT[:, 2 * h:2 * h + 2, 16 * gp:16 * gp + 16], False, False,
                    mk + " CT%d" % h, pk)
         gather(2)
-        pull()
         gather(3)
         if t:
             mm(k[:, 0, 0:68:17], T.IB[:], T.CA[:], False, False, "IB CA", pk)
         for j in range(16):
             mm(k[:, 0, 0:68], T.SW[:, 15 - j:143 - j], T.AB[:, a + j:a + 64:16, :], False, j == 15,
                "SW AB%d0 AB%d2 AB%d3 AB%ds" % (h, h, h, h), pk)
-        pull()
-        next(other, "end")
-        pull()
+        if s or h:
+            pull()
+            next(other)
+            pull()
 
     def least(t, s, h):
         q, k, pk, a = 4 * t + s + 1, kk[h], "k%d" % h, 68 * h
@@ -515,6 +541,11 @@ def rank_program(g, core, T, topo):
         bl, bk = T.BL[:, 16 * q + 4 * h:16 * q + 4 * h + 4], "BL%d%d" % (q, h)
         bf, fk = T.SC[:, 68 * h + 16:68 * h + 68:17], "SC%d" % h
         cnt, pk, c4 = kk[h][:, 3, 0:12], "k%d" % h, slice(4 * h, 4 * h + 4)
+
+        def zsum():
+            mm(dz[:, a:a + 64], T.IB[:], T.XB[:, a:a + 64], True, False, "IB XB%d" % h, "dz")
+            mm(dz[:, a:a + 64], T.IB[:], T.ZR[:, 16 * a:16 * a + 1024:16], False, True, "IB ZR%d" % h, "dz")
+
         if h == 0:
             act(T.CDE[:, 0:64], T.BT[:].indirect(bl), AF.Copy, "BT EV " + bk, "CDE0", scale=EV)
         else:
@@ -525,12 +556,12 @@ def rank_program(g, core, T, topo):
             act(T.BN[:, h, i:i + 4], bf, AF.Copy, fk, "+BN%d" % h)
         act(T.PO[:, c4], L["sq3"][:, c4], AF.Relu, "sq3%d" % h, "PO%d" % h, scale=-64.0, bias=262144.0)
         act(T.XB[:, a:a + 64], T.X[:, 0:NW].indirect(bl), AF.Copy, "X XL " + bk, "XB%d" % h)
-        act(T.VK[:, h, 64:128], kwin().indirect(bl), AF.Copy, "KN " + bk, "VKb%d" % h)
-        act(T.VK[:, h, 0:64], kwin().indirect(bl), AF.Copy, "KN NM0 " + bk, "VKa%d" % h, scale=NM0)
         for gr in range(8):
             r = 32 * (gr // 2)
             cd, ck = (T.CDE, "CDE") if gr % 2 == 0 else (T.CDO, "CDO")
             if h == 0:
+                if gr == 4:
+                    zsum()
                 if gr in (2, 4, 6):
                     need("P", "P", tot["P"])
                 mm(eA[0:64, :, 16 * gr:16 * gr + 16], cd[r:r + 32, 0:64], cd[r:r + 32, 0:64], False, gr == 7, ck + "0", "eA")
@@ -542,11 +573,32 @@ def rank_program(g, core, T, topo):
             mm(cnt[:, i:i + 4], T.IB[:], T.NL[:, c4], False, False, "IB NL", pk)
             mm(cnt[:, i:i + 4], T.IB[:], T.PO[:, c4], False, False, "IB PO%d" % h, pk)
         if h == 0:
-            act(T.VF[:, 256 * t:256 * t + 64], T.ID[:].indirect(bl), AF.Copy, "ID " + bk, "VF0")
-            act(T.EQ[0:64, 0:4, :], eA[0:64], AF.Relu, "", "EQA", "eA", bias=-12.0 + EPS)
+            seat_kin_of(t, 0)
+            seat_z(t, 0)
         else:
+            zsum()
+            if t == VIS - 1:
+                seat_kin_of(t, 1)
             for i in (2, 3):
                 act(T.EQ[:, 4:8, 32 * i:32 * i + 32], eq[i][:, 0:4, :], AF.Relu, "", "EQ%d" % i, "e%d" % i, bias=-12.0 + EPS)
+
+    def seat_kin_of(t, h):
+        bl, bk = T.BL[:, 64 * t + 48 + 4 * h:64 * t + 52 + 4 * h], "BL%d%d" % (4 * t + 3, h)
+        act(T.VK[:, h, 64:128], kwin().indirect(bl), AF.Copy, "KN " + bk, "VKb%d" % h)
+        act(T.VK[:, h, 0:64], kwin().indirect(bl), AF.Copy, "KN NM0 " + bk, "VKa%d" % h, scale=NM0)
+
+    def parents(t):
+        mm(eA[:, 0, :], T.B0[:], T.VK[:, :, 64:128], True, True, "B0 VKb0 VKb1", "eA")
+
+    def seat_z(t, h):
+        a = 128 * t + 64 * h
+        act(T.ZQ[:, 64 * h:64 * h + 64], dz[:, 64 * h:64 * h + 64], AF.Identity, "", "ZQ%d" % h, "dz", scale=0.4999, bias=M0C)
+        act(T.VF[:, 128 * t + a:128 * t + a + 64], T.ID[:].indirect(T.BL[:, 64 * t + 48 + 4 * h:64 * t + 52 + 4 * h]), AF.Copy,
+            "ID BL%d%d" % (4 * t + 3, h), "VF%d" % h)
+        act(T.ZN[:, a:a + 64], T.ZQ[:, 64 * h:64 * h + 64], AF.Identity, "ZQ%d" % h, "ZN%d" % h, bias=-M0C)
+        if t < VIS - 1:
+            send(nxt, T.ZL[:, 128 + a:192 + a], T.ZN[:, a:a + 64], "aZ%d%d" % (h, t), "ZN%d" % h)
+            arrives("aZ%d%d" % (h, t), "Z%d%d" % (t + 1, h))
 
     def seat_count(h):
         for c in range(4):
@@ -563,88 +615,81 @@ def rank_program(g, core, T, topo):
 
     def seat_feet(t):
         v = T.MS3[:, 15::16]
-        tt(T.MV[:], dz[:, 128:256], D, A.mult, "D", "MV", "dz")
+        tt(T.MV[:], eA[:, 0, :], D, A.mult, "D", "MV", "eA")
         yield
         scan(T.MS3[:], RS, T.MV[:], 0.0, A.mult, A.add, "RS MV", "MS3")
         yield
         cp(T.VL[:], v, "MS3", "VL")
-        tt(L["bov"], v, L["dum"], A.subtract, "MS3 dum", "bov")
+        tt(L["bov"], L["dum"], v, A.subtract, "MS3 dum", "bov")
         yield
-        tt(T.MU2[:], fwin().indirect(T.VL[:]), D, A.mult, "FX FXa VL D", "MU2")
-        tt(L["m1"], L["bov"], T.SN[:], A.mult, "bov SN", "m1")
+        tt(T.MU2[:], fwin().indirect(T.VL[:]), D, A.mult, "FX FXa FXb VL D", "MU2")
         yield
+        while seated[0] < t:
+            yield
         scan(T.MS2[:], RS, T.MU2[:], 0.0, A.mult, A.add, "RS MU2", "MS2")
+        tt(T.PK1[:, 0::2], L["bov"], T.SN[:], A.mult, "bov SN", "PK1a")
         yield
-        tt(L["e3"], T.MS2[:, 15::16], T.BN[:, :, 0:4], A.is_equal, "MS2 BN0 BN1", "e3")
+        cp(fwin().indirect(T.LN[:, 0:8]), T.VF[:, 256 * t:256 * t + 128], "LNa VF0 VF1", "FX")
+        for _ in place(T.BN[:, :, 0:4], "BN0 BN1", T.LN[:, 8:16], "LNb"):
+            yield
+        cp(fwin().indirect(T.LN[:, 8:16]), T.VF[:, 256 * t + 128:256 * t + 256], "LNb VFr", "FX")
         yield
-        t3("m2", "m1", A.mult, "e3")
-        yield
-        t3("ofv", "dum", A.subtract, "m2")
-        yield
-        cp(T.LN[:, 8:16], L["ofv"], "ofv", "LNb")
-        yield
-        cp(fwin().indirect(T.LN[:]), T.VF[:, 256 * t:256 * t + 256], "LNa LNb VFr VF0 VF1", "FX")
-        yield
-
-    def seat_z(t):
-        fin = t == VIS - 1
-        zn, znk = (T.ZN[:], "ZN") if fin else (T.SND[:, 136 * t:136 * t + 128], "SND%d" % t)
-        mm(dz[:, 0:128], T.IB[:], T.XB[:], True, False, "IB XB0 XB1", "dz")
-        mm(dz[:, 0:128], T.IB[:], T.ZR[:, 0::16], False, True, "IB ZR0 ZR1", "dz")
-        act(T.ZQ[:], dz[:, 0:128], AF.Identity, "", "ZQ", "dz", scale=0.4999, bias=M0C)
-        if not fin:
-            act(T.SND[:, 136 * t + 128:136 * t + 136], T.SC[:, 16::17], AF.Copy, "SC0 SC1", "SNb%d" % t)
-        act(zn, T.ZQ[:], AF.Identity, "ZQ", znk, bias=-M0C)
-        if not fin:
-            send(nxt, T.LND[:, 136 * t:136 * t + 136], T.SND[:, 136 * t:136 * t + 136], "aZ%d" % t, "%s SNb%d" % (znk, t))
-            arrives("aZ%d" % t, "Z%d" % t)
-        act(T.VF[:, 256 * t + 64:256 * t + 128], T.ID[:].indirect(T.BL[:, 64 * t + 52:64 * t + 56]), AF.Copy, "ID BL%d1" % (4 * t + 3), "VF1")
-        mm(dz[:, 128:256], T.B0[:], T.VK[:, :, 64:128], True, True, "B0 VKb0 VKb1", "dz")
 
     def seat_rest(t):
         fin = t == VIS - 1
         a, m0 = lo[t], 16 * t
-        zn, znk = (T.ZN[:], "ZN") if fin else (T.SND[:, 136 * t:136 * t + 128], "SND%d" % t)
+        zn, znk = T.ZN[:, 128 * t:128 * t + 128], "ZN0 ZN1"
+        seated[0] = t
         ts(T.SN[:], T.OF[:, :, 0:4], float(NW), A.is_lt, -1.0, A.mult, rd="OF0 OF1", wr="SN")
         cp(T.LN[:, 0:8], T.OF[:, :, 4:8], "OF0 OF1", "LNa")
         if not fin:
             mm(dz[:, 384:392], T.ONB[:], T.LIVE[:, 0:8], True, False, "ONB LIVE", "dz")
             mm(dz[:, 384:392], T.ONB[:], T.SN[:], False, True, "ONB SN", "dz")
             act(T.MS[:, m0:m0 + 8], T.OF[:, :, 8:12], AF.Copy, "OF0 OF1", "MS")
-            act(T.AQ[:], dz[:, 384:392], AF.Copy, "", "AQ AS", "dz", accum_out=AS)
+            act(L["aq"], dz[:, 384:392], AF.Copy, "", "AQ AS", "dz", accum_out=AS)
             act(T.MS[:, m0 + 8:m0 + 12], T.ONB[:, 0:4], AF.Copy, "ONB AS", "MSa", scale=AS)
             send(nxt, T.ML[:, m0:m0 + 16], T.MS[:, m0:m0 + 16], "aM%d" % t, "MS MSa")
             arrives("aM%d" % t, "M%d" % t)
+            zrep(t + 1, 0)
         yield
         if t in (1, 2):
             cp(T.TT[:].indirect(T.L8[:]), T.VF[:, 256 * t:256 * t + 128], "L8 VF0 VF1", "TT TTd")
-            yield
-        cp(T.X[:].indirect(T.LN[:, 0:8]), zn, "LNa " + znk, "X XL")
+        if fin:
+            act(T.OR[:], T.ID[:].indirect(T.CL[:, 24:32]), AF.Copy, "ID C4", "OR")
+        yield
+        yield
+        cp(T.X[:].indirect(T.LN[:, 0:8]), zn, "LNa " + znk, "X XL Xt")
         if not fin:
             act(T.XW[:, a:a + 128], T.X[:, a:a + 128], AF.Copy, "X", "XW")
-            zrep(t + 1, 0)
-            zrep(t + 1, 1)
+        yield
         yield
         if not fin:
             for _ in start(t + 1):
                 yield
             if t == 2:
                 cp(T.L8[:], T.OF[:, :, 8:12], "OF0 OF1", "L8")
+        else:
+            cp(T.OT[:].indirect(T.L8[:]), T.OR[:], "L8 OR", "OT")
 
     def convert(i):
         a, z = KCH[i]
         cp(T.KN[:, a:z], T.KI[:, a:z], "KI%d" % i, "+KN")
 
-    zrep(0, 0)
-    far(0)
+    def converts():
+        for i in range(2, len(KCH)):
+            convert(i)
+            yield
+
     convert(0)
-    lines[:] = [[out_before(0)], [start(0)]]
-    drain()
+    convert(1)
+    lines[:] = [[out_before(0)], [converts()], [late(), later()], [start(0)]]
+    while lines[0] or lines[1]:
+        pull()
+    zrep(0, 0)
     zrep(0, 1)
-    for i in (1, 2, 3):
-        convert(i)
-    lines[:] = [[out(0)], [late()]]
+    lines[0] = [out(0)]
     drain()
+    far(0)
     for t in range(VIS):
         fin = t == VIS - 1
         if fin:
@@ -660,49 +705,69 @@ def rank_program(g, core, T, topo):
                 for h in range(2):
                     act(T.BN[:, h, 4:8], T.J8[:, 4 * h:4 * h + 4], AF.Identity, "J8", "+BN%d" % h, bias=float(lo[t]))
             if i in (2, 3, 4):
+                while lines[1]:
+                    pull(1)
+                while i == 4 and "none%d" % t not in read:
+                    pull()
                 seat_begin(i - 2)
         seat_sums(t, 0)
-        seat_count(0)
         if t in (1, 2):
             cp(T.L8[:], T.ML[:, 16 * (t - 1):16 * (t - 1) + 8], "M%d" % (t - 1), "L8")
-        for _ in range(3):
+        while lines[0] and (fin or -t - 1 not in read):
             pull()
-        for _ in other:
+        act(T.EQ[0:64, 0:4, :], eA[0:64], AF.Relu, "", "EQA", "eA", bias=-12.0 + EPS)
+        for i, _ in enumerate(other):
             pull()
-        if fin:
-            send(prv, T.CL[:, 8:16], T.BL[:, 64 * t + 48:64 * t + 56], "aB", "BL%d0 BL%d1" % (4 * t + 3, 4 * t + 3))
-        else:
-            far(t + 1)
+            if i == 1:
+                seat_count(0)
+        send(prv if fin else nxt, T.CL[:, 8 * t:8 * t + 8], T.BL[:, 64 * t + 48:64 * t + 56], "aB" if fin else "aC%d" % t,
+             "BL%d0 BL%d1" % (4 * t + 3, 4 * t + 3))
+        arrives("aB" if fin else "aC%d" % t, "C%d" % (t + 1))
         seat_sums(t, 1)
         first, second = seat_kin(t, 0), seat_kin(t, 1)
         next(first)
-        drain()
+        pull()
         next(first)
+        pull()
+        while not fin and lines[0] and t + 1 not in read:
+            pull()
         for i in (0, 1):
             ts(T.EQ[:, 4:8, 32 * i:32 * i + 32], eq[i][:, 0:4, :], -12.0 + EPS, A.add, 0.0, A.max, wr="EQ%d" % i, ps="e%d" % i)
+        if fin:
+            parents(t)
+            lines[:] = [[seat_feet(t)]]
         seat_count(1)
-        seat_z(t)
+        if fin:
+            pull()
         next(first)
+        if not fin:
+            seat_kin_of(t, 1)
+            parents(t)
+        seat_z(t, 1)
+        pull()
         next(second)
-        lines[:] = [[second] + ([] if fin else [out(t + 1)]), [seat_rest(t)] + ([seat_feet(t)] if fin else [])]
+        if fin:
+            lines[1:] = [[second], [seat_rest(t)]]
+        else:
+            far(t + 1)
+            lines[1:] = [[second, out(t + 1)], [seat_rest(t)]]
         drain()
+        if not fin:
+            zrep(t + 1, 1)
         if t == 2:
             dma("Y", "tb", T.TB[:], T.TT[0::16, 0:NW], rd="TT", wr="TB")
             send(prv, T.TBL[:], T.TB[:], "aTB", "TB")
             arrives("aTB", "TBL")
             dma("Y", "ot", T.OT[0::16, 0:NW], T.TBL[:], rd="TBL", wr="OT")
     a = lo[VIS - 1]
-    arrives("aB", "CLB")
-    act(T.OR[:], T.ID[:].indirect(T.CL[:, 8:16]), AF.Copy, "ID CLB", "OR")
-    dma("Y", "out", T.yz[:], T.ZN[:], rd="ZN")
+    dma("Y", "out", T.yz[:], T.ZN[:, 384:512], rd="ZN0 ZN1")
     dma("Y", "out", T.yp[:], T.KN[0::16, 0:NB], rd="KN")
     dma("S", "out", T.yk[:, a - NB:a - NB + 128], T.KN[:, a:a + 128], rd="KN", wr="yk")
     for u, z in ((NB, a), (a + 128, NW)):
         if z > u:
             dma("Y", "out", T.yk[0::16, u - NB:z - NB], T.KN[0::16, u:z], rd="KN", wr="yk")
     dma("Y", "out", T.yx[:, a - NB:a - NB + 128], T.X[:, a:a + 128], rd="X", wr="yx")
-    cp(T.OT[:].indirect(T.L8[:]), T.OR[:], "L8 OR", "OT")
+    dma("Y", "out", T.yt[:], T.OT[0::16, 0:NW], rd="OT")
     dma("S", "out", T.yf[:], T.FX[0::16, NB:NW], rd="FX")
-    dma("S", "out", T.yt[:], T.OT[0::16, 0:NW], rd="OT")
     for s in list(tot):
         need("G", s, tot[s])

@@ -6,19 +6,21 @@ DA, DB = 3600, 3728
 WT, SL = 131072.0, 4096
 BIG = 4096.0
 OFS = 1792.0
+SAT = 2
 M0C = 1.5 * 2.0 ** 23
 EPS = 2.0 ** -20
-CUTS = (0, 28, 40, 52, 64)
-LISTS = "y1 po1 por sq1 sqr ne pe pen d1 nc0 oy0 nch oy dead bov bou held dum dumo sq3 aq".split()
+CUTS = (0, 24, 32, 40, 48)
+ABS = {0: 0, 2: 1, 3: 3}
+LISTS = "d0 d1 e0 c0 cn ch ny bov bou held dum ndum sq3 aq".split()
 BUFS = {
     "float32": "KN:3856 FX:3856 TT:3856 OT:3856 ID:3584 TRF:224 ML:48 MS:48 COLF:16 CF:160 C15F:128 CGF:128 D:128 B0:128 IF:128 RG8:128 "
                "R0:68 RS:128 I8:8 J8:8 NN:32 NR:1024 VF:1024 FVO:128 TM:128 TS:128 MU:128 MS1:128 GZ:128 UM:128 "
-               "MU2:128 MS2:128 MS3:128 MV:128 SM:192 OR:128 VM:136 GG:136 BB:136 SC:136 ZQ:128 "
-               "BF8:128 RPI:128 CMP:16 E2:48 A1:24 AO:24 B1:24 OO:24 PK0:16 PK1:16 PKO:16",
-    "bfloat16": "X:3856 XW:3584 BT:4096 ZL:512 ZN:512 ZR:2048 IB:128 NIB:128 ONB:128 BON:128 SW:144 CK:204 CW:4 CA:4 BCB:1024 DIFF:2048 "
+               "MU2:128 MS2:128 MS3:128 MV:128 SM:112 OR:128 VM:136 GG:136 BB:136 SC:136 N0:136 ZQ:128 "
+               "BF8:128 BIT:8 RPI:128 CMP:16 E2:32 A1:32 OO:32 SQ:16 NO:16 PK0:16 PK1:16 PKO:16",
+    "bfloat16": "X:3856 XW:3584 BT:4096 ZL:512 ZN:512 ZR:2048 IB:128 NIB:128 ONB:128 BON:128 SW:144 CK:68 CW:4 BCB:1024 DIFF:2048 "
                 "XB:128 CDE:128 CDO:128 LIVE:16 LX:128 SN:8 NL:8 PO:8 NUA:512 NUB:128 RG:512 RP:128",
     "float16": "C16:128 C2:256 IE:160 IO:160 RH8:128 F16:1024",
-    "int32": "KI:3584 FI:1024 BI:128 TRI:224 CI:128 C15:128 CG:128 COLI:4 NI:64 BC:768 AI:8 C8I:8",
+    "int32": "KI:3584 FI:1024 BI:128 TRI:224 COLI:4 BC:8 AI:8 C8I:8",
     "uint16": "CL:32 BL:256 KL:128 YL:16 LO:16 VL:8 LS:16 LN:16 L8:8 C8:8",
 }
 SCRATCH = {"TD": ("dram", [128, 224], "float32"), "TB": ("dram", [128, 224], "float32"), "TBL": ("dram", [128, 224], "float32"),
@@ -35,7 +37,7 @@ for _i in range(4):
     SCRATCH["e%d" % _i] = ("psum", [128, 16, 32], "float32")
 for _i in range(2):
     SCRATCH["k%d" % _i] = ("psum", [128, 4, 128], "float32")
-KCH = [(a % NW, a % NW + 512) for a in range(NB, NB + NW, 512)]
+KCH = [(NB, NW), (0, 1024), (1024, 2048), (2048, NB)]
 SEMAPHORES = (["V", "S", "P", "G", "lx", "lw", "lf", "lb", "lz", "lt", "btd", "bt", "tt", "tb", "ot", "out", "early", "aT", "aB", "aTB", "loc"]
               + ["kn%d" % i for i in range(len(KCH))] + ["a%s%d" % (k, t) for k in ("C", "Z0", "Z1", "M") for t in range(3)])
 
@@ -162,8 +164,8 @@ def rank_program(g, core, T, topo):
     def t3(out, a, o, b):
         tt(L[out], L[a], L[b], o, a + " " + b, out)
 
-    dma("S", "lf", T.FI[0:8, :], T.ft[:], wr="FI")
-    dma("S", "lb", T.BI[0:8, :], T.bs[:], wr="BI")
+    dma("Y", "lf", T.FI[0:8, :], T.ft[:], wr="FI")
+    dma("Y", "lb", T.BI[0:8, :], T.bs[:], wr="BI")
     dma("S", "lz", T.ZL[:, 0:128], T.z0[:], wr="Z00 Z01")
     dma("S", "lt", T.TRI[:], T.tr[:], wr="TRI")
     for i, (a, z) in enumerate(KCH):
@@ -172,36 +174,34 @@ def rank_program(g, core, T, topo):
     dma("Y", "lx", T.X[:, 0:NW], T.x0[:], wr="XL")
 
     iota(PI, [[0, 1]], 0, 1, "PI", False)
-    iota(T.CI[:], [[1, 128]], 0, 0, "CI", False)
     iota(PF, [[0, 1]], 0, 1, "PF")
-    iota(T.CF[:], [[1, 160]], 0, 0, "CF")
-    iota(T.NI[0:64, :], [[1, 64]], 0, 64, "NI", False)
+    iota(T.CGF[:], [[1, 8], [0, 16]], 0, 0, "CGF")
     iota(T.I8[:], [[16, 8]], 0, 0, "I8")
-    iota(T.C8I[:], [[1, 8]], 0, 0, "C8I", False)
+    iota(T.C15F[:], [[0, 8], [1, 16]], 0, 0, "C15F")
+    iota(T.CF[:], [[1, 160]], 0, 0, "CF")
     fill(T.CK[:], 0.0, "CK")
     fill(RS, 1.0, "RS")
     fill(T.R0[:], -1.0e9, "R0")
     fill(T.ONB[:], 1.0, "ONB")
-    fill(T.B1[:], 1.0e9, "B1")
-    fill(T.E2[:], 0.0, "E2")
-    fill(T.CK[0:1, 68:204], OFS, "CK")
+    fill(T.E2[:, 0::4], 0.0, "E2")
+    fill(T.E2[:, 2::4], 1.0, "+E2")
+    fill(T.A1[:, 2::4], 0.0, "A1c")
+    fill(T.N0[:], OFS, "N00 N01")
     fill(T.RS[:, 0::16], 0.0, "RS")
     fill(T.R0[:, 0::17], 1.0e9, "R0")
-    fill(L["pen"], BIG + OFS, "pen")
-    fill(T.CK[0:1, 68:204:17], 0.0, "CK")
+    fill(L["c0"], 0.0, "c0")
     iota(T.CK[0:1, 0:68], [[0, 4], [SL, 17]], 0, 0, "CK")
     iota(T.KN[:, NW:WN], [[0, WN - NW]], -1, 0, "KNt")
     ts(P15I, PI, 15, A.bitwise_and, rd="PI", wr="P15I")
     ts(PGI, PI, 4, A.arith_shift_right, rd="PI", wr="PGI")
     ts(PEI, PI, 4, A.arith_shift_right, 1, A.bitwise_and, rd="PI", wr="PEI")
-    ts(T.CG[:], T.CI[:], 4, A.arith_shift_right, rd="CI", wr="CG")
-    ts(T.C15[:], T.CI[:], 15, A.bitwise_and, rd="CI", wr="C15")
+    for b in range(6):
+        ts(T.BC[0:64, b:b + 1], PI[0:64, :], b, A.arith_shift_right, 1, A.bitwise_and, rd="PI", wr="+BC")
     cp(P15, P15I, "P15I", "P15")
     cp(PG, PGI, "PGI", "PG")
     cp(OD, PEI, "PEI", "OD")
-    cp(T.CGF[:], T.CG[:], "CG", "CGF")
-    cp(T.C15F[:], T.C15[:], "C15", "C15F")
     ts(P16, PF, 16.0, A.add, rd="PF", wr="P16")
+    ts(T.BIT[0:64, 0:6], T.BC[0:64, 0:6], 2.0, A.mult, rd="BC", wr="BIT")
     ts(T.RH8[:], T.CGF[:], PF, A.is_equal, rd="CGF PF", wr="RH8")
     ts(T.RG8[:], T.CGF[:], PF, A.is_equal, rd="CGF PF", wr="RG8")
     ts(M0, P15, 0.0, A.is_equal, rd="P15", wr="M0")
@@ -224,7 +224,8 @@ def rank_program(g, core, T, topo):
     ts(T.IO[:], T.CF[:], P16, A.is_equal, OD, A.mult, rd="CF P16 OD", wr="IO")
     ts(T.IF[:], T.CF[:, 0:128], PF, A.is_equal, rd="CF PF", wr="IF")
     ts(T.SW[:], T.CF[:, 0:144], PW, A.is_equal, WT, A.mult, rd="CF PW", wr="SW")
-    for out, d, key in ((L["dum"], DA, "dum"), (L["dumo"], DA - OFS, "dumo"), (T.A1[:, 2::3], DA, "A1c"), (T.PK1[:, 1::2], DA, "PK1b"),
+    act(L["ndum"], T.J8[:], AF.Identity, "J8", "ndum", scale=-1.0, bias=OFS - DA)
+    for out, d, key in ((L["dum"], DA, "dum"), (T.A1[:, 3::4], DA, "A1d"), (T.PK1[:, 1::2], DA, "PK1b"),
                         (T.DUM[:, :, 0:4], DA, "DUM"), (T.DUM[:, :, 4:8], DB, "+DUM"), (T.DUM[:, :, 8:12], DA, "+DUM")):
         act(out, T.J8[:], AF.Identity, "J8", key, bias=float(d))
     for t in range(VIS):
@@ -234,19 +235,26 @@ def rank_program(g, core, T, topo):
     last["XWp"] = last["XW"]
 
     iota(T.RPI[:], [[0, 4], [1, 2], [0, 16]], 0, 0, "RPI")
+    iota(T.C8I[:], [[1, 8]], 0, 0, "C8I", False)
+    for b in range(6):
+        iota(T.BCB[0:64, 64 * b:64 * b + 64], [[0, 32 >> b], [2, 2], [0, 1 << b]], -1, 0, "+BCa")
+        act(T.BCB[0:64, 384 + 64 * b:448 + 64 * b], T.ONB[0:64, 0:64], AF.Identity, "ONB BIT", "+BCb", scale=T.BIT[0:64, b:b + 1], bias=-1.0)
+    iota(T.BCB[0:64, 768:1024], [[0, 256]], 0, 0, "+BCa")
     iota(T.FX[:, 0:NB], [[0, NB]], -1, 0, "FXa")
 
     def constants_g():
         iota(T.NUA[:], [[0, 512]], -32, 0, "NUA")
-        iota(T.NUB[:], [[0, 128]], -32, 0, "NUB")
-        iota(T.RG[:], [[0, 512]], 1, 0, "RG")
+        iota(T.FX[:, NW:WN], [[0, WN - NW]], -1, 0, "FXb")
         keep(T.NUA[:], [[-16, 4], [0, 8], [-1, 16]], 0, 1, "NUA")
+        iota(T.RG[:], [[0, 512]], 1, 0, "RG")
+        iota(T.NUB[:], [[0, 128]], -32, 0, "NUB")
         keep(T.RG[:], [[0, 4], [-16, 8], [0, 16]], 0, 1, "RG")
         keep(T.NUB[:], [[-16, 4], [0, 2], [-1, 16]], -64, 1, "NUB")
         keep(T.RG[:], [[0, 4], [16, 8], [0, 16]], 15, -1, "RG")
-        iota(T.FX[:, NW:WN], [[0, WN - NW]], -1, 0, "FXb")
-        iota(T.TT[:, NW:WN], [[0, WN - NW]], 0, 0, "TT")
         iota(T.ID[:], [[1, NW]], 0, 0, "ID")
+        iota(T.EQ[:, 0:4, :], [[0, 512]], 0, 0, "EQz EQA")
+        iota(T.X[:, NW:WN], [[0, WN - NW]], 0, 0, "Xt")
+        iota(T.TT[:, NW:WN], [[0, WN - NW]], 0, 0, "TT")
 
     def kwin():
         return T.KN[:, 0:WN]
@@ -261,51 +269,39 @@ def rank_program(g, core, T, topo):
             while line and next(line[0], "end") == "end":
                 line.pop(0)
 
-    def drain():
-        while any(lines):
-            pull()
-
     def late():
+        for _ in range(4):
+            yield
         cp(T.TRF[:], T.TRI[:], "TRI", "TRF")
         send(nxt, T.TD[:], T.TRF[:], "aT", "TRF")
         arrives("aT", "TD")
         constants_g()
-        yield
-        fill(T.BCB[0:64, 768:1024], 0.0, "BCB")
-        yield
-        for b in range(12):
-            ts(T.BC[0:64, 64 * b:64 * b + 64], T.NI[0:64, :], b, A.arith_shift_right, 1, A.bitwise_and, rd="NI", wr="+BC")
-            if b % 3 == 2:
-                yield
-        for i in range(3):
-            ts(T.BCB[0:64, 256 * i:256 * i + 256], T.BC[0:64, 256 * i:256 * i + 256], 2.0, A.mult, -1.0, A.add, rd="BC", wr="+BCB")
-            yield
         for b in range(16):
-            dma("Y", "btd", T.BTD[b], T.BCB[0:64, 64 * b:64 * b + 64], rd="BCB", wr="BTD")
+            dma("Y", "btd", T.BTD[b], T.BCB[0:64, 64 * b:64 * b + 64], rd="BCa BCb", wr="BTD")
         for i in range(8):
             dma("Y", "bt", T.BT[16 * i:16 * i + 16, :], T.BTD[:], rd="BTD", wr="BT")
         for p in range(16):
             dma("Y", "tt", T.TT[p::16, 0:NW], T.TD[:], rd="TD", wr="TTd")
+        yield
+        yield
+        yield
+        ts(T.BON[:], T.CGF[:], PG, A.is_equal, float(NW), A.mult, rd="CGF PG", wr="BON")
+        act(T.B0[:], T.BON[:], AF.Copy, "BON M0", "B0", scale=M0)
+        act(T.B0[:], T.B0[:], AF.Sign, "B0", "B0")
+        yield
         fill(T.LIVE[:], 0.0, "LIVE")
         cp(T.C8[:], T.C8I[:], "C8I", "C8")
         fill(T.PK0[:], 0.0, "PK0")
         yield
-        ts(T.BON[:], T.CGF[:], PG, A.is_equal, float(NW), A.mult, rd="CGF PG", wr="BON")
-        yield
-
-    def later():
-        feet(1 - rank // 4)
-        yield
-        ts(T.B0[:], T.CGF[:], PG, A.is_equal, M0, A.mult, rd="CGF PG M0", wr="B0")
         ts(T.RP[:], T.RPI[:], OD, A.is_equal, rd="RPI OD", wr="RP")
-        yield
-        fill(T.EQ[64:128, 0:4, :], 0.0, "EQz")
         yield
         fill(T.CW[:, 0:2], BIG, "CW")
         fill(T.CW[:, 2:4], BIG / EPS, "+CW")
         fill(T.MS[:], 0.0, "MS")
         yield
-        fill(T.X[:, NW:WN], 0.0, "Xt")
+
+    def later():
+        feet(1 - rank // 4)
         yield
 
     def rows(t):
@@ -321,12 +317,9 @@ def rank_program(g, core, T, topo):
                 w = 16 + 16 * (c - gp)
                 mm(out[:, 2 * b0 + c:2 * b1:2], m[:, w:w + 128], T.CT2[:, b0:b1, 16 * gp], gp == 0, gp == 1, mk + " CT2", pk)
 
-    def mine(out, sq):
-        act(L[out], L[sq], AF.Relu, sq, out, scale=-64.0, bias=262144.0)
-
     def out_before(t):
         a, z = lo[t], lo[t] + 128
-        y0, pl = T.MS1[:, 15::16], dz[:, 400:416]
+        y0, pl = T.MS1[:, 15::16], dz[:, 64:80]
         tt(T.MU[:], T.FX[:, a:z], D, A.mult, "FX D", "MU")
         act(T.CMP[:, 0:8], T.J8[:], AF.Identity, "J8", "CMPa", bias=a - OFS)
         yield
@@ -334,36 +327,35 @@ def rank_program(g, core, T, topo):
         ts(T.C2[:, 128:256], T.KN[:, a:z], -OFS, A.add, rd="KN", wr="C2b")
         yield
         cp(T.YL[:, 0:8], y0, "MS1", "YLa")
-        act(L["sq1"], y0, AF.Square, "MS1", "sq1", bias=-a - 63.5)
+        tt(L["d0"], y0, L["dum"], A.subtract, "MS1 dum", "d0")
+        act(T.SQ[:, 0:8], y0, AF.Square, "MS1", "SQ", bias=-a - 63.5)
+        act(T.SQ[:, 8:16], y0, AF.Square, "MS1", "+SQ", bias=-lo[t - 1] - 63.5)
         if t:
-            act(L["sqr"], y0, AF.Square, "MS1", "sqr", bias=-lo[t - 1] - 63.5)
-        mine("po1", "sq1")
-        if t:
-            mine("por", "sqr")
-            read.append(-t)
             yield
             ts(T.C2[:, 0:128], kwin().indirect(T.YL[:, 0:8]), -OFS, A.add, rd="KN YLa", wr="C2a")
             read.append(t)
         yield
+        while t and "end%d" % (t - 1) not in read:
+            yield
         b0 = 0 if t else 4
         turn32(T.CT2[:, b0:8, :], T.C2[:, 32 * b0:256], "C2a C2b", "CT2")
         to_list(pl, b0, 8, "dz")
         yield
+        ts(T.NO[:], T.SQ[:], 4096.0, A.is_ge, rd="SQ", wr="NO")
         yield
         if t:
-            tt(L["ne"], pl[:, 0:8], T.CMP[:, 0:8], A.not_equal, "CMPa", "ne", "dz")
+            tt(L["e0"], pl[:, 0:8], T.CMP[:, 0:8], A.is_equal, "CMPa", "e0l", "dz")
         ts(T.CMP[:, 8:16], pl[:, 8:16], a - OFS - 0.5, A.max, z - OFS - 0.5, A.min, wr="CMPb", ps="dz")
+        tt(L["d1"] if t else T.A1[:, 0::4], L["d0"], T.NO[:, 0:8], A.mult, "d0 NO", "d1 A1a")
         yield
-        tt(L["y1"], y0, L["po1"], A.add, "MS1 po1", "y1")
         if t:
-            ts(L["pe"], L["ne"], BIG, A.mult, OFS, A.add, rd="ne", wr="pe")
-        yield
-        tt(L["d1"], L["y1"], T.CMP[:, 0:8], A.subtract, "y1 CMPa", "d1")
-        if t:
-            t3("pen", "pe", A.add, "por")
-        yield
-        tt(T.A1[:, 0::3], L["d1"], L["pen"], A.subtract, "d1 pen", "A1a")
-        yield
+            tt(L["c0"], L["e0"], T.NO[:, 8:16], A.mult, "e0l NO", "c0")
+            yield
+            ts(L["cn"], L["c0"], float(a - DA), A.mult, rd="c0", wr="cn")
+            tt(T.A1[:, 2::4], L["c0"], L["ndum"], A.mult, "c0 ndum", "A1c")
+            yield
+            tt(T.A1[:, 0::4], L["d1"], L["cn"], A.subtract, "d1 cn", "A1a")
+            yield
 
     def out(t):
         a, z = lo[t], lo[t] + 128
@@ -379,42 +371,41 @@ def rank_program(g, core, T, topo):
         to_list(pl, 0, 8, "e0")
         yield
         yield
-        tt(T.E2[:, 1::3], pl, T.CMP[:], A.is_equal, "CMPa CMPb", "E2", "e0")
-        tt(T.A1[:, 1::3], pl[:, 0:8], L["pen"], A.add, "pen", "A1b", "e0")
+        tt(T.E2[:, 1::4], pl[:, 0:8], T.CMP[:, 0:8], A.is_equal, "CMPa", "E2a", "e0")
+        tt(T.A1[:, 1::4], pl[:, 0:8], L["c0"], A.mult, "c0", "A1b", "e0")
+        tt(T.E2[:, 3::4], pl[:, 8:16], T.CMP[:, 8:16], A.not_equal, "CMPb", "E2b", "e0")
+        read.append("met%d" % t)
         yield
-        tt(T.B1[:, 2::3], T.E2[:, 25::3], L["dum"], A.mult, "E2 dum", "B1")
-        scan(T.AO[:], T.E2[:, 0:24], T.A1[:], 0.0, A.mult, A.add, "E2 A1a A1b A1c", "AO")
+        scan(T.OO[:], T.E2[:], T.A1[:], 0.0, A.mult, A.add, "E2 E2a E2b A1a A1b A1c A1d", "OO")
         yield
-        scan(T.OO[:], T.B1[:], T.AO[:], 0.0, A.max, A.min, "B1 AO", "OO")
-        yield
-        cp(T.LO[:, 0:8], T.OO[:, 2::3], "OO", "LOa")
+        cp(T.LO[:, 0:8], T.OO[:, 3::4], "OO", "LOa")
         yield
         tt(kwin().indirect(T.LO[:, 0:8]), T.GZ[:], T.UM[:], A.add, "LOa GZ UM", "KN")
         yield
 
     def live(t):
         pl = eq[0][:, 4, 0:16]
-        act(L["nc0"], L["pen"], AF.Sign, "pen", "nc0", bias=-OFS)
-        act(L["oy0"], L["po1"], AF.Sign, "po1", "oy0")
+        while "met%d" % t not in read:
+            yield
         ts(T.YL[:, 8:16], pl[:, 8:16], OFS, A.add, wr="YLb", ps="e0")
+        tt(L["bou"], pl[:, 8:16], L["ndum"], A.add, "ndum", "bou", "e0")
         yield
+        tt(L["ch"], L["c0"], T.E2[:, 1::4], A.is_gt, "c0 E2a", "ch")
+        yield
+        tt(L["ny"], L["ch"], T.NO[:, 0:8], A.max, "ch NO", "ny")
+        ts(L["held"], T.OO[:, 3::4], float(NW), A.is_lt, rd="OO", wr="held")
+        yield
+        tt(T.LIVE[:, 0:8], L["ny"], T.E2[:, 3::4], A.mult, "ny E2b", "LIVE")
+        yield
+        while "walk%d" % t not in read:
+            yield
+        act(T.NL[:], T.LIVE[:, 0:8], AF.Identity, "LIVE", "NL", scale=-BIG, bias=BIG)
         if t:
             cp(T.AI[:, 0:4], T.ML[:, 16 * t - 8:16 * t - 4], "M%d" % (t - 1), "AI0")
-        tt(L["nch"], T.E2[:, 1:24:3], L["nc0"], A.max, "E2 nc0", "nch")
-        yield
-        if t:
+            yield
             ts(T.AI[:, 4:8], T.AI[:, 0:4], 31, A.bitwise_and, rd="AI0", wr="AI1")
-        t3("oy", "nch", A.mult, "oy0")
-        yield
-        if t:
-            ts(T.CA[:], T.AI[:, 4:8], WT, A.mult, rd="AI1", wr="CA")
-        tt(L["dead"], L["oy"], T.E2[:, 25::3], A.max, "oy E2", "dead")
-        yield
-        act(T.LIVE[:, 0:8], L["dead"], AF.Identity, "dead", "LIVE", scale=-1.0, bias=1.0)
-        act(T.NL[:], L["dead"], AF.Copy, "dead", "NL", scale=BIG)
-        tt(L["bou"], pl[:, 8:16], L["dumo"], A.subtract, "dumo", "bou", "e0")
-        yield
-        ts(L["held"], T.OO[:, 2::3], float(NW), A.is_lt, rd="OO", wr="held")
+            yield
+            ts(T.CK[0:1, 0::17], T.AI[0:1, 4:8], WT, A.mult, rd="AI1", wr="CK")
         yield
         tt(T.LX[:], T.LIVE[:].indirect(T.C8[:]), D, A.mult, "LIVE C8 D", "LX")
         mm(eq[3][:, 4:8, :], T.BON[:], T.LX[:], True, True, "BON LX", "e3")
@@ -445,12 +436,17 @@ def rank_program(g, core, T, topo):
         cp(fwin().indirect(T.LO[:, 8:16]), T.FVO[:], "LOb FVO", "FX")
         yield
 
-    def seat_begin(part):
-        if part == 0:
+    def seat_begin(t, i):
+        while i == 3 and lines[1]:
+            pull(1)
+        while i == 5 and "none%d" % t not in read:
+            pull()
+        if i == 2:
             mm(eA[0:64], T.IB[:, 0:64], T.NUA[:], True, False, "IB NUA", "eA")
+        elif i == 3:
             mm(eA[0:64], T.LX[:, 0:64], T.RG[:], False, False, "LX RG", "eA")
-        else:
-            for q in (2 * part - 2, 2 * part - 1):
+        elif i > 3:
+            for q in (2 * i - 8, 2 * i - 7):
                 mm(eq[q][:, 0:4, :], T.IB[:], T.NUB[:], True, False, "IB NUB", "e%d" % q)
                 mm(eq[q][:, 0:4, :], T.LX[32 * q:32 * q + 32, :], T.RP[32 * q:32 * q + 32, :], False, False, "LX RP", "e%d" % q)
 
@@ -482,44 +478,51 @@ def rank_program(g, core, T, topo):
             u, z = a + CUTS[c], a + CUTS[c + 1]
             tt(T.DIFF[:, 16 * u:16 * z], T.XW[:].indirect(T.KL[:, u:z]), T.ZR[:, 16 * u:16 * z], A.subtract,
                "XW XWp KL%d ZR%d" % (h, h), "DF%d%d" % (h, c))
-            if c != 1:
-                u = a + CUTS[c - (c == 2)]
-                act(T.AB[:, u:z, 1:17], T.DIFF[:, 16 * u:16 * z], AF.Abs, "DF%d%d DF%d%d" % (h, c, h, c - (c == 2)), "AB%d%d" % (h, c))
-            if next(other, "end") == "end":
+            if c in ABS:
+                u = a + CUTS[ABS[c]]
+                if c == len(CUTS) - 2:
+                    readers["AB%d" % h] = {}
+                act(T.AB[:, u:z, 1:17], T.DIFF[:, 16 * u:16 * z], AF.Abs, "DF%d%d" % (h, c), "+AB%d" % h)
+            if c < 4 and next(other, "end") == "end":
                 pull(1)
 
-        cp(T.KL[:, a:a + 64], kwin().indirect(bl), "KN " + bk, "KL%d" % h)
-        def here():
-            act(T.XB[:, a:a + 64], T.X[:, 0:NW].indirect(bl), AF.Copy, "X XL " + bk, "XB%d" % h)
-            mm(dz[:, a:a + 64], T.IB[:], T.XB[:, a:a + 64], True, False, "IB XB%d" % h, "dz")
-            mm(dz[:, a:a + 64], T.NIB[:], T.ZR[:, 16 * a:16 * a + 1024:16], False, True, "NIB ZR%d" % h, "dz")
+        def keys(j0, j1):
+            for j in range(j0, j1):
+                mm(k[:, 0, 0:68], T.SW[:, 15 - j:143 - j], T.AB[:, a + j:a + 64:16, :], False, j == 15, "SW AB%d" % h, pk)
 
-        if q or h:
-            here()
-        mm(k[:, 0:3, 0:68], T.ONB[:], T.CK[:], True, False, "ONB CK", pk)
-        mm(k[:, 1:3, 0:34:17], T.IF[:], bf, False, False, "IF " + fk, pk)
+        cp(T.KL[:, a:a + 64], kwin().indirect(bl), "KN " + bk, "KL%d" % h)
+        act(T.N0[:, 68 * h:68 * h + 68:17], bf, AF.Copy, fk, "N0%d" % h)
+        if q:
+            act(T.XB[:, a:a + 64], T.X[:, 0:NW].indirect(bl), AF.Copy, "X XL " + bk, "XB%d" % h)
+        u, z, w = a + CUTS[-1], a + 64, 16 * (64 - CUTS[-1])
+        act(T.DIFF[:, 16 * u:16 * z], T.XW[:].indirect(T.KL[:, u:z]), AF.Copy, "XW XWp KL%d" % h, "DF%ds" % h)
+        mm(dz[:, 128:128 + w], T.NIB[:], T.ZR[:, 16 * u:16 * z], True, False, "NIB ZR%d" % h, "dz")
+        mm(dz[:, 0:64], T.NIB[:], T.ZR[:, 16 * a:16 * a + 1024:16], False, False, "NIB ZR%d" % h, "dz")
+        mm(dz[:, 0:64], T.IB[:], T.XB[:, a:a + 64], False, False, "IB XB%d" % h, "dz")
+        mm(dz[:, 128:128 + w], T.IB[:], T.DIFF[:, 16 * u:16 * z], False, True, "IB DF%ds" % h, "dz")
+        mm(k[:, 1:3, 0:34], T.IF[:], T.N0[:, 68 * h:68 * h + 68], True, False, "IF N0%d" % h, pk)
         pull()
         gather(0)
-        if not (q or h):
-            here()
-        act(T.AB[:, a:a + 64, 0], dz[:, a:a + 64], AF.Abs, "", "AB%ds" % h, "dz")
         ts(T.C16[:, a:a + 64], T.KL[:, a:a + 64], -OFS, A.add, rd="KL%d" % h, wr="C16%d" % h)
         gather(1)
         turn32(T.CT[:, 2 * h:2 * h + 2, :], T.C16[:, a:a + 64], "C16%d" % h, "CT%d" % h)
         for c, (m, mk) in enumerate(((T.IE, "IE"), (T.IO, "IO"))):
             for gp in range(2):
-                w = 16 + 16 * (c - gp)
-                mm(k[:, 1:3, 17 * c + 1:17 * c + 17], m[:, w:w + 128], T.CT[:, 2 * h:2 * h + 2, 16 * gp:16 * gp + 16], False, False,
-                   mk + " CT%d" % h, pk)
-        gather(2)
-        gather(3)
-        if t:
-            mm(k[:, 0, 0:68:17], T.IB[:], T.CA[:], False, False, "IB CA", pk)
-        for j in range(16):
-            mm(k[:, 0, 0:68], T.SW[:, 15 - j:143 - j], T.AB[:, a + j:a + 64:16, :], False, j == 15,
-               "SW AB%d0 AB%d2 AB%d3 AB%ds" % (h, h, h, h), pk)
+                mm(k[:, 1:3, 17 * c + 1:17 * c + 17], m[:, 16 + 16 * (c - gp):144 + 16 * (c - gp)],
+                   T.CT[:, 2 * h:2 * h + 2, 16 * gp:16 * gp + 16], False, False, mk + " CT%d" % h, pk)
+        for c in range(2, len(CUTS) - 1):
+            if c == SAT:
+                act(T.AB[:, u:z, 1:17], dz[:, 128:128 + w], AF.Abs, "", "+AB%d" % h, "dz")
+                act(T.AB[:, a:a + 64, 0], dz[:, 0:64], AF.Abs, "", "+AB%d" % h, "dz")
+            if c == len(CUTS) - 2:
+                mm(k[:, 0, 0:68], T.ONB[:], T.CK[:], False, False, "ONB CK", pk)
+                seat_begin(t, 2 * s + h)
+                keys(0, 8)
+            gather(c)
+        keys(8, 16)
         if s or h:
-            pull()
+            if len(CUTS) < 6:
+                pull()
             next(other)
             pull()
 
@@ -543,8 +546,8 @@ def rank_program(g, core, T, topo):
         cnt, pk, c4 = kk[h][:, 3, 0:12], "k%d" % h, slice(4 * h, 4 * h + 4)
 
         def zsum():
-            mm(dz[:, a:a + 64], T.IB[:], T.XB[:, a:a + 64], True, False, "IB XB%d" % h, "dz")
-            mm(dz[:, a:a + 64], T.IB[:], T.ZR[:, 16 * a:16 * a + 1024:16], False, True, "IB ZR%d" % h, "dz")
+            mm(dz[:, 128 + a:192 + a], T.IB[:], T.XB[:, a:a + 64], True, False, "IB XB%d" % h, "dz")
+            mm(dz[:, 128 + a:192 + a], T.IB[:], T.ZR[:, 16 * a:16 * a + 1024:16], False, True, "IB ZR%d" % h, "dz")
 
         if h == 0:
             act(T.CDE[:, 0:64], T.BT[:].indirect(bl), AF.Copy, "BT EV " + bk, "CDE0", scale=EV)
@@ -592,7 +595,7 @@ def rank_program(g, core, T, topo):
 
     def seat_z(t, h):
         a = 128 * t + 64 * h
-        act(T.ZQ[:, 64 * h:64 * h + 64], dz[:, 64 * h:64 * h + 64], AF.Identity, "", "ZQ%d" % h, "dz", scale=0.4999, bias=M0C)
+        act(T.ZQ[:, 64 * h:64 * h + 64], dz[:, 128 + 64 * h:192 + 64 * h], AF.Identity, "", "ZQ%d" % h, "dz", scale=0.4999, bias=M0C)
         act(T.VF[:, 128 * t + a:128 * t + a + 64], T.ID[:].indirect(T.BL[:, 64 * t + 48 + 4 * h:64 * t + 52 + 4 * h]), AF.Copy,
             "ID BL%d%d" % (4 * t + 3, h), "VF%d" % h)
         act(T.ZN[:, a:a + 64], T.ZQ[:, 64 * h:64 * h + 64], AF.Identity, "ZQ%d" % h, "ZN%d" % h, bias=-M0C)
@@ -615,6 +618,8 @@ def rank_program(g, core, T, topo):
 
     def seat_feet(t):
         v = T.MS3[:, 15::16]
+        if t < VIS - 1:
+            yield
         tt(T.MV[:], eA[:, 0, :], D, A.mult, "D", "MV", "eA")
         yield
         scan(T.MS3[:], RS, T.MV[:], 0.0, A.mult, A.add, "RS MV", "MS3")
@@ -629,8 +634,14 @@ def rank_program(g, core, T, topo):
         scan(T.MS2[:], RS, T.MU2[:], 0.0, A.mult, A.add, "RS MU2", "MS2")
         tt(T.PK1[:, 0::2], L["bov"], T.SN[:], A.mult, "bov SN", "PK1a")
         yield
-        cp(fwin().indirect(T.LN[:, 0:8]), T.VF[:, 256 * t:256 * t + 128], "LNa VF0 VF1", "FX")
+        if t == VIS - 1:
+            cp(fwin().indirect(T.LN[:, 0:8]), T.VF[:, 256 * t:256 * t + 128], "LNa VF0 VF1", "FX")
         for _ in place(T.BN[:, :, 0:4], "BN0 BN1", T.LN[:, 8:16], "LNb"):
+            yield
+        if t < VIS - 1:
+            while "walk%d" % (t + 1) not in read:
+                yield
+            cp(fwin().indirect(T.LN[:, 0:8]), T.VF[:, 256 * t:256 * t + 128], "LNa VF0 VF1", "FX")
             yield
         cp(fwin().indirect(T.LN[:, 8:16]), T.VF[:, 256 * t + 128:256 * t + 256], "LNb VFr", "FX")
         yield
@@ -643,10 +654,10 @@ def rank_program(g, core, T, topo):
         ts(T.SN[:], T.OF[:, :, 0:4], float(NW), A.is_lt, -1.0, A.mult, rd="OF0 OF1", wr="SN")
         cp(T.LN[:, 0:8], T.OF[:, :, 4:8], "OF0 OF1", "LNa")
         if not fin:
-            mm(dz[:, 384:392], T.ONB[:], T.LIVE[:, 0:8], True, False, "ONB LIVE", "dz")
-            mm(dz[:, 384:392], T.ONB[:], T.SN[:], False, True, "ONB SN", "dz")
+            mm(dz[:, 80:88], T.ONB[:], T.LIVE[:, 0:8], True, False, "ONB LIVE", "dz")
+            mm(dz[:, 80:88], T.ONB[:], T.SN[:], False, True, "ONB SN", "dz")
             act(T.MS[:, m0:m0 + 8], T.OF[:, :, 8:12], AF.Copy, "OF0 OF1", "MS")
-            act(L["aq"], dz[:, 384:392], AF.Copy, "", "AQ AS", "dz", accum_out=AS)
+            act(L["aq"], dz[:, 80:88], AF.Copy, "", "AQ AS", "dz", accum_out=AS)
             act(T.MS[:, m0 + 8:m0 + 12], T.ONB[:, 0:4], AF.Copy, "ONB AS", "MSa", scale=AS)
             send(nxt, T.ML[:, m0:m0 + 16], T.MS[:, m0:m0 + 16], "aM%d" % t, "MS MSa")
             arrives("aM%d" % t, "M%d" % t)
@@ -676,26 +687,31 @@ def rank_program(g, core, T, topo):
         cp(T.KN[:, a:z], T.KI[:, a:z], "KI%d" % i, "+KN")
 
     def converts():
-        for i in range(2, len(KCH)):
-            convert(i)
+        for i in range(1, len(KCH)):
             yield
+            yield
+            convert(i)
 
     convert(0)
-    convert(1)
-    lines[:] = [[out_before(0)], [converts()], [late(), later()], [start(0)]]
+    lines[:] = [[out_before(0)], [converts()], [late()], [start(0)]]
     while lines[0] or lines[1]:
         pull()
     zrep(0, 0)
     zrep(0, 1)
-    lines[0] = [out(0)]
-    drain()
+    alive = live(0)
+    lines[0:2] = [[out(0)], []]
+    lines.append([alive])
+    while any(lines[0:4]):
+        pull()
+    act(T.XB[:], T.XW[:].indirect(T.BL[:, 0:8]), AF.Copy, "XW BL00 BL01", "XB0 XB1 XWp")
     far(0)
     for t in range(VIS):
         fin = t == VIS - 1
         if fin:
             dma("Y", "early", T.yk[:], T.KN[:, NB:NW], rd="KN", wr="yk")
             dma("Y", "early", T.yx[:], T.X[:, NB:NW], rd="X", wr="yx")
-        lines[:] = [([seat_feet(t - 1)] if t else []) + [out_feet(t)] + ([] if fin else [out_before(t + 1)]), [live(t)]]
+        read.append("walk%d" % t)
+        lines[:] = [[feet3 if t else later()] + [out_feet(t)] + ([] if fin else [out_before(t + 1)]), [alive]]
         other = iter(())
         for i in range(2 * ST):
             sums(t, i // 2, i % 2, other)
@@ -704,22 +720,17 @@ def rank_program(g, core, T, topo):
                 rows(t)
                 for h in range(2):
                     act(T.BN[:, h, 4:8], T.J8[:, 4 * h:4 * h + 4], AF.Identity, "J8", "+BN%d" % h, bias=float(lo[t]))
-            if i in (2, 3, 4):
-                while lines[1]:
-                    pull(1)
-                while i == 4 and "none%d" % t not in read:
-                    pull()
-                seat_begin(i - 2)
         seat_sums(t, 0)
+        read.append("end%d" % t)
         if t in (1, 2):
             cp(T.L8[:], T.ML[:, 16 * (t - 1):16 * (t - 1) + 8], "M%d" % (t - 1), "L8")
-        while lines[0] and (fin or -t - 1 not in read):
-            pull()
+        pull()
         act(T.EQ[0:64, 0:4, :], eA[0:64], AF.Relu, "", "EQA", "eA", bias=-12.0 + EPS)
-        for i, _ in enumerate(other):
+        seat_count(0)
+        for _ in other:
             pull()
-            if i == 1:
-                seat_count(0)
+        while fin and lines[0]:
+            pull()
         send(prv if fin else nxt, T.CL[:, 8 * t:8 * t + 8], T.BL[:, 64 * t + 48:64 * t + 56], "aB" if fin else "aC%d" % t,
              "BL%d0 BL%d1" % (4 * t + 3, 4 * t + 3))
         arrives("aB" if fin else "aC%d" % t, "C%d" % (t + 1))
@@ -750,8 +761,10 @@ def rank_program(g, core, T, topo):
             lines[1:] = [[second], [seat_rest(t)]]
         else:
             far(t + 1)
-            lines[1:] = [[second, out(t + 1)], [seat_rest(t)]]
-        drain()
+            feet3, alive = seat_feet(t), live(t + 1)
+            lines[1:] = [[second, out(t + 1)], [seat_rest(t)], [alive]]
+        while any(lines[0:3]):
+            pull()
         if not fin:
             zrep(t + 1, 1)
         if t == 2:

@@ -11,17 +11,18 @@ M0C = 1.5 * 2.0 ** 23
 EPS = 2.0 ** -20
 CUTS = (0, 24, 32, 40, 48)
 ABS = {0: 0, 2: 1, 3: 3}
+LAST = [j % 16 for j in range(CUTS[-2], CUTS[-1])]
 LISTS = "d0 d1 e0 c0 cn ch ny bov bou held dum ndum sq3 aq".split()
 BUFS = {
     "float32": "KN:3856 FX:3856 TT:3856 OT:3856 ID:3584 TRF:224 ML:48 MS:48 COLF:16 CF:160 C15F:128 CGF:128 D:128 B0:128 IF:128 RG8:128 "
                "R0:68 RS:128 I8:8 J8:8 NN:32 NR:1024 VF:1024 FVO:128 TM:128 TS:128 MU:128 MS1:128 GZ:128 UM:128 "
                "MU2:128 MS2:128 MS3:128 MV:128 SM:112 OR:128 VM:136 GG:136 BB:136 SC:136 N0:136 ZQ:128 "
-               "BF8:128 BIT:8 RPI:128 CMP:16 E2:32 A1:32 OO:32 SQ:16 NO:16 PK0:16 PK1:16 PKO:16",
-    "bfloat16": "X:3856 XW:3584 BT:4096 ZL:512 ZN:512 ZR:2048 IB:128 NIB:128 ONB:128 BON:128 SW:144 CK:68 CW:4 BCB:1024 DIFF:2048 "
-                "XB:128 CDE:128 CDO:128 LIVE:16 LX:128 SN:8 NL:8 PO:8 NUA:512 NUB:128 RG:512 RP:128",
+               "SND:408 LND:408 BF8:128 BLK:128 FB:128 LB:8 BIT:8 RPI:128 CMP:16 E2:32 A1:32 OO:32 SQ:16 NO:16 PK0:16 PK1:16 PKO:16",
+    "bfloat16": "X:3856 XW:3584 BT:4096 Z0:128 ZN:128 ZR:2048 IB:128 NIB:128 ONB:128 BON:128 SW:144 CK:68 CW:4 BCB:1024 DIFF:2048 "
+                "XB:128 CDE:128 CDO:128 LIVE:16 LX:128 SN:8 NL:8 PO:8 NU:256 RP:128",
     "float16": "C16:128 C2:256 IE:160 IO:160 RH8:128 F16:1024",
-    "int32": "KI:3584 FI:1024 BI:128 TRI:224 COLI:4 BC:8 AI:8 C8I:8",
-    "uint16": "CL:32 BL:256 KL:128 YL:16 LO:16 VL:8 LS:16 LN:16 L8:8 C8:8",
+    "int32": "KI:3592 FI:1024 BI:128 TRI:224 COLI:4 BC:8 AI:8 C8I:8",
+    "uint16": "CL:16 BL:256 KL:128 YL:16 LO:16 VL:8 LS:16 LN:16 L8:8 C8:8",
 }
 SCRATCH = {"TD": ("dram", [128, 224], "float32"), "TB": ("dram", [128, 224], "float32"), "TBL": ("dram", [128, 224], "float32"),
            "BTD": ("dram", [16, 64, 64], "bfloat16"),
@@ -39,7 +40,7 @@ for _i in range(2):
     SCRATCH["k%d" % _i] = ("psum", [128, 4, 128], "float32")
 KCH = [(NB, NW), (0, 1024), (1024, 2048), (2048, NB)]
 SEMAPHORES = (["V", "S", "P", "G", "lx", "lw", "lf", "lb", "lz", "lt", "btd", "bt", "tt", "tb", "ot", "out", "early", "aT", "aB", "aTB", "loc"]
-              + ["kn%d" % i for i in range(len(KCH))] + ["a%s%d" % (k, t) for k in ("C", "Z0", "Z1", "M") for t in range(3)])
+              + ["kn%d" % i for i in range(len(KCH))] + ["a%s%d" % (k, t) for k in ("Z0", "Z1", "M") for t in range(3)])
 
 
 def rank_program(g, core, T, topo):
@@ -166,7 +167,7 @@ def rank_program(g, core, T, topo):
 
     dma("Y", "lf", T.FI[0:8, :], T.ft[:], wr="FI")
     dma("Y", "lb", T.BI[0:8, :], T.bs[:], wr="BI")
-    dma("S", "lz", T.ZL[:, 0:128], T.z0[:], wr="Z00 Z01")
+    dma("S", "lz", T.Z0[:], T.z0[:], wr="Z00 Z01")
     dma("S", "lt", T.TRI[:], T.tr[:], wr="TRI")
     for i, (a, z) in enumerate(KCH):
         dma("Y", "kn%d" % i, T.KI[:, a:z], T.kn[:, a:z], wr="KI%d" % i)
@@ -190,6 +191,7 @@ def rank_program(g, core, T, topo):
     fill(T.RS[:, 0::16], 0.0, "RS")
     fill(T.R0[:, 0::17], 1.0e9, "R0")
     fill(L["c0"], 0.0, "c0")
+    fill(T.KI[:, NW:], -1, "KIt")
     iota(T.CK[0:1, 0:68], [[0, 4], [SL, 17]], 0, 0, "CK")
     iota(T.KN[:, NW:WN], [[0, WN - NW]], -1, 0, "KNt")
     ts(P15I, PI, 15, A.bitwise_and, rd="PI", wr="P15I")
@@ -214,7 +216,7 @@ def rank_program(g, core, T, topo):
     mm(eq[2][:, 4:8, :], T.RG8[0:8, :], T.BF8[0:8, :], True, True, "RG8 BF8", "e2")
 
     def feet(h):
-        ps, pk = (eA[:], "eA") if h else (eq[3][:], "e3")
+        ps, pk = eq[1 + 2 * h][:], "e%d" % (1 + 2 * h)
         ts(T.F16[0:8, 512 * h:512 * h + 512], T.FI[0:8, 512 * h:512 * h + 512], -OFS, A.add, rd="FI", wr="F16%d" % h)
         mm(ps, T.RH8[0:8, :], T.F16[0:8, 512 * h:512 * h + 512], True, True, "RH8 F16%d" % h, pk)
         act(T.FX[:, NB + 512 * h:NB + 512 * h + 512], ps, AF.Identity, "", "+FX", pk, bias=OFS)
@@ -224,6 +226,7 @@ def rank_program(g, core, T, topo):
     ts(T.IO[:], T.CF[:], P16, A.is_equal, OD, A.mult, rd="CF P16 OD", wr="IO")
     ts(T.IF[:], T.CF[:, 0:128], PF, A.is_equal, rd="CF PF", wr="IF")
     ts(T.SW[:], T.CF[:, 0:144], PW, A.is_equal, WT, A.mult, rd="CF PW", wr="SW")
+    feet(1 - rank // 4)
     act(L["ndum"], T.J8[:], AF.Identity, "J8", "ndum", scale=-1.0, bias=OFS - DA)
     for out, d, key in ((L["dum"], DA, "dum"), (T.A1[:, 3::4], DA, "A1d"), (T.PK1[:, 1::2], DA, "PK1b"),
                         (T.DUM[:, :, 0:4], DA, "DUM"), (T.DUM[:, :, 4:8], DB, "+DUM"), (T.DUM[:, :, 8:12], DA, "+DUM")):
@@ -243,16 +246,10 @@ def rank_program(g, core, T, topo):
     iota(T.FX[:, 0:NB], [[0, NB]], -1, 0, "FXa")
 
     def constants_g():
-        iota(T.NUA[:], [[0, 512]], -32, 0, "NUA")
+        iota(T.NU[:], [[0, 256]], -32, 0, "NU")
         iota(T.FX[:, NW:WN], [[0, WN - NW]], -1, 0, "FXb")
-        keep(T.NUA[:], [[-16, 4], [0, 8], [-1, 16]], 0, 1, "NUA")
-        iota(T.RG[:], [[0, 512]], 1, 0, "RG")
-        iota(T.NUB[:], [[0, 128]], -32, 0, "NUB")
-        keep(T.RG[:], [[0, 4], [-16, 8], [0, 16]], 0, 1, "RG")
-        keep(T.NUB[:], [[-16, 4], [0, 2], [-1, 16]], -64, 1, "NUB")
-        keep(T.RG[:], [[0, 4], [16, 8], [0, 16]], 15, -1, "RG")
+        keep(T.NU[:], [[-16, 8], [0, 2], [-1, 16]], 0, 1, "NU")
         iota(T.ID[:], [[1, NW]], 0, 0, "ID")
-        iota(T.EQ[:, 0:4, :], [[0, 512]], 0, 0, "EQz EQA")
         iota(T.X[:, NW:WN], [[0, WN - NW]], 0, 0, "Xt")
         iota(T.TT[:, NW:WN], [[0, WN - NW]], 0, 0, "TT")
 
@@ -286,8 +283,10 @@ def rank_program(g, core, T, topo):
         yield
         yield
         ts(T.BON[:], T.CGF[:], PG, A.is_equal, float(NW), A.mult, rd="CGF PG", wr="BON")
-        act(T.B0[:], T.BON[:], AF.Copy, "BON M0", "B0", scale=M0)
-        act(T.B0[:], T.B0[:], AF.Sign, "B0", "B0")
+        act(T.BLK[:], T.BON[:], AF.Sign, "BON", "BLK")
+        act(T.CDE[:, 64:128], T.ONB[:, 0:64], AF.Copy, "ONB", "CDE1")
+        act(T.CDO[:, 64:128], T.ONB[:, 0:64], AF.Copy, "ONB", "CDO1")
+        act(T.B0[:], T.BLK[:], AF.Copy, "BLK M0", "B0", scale=M0)
         yield
         fill(T.LIVE[:], 0.0, "LIVE")
         cp(T.C8[:], T.C8I[:], "C8I", "C8")
@@ -298,10 +297,6 @@ def rank_program(g, core, T, topo):
         fill(T.CW[:, 0:2], BIG, "CW")
         fill(T.CW[:, 2:4], BIG / EPS, "+CW")
         fill(T.MS[:], 0.0, "MS")
-        yield
-
-    def later():
-        feet(1 - rank // 4)
         yield
 
     def rows(t):
@@ -319,7 +314,7 @@ def rank_program(g, core, T, topo):
 
     def out_before(t):
         a, z = lo[t], lo[t] + 128
-        y0, pl = T.MS1[:, 15::16], dz[:, 64:80]
+        y0, pl = T.MS1[:, 15::16], eA[:, 1, 0:16]
         tt(T.MU[:], T.FX[:, a:z], D, A.mult, "FX D", "MU")
         act(T.CMP[:, 0:8], T.J8[:], AF.Identity, "J8", "CMPa", bias=a - OFS)
         yield
@@ -335,17 +330,17 @@ def rank_program(g, core, T, topo):
             ts(T.C2[:, 0:128], kwin().indirect(T.YL[:, 0:8]), -OFS, A.add, rd="KN YLa", wr="C2a")
             read.append(t)
         yield
-        while t and "end%d" % (t - 1) not in read:
-            yield
         b0 = 0 if t else 4
         turn32(T.CT2[:, b0:8, :], T.C2[:, 32 * b0:256], "C2a C2b", "CT2")
-        to_list(pl, b0, 8, "dz")
+        to_list(pl, b0, 8, "eA")
         yield
         ts(T.NO[:], T.SQ[:], 4096.0, A.is_ge, rd="SQ", wr="NO")
         yield
+        if t == 1:
+            yield
         if t:
-            tt(L["e0"], pl[:, 0:8], T.CMP[:, 0:8], A.is_equal, "CMPa", "e0l", "dz")
-        ts(T.CMP[:, 8:16], pl[:, 8:16], a - OFS - 0.5, A.max, z - OFS - 0.5, A.min, wr="CMPb", ps="dz")
+            tt(L["e0"], pl[:, 0:8], T.CMP[:, 0:8], A.is_equal, "CMPa", "e0l", "eA")
+        ts(T.CMP[:, 8:16], pl[:, 8:16], a - OFS - 0.5, A.max, z - OFS - 0.5, A.min, wr="CMPb", ps="eA")
         tt(L["d1"] if t else T.A1[:, 0::4], L["d0"], T.NO[:, 0:8], A.mult, "d0 NO", "d1 A1a")
         yield
         if t:
@@ -359,17 +354,23 @@ def rank_program(g, core, T, topo):
 
     def out(t):
         a, z = lo[t], lo[t] + 128
-        pl = eq[0][:, 4, 0:16]
+        pl = eq[0][:, 8, 0:16]
         while t and lines[0]:
             yield
-        ts(T.C2[:, 0:128], kwin().indirect(T.YL[:, 0:8]), -OFS, A.add, rd="KN KNt YLa", wr="C2a")
-        ts(T.C2[:, 128:256], T.KN[:, a:z], -OFS, A.add, rd="KN", wr="C2b")
-        act(T.GZ[:], kwin().indirect(T.YL[:, 0:8]), AF.Copy, "KN KNt YLa NM0", "GZ", scale=NM0)
-        act(T.UM[:], T.KN[:, a:z], AF.Copy, "KN M0", "UM", scale=M0)
+        if t:
+            ts(T.C2[:, 0:128], kwin().indirect(T.YL[:, 0:8]), -OFS, A.add, rd="KN YLa", wr="C2a")
+            ts(T.C2[:, 128:256], T.KN[:, a:z], -OFS, A.add, rd="KN", wr="C2b")
+        else:
+            ts(T.C2[:, 0:128], T.KI[:].indirect(T.YL[:, 0:8]), -OFS, A.add, rd="KI0 KI1 KI2 KI3 KIt YLa", wr="C2a")
         yield
         turn32(T.CT2[:], T.C2[:], "C2a C2b", "CT2")
         to_list(pl, 0, 8, "e0")
-        yield
+        if t == 0:
+            convert(len(KCH) - 1)
+        act(T.GZ[:], kwin().indirect(T.YL[:, 0:8]), AF.Copy, "KN KNt YLa NM0", "GZ", scale=NM0)
+        act(T.UM[:], T.KN[:, a:z], AF.Copy, "KN M0", "UM", scale=M0)
+        if t:
+            yield
         yield
         tt(T.E2[:, 1::4], pl[:, 0:8], T.CMP[:, 0:8], A.is_equal, "CMPa", "E2a", "e0")
         tt(T.A1[:, 1::4], pl[:, 0:8], L["c0"], A.mult, "c0", "A1b", "e0")
@@ -384,31 +385,39 @@ def rank_program(g, core, T, topo):
         yield
 
     def live(t):
-        pl = eq[0][:, 4, 0:16]
+        pl = eq[0][:, 8, 0:16]
         while "met%d" % t not in read:
             yield
-        ts(T.YL[:, 8:16], pl[:, 8:16], OFS, A.add, wr="YLb", ps="e0")
-        tt(L["bou"], pl[:, 8:16], L["ndum"], A.add, "ndum", "bou", "e0")
         yield
         tt(L["ch"], L["c0"], T.E2[:, 1::4], A.is_gt, "c0 E2a", "ch")
         yield
         tt(L["ny"], L["ch"], T.NO[:, 0:8], A.max, "ch NO", "ny")
-        ts(L["held"], T.OO[:, 3::4], float(NW), A.is_lt, rd="OO", wr="held")
+        ts(T.YL[:, 8:16], pl[:, 8:16], OFS, A.add, wr="YLb", ps="e0")
         yield
         tt(T.LIVE[:, 0:8], L["ny"], T.E2[:, 3::4], A.mult, "ny E2b", "LIVE")
+        ts(L["held"], T.OO[:, 3::4], float(NW), A.is_lt, rd="OO", wr="held")
+        tt(L["bou"], pl[:, 8:16], L["ndum"], A.add, "ndum", "bou", "e0")
         yield
         while "walk%d" % t not in read:
             yield
         act(T.NL[:], T.LIVE[:, 0:8], AF.Identity, "LIVE", "NL", scale=-BIG, bias=BIG)
         if t:
-            cp(T.AI[:, 0:4], T.ML[:, 16 * t - 8:16 * t - 4], "M%d" % (t - 1), "AI0")
+            second = start(t, 1)
+            next(second)
             yield
+            next(second)
+            cp(T.AI[:, 0:4], T.ML[:, 16 * t - 8:16 * t - 4], "ML%d" % (t - 1), "AI0")
+            yield
+            next(second)
             ts(T.AI[:, 4:8], T.AI[:, 0:4], 31, A.bitwise_and, rd="AI0", wr="AI1")
             yield
+            next(second)
             ts(T.CK[0:1, 0::17], T.AI[0:1, 4:8], WT, A.mult, rd="AI1", wr="CK")
         yield
+        yield
         tt(T.LX[:], T.LIVE[:].indirect(T.C8[:]), D, A.mult, "LIVE C8 D", "LX")
-        mm(eq[3][:, 4:8, :], T.BON[:], T.LX[:], True, True, "BON LX", "e3")
+        yield
+        mm(eA[:, 2, :], T.BON[:], T.LX[:], True, True, "BON LX", "eA")
         yield
 
     def place(met, rd, out, key):
@@ -429,42 +438,41 @@ def rank_program(g, core, T, topo):
         scan(T.MS2[:], RS, T.MU2[:], 0.0, A.mult, A.add, "RS MU2", "MS2")
         tt(T.PK1[:, 0::2], L["held"], L["bou"], A.mult, "held bou", "PK1a")
         yield
-        tt(T.FX[:, a:z], eq[3][:, 4:8, :], T.FX[:, a:z], A.max, "FX", "FX", "e3")
-        read.append("none%d" % t)
+        tt(T.FX[:, a:z], eA[:, 2, :], T.FX[:, a:z], A.max, "FX", "FX", "eA")
         for _ in place(T.NN[:, 8 * t:8 * t + 8], "NN", T.LO[:, 8:16], "LOb"):
             yield
         cp(fwin().indirect(T.LO[:, 8:16]), T.FVO[:], "LOb FVO", "FX")
         yield
 
     def seat_begin(t, i):
-        while i == 3 and lines[1]:
+        while i == 2 and lines[1]:
             pull(1)
-        while i == 5 and "none%d" % t not in read:
-            pull()
-        if i == 2:
-            mm(eA[0:64], T.IB[:, 0:64], T.NUA[:], True, False, "IB NUA", "eA")
-        elif i == 3:
-            mm(eA[0:64], T.LX[:, 0:64], T.RG[:], False, False, "LX RG", "eA")
-        elif i > 3:
-            for q in (2 * i - 8, 2 * i - 7):
-                mm(eq[q][:, 0:4, :], T.IB[:], T.NUB[:], True, False, "IB NUB", "e%d" % q)
-                mm(eq[q][:, 0:4, :], T.LX[32 * q:32 * q + 32, :], T.RP[32 * q:32 * q + 32, :], False, False, "LX RP", "e%d" % q)
+        if i >= 2:
+            order(0, i - 2)
 
-    def start(t):
+    def order(h, q):
+        out = eq[q][:, 4 * h:4 * h + 4, :]
+        mm(out, T.IB[:], T.NU[:, 128 * h:128 * h + 128], True, False, "IB NU", "e%d" % q)
+        mm(out, T.LX[32 * q:32 * q + 32, :], T.RP[32 * q:32 * q + 32, :], False, False, "LX RP", "e%d" % q)
+
+    def start(t, h):
+        a, c = 64 * h, T.CL[:, 4 * h:4 * h + 4]
         if t == 0:
-            tt(T.TM[:], eq[2][:, 4:8, :], D, A.mult, "D", "TM", "e2")
+            tt(T.TM[:, a:a + 64], eq[2][:, 4 + 2 * h:6 + 2 * h, :], T.D[:, 0:64], A.mult, "D", "TM%d" % h, "e2")
         else:
-            tt(T.TM[:], T.TT[:].indirect(T.CL[:, 8 * t - 8:8 * t]), D, A.mult, "TT TTd D C%d" % t, "TM")
+            cp(c, T.LND[:, 136 * t - 136 + 132 * h:136 * t - 132 + 132 * h], "Z%d%d" % (t, h), "CL%d" % h)
+            yield
+            tt(T.TM[:, a:a + 64], T.TT[:].indirect(c), T.D[:, 0:64], A.mult, "TT TTd D CL%d" % h, "TM%d" % h)
         yield
-        scan(T.TS[:], RS, T.TM[:], 0.0, A.mult, A.add, "RS TM", "TS")
+        scan(T.TS[:, a:a + 64], T.RS[:, 0:64], T.TM[:, a:a + 64], 0.0, A.mult, A.add, "RS TM%d" % h, "TS%d" % h)
         yield
-        cp(T.BL[:, 64 * t:64 * t + 8], T.TS[:, 15::16], "TS", "BL%d0 BL%d1" % (4 * t, 4 * t))
+        cp(T.BL[:, 64 * t + 4 * h:64 * t + 4 * h + 4], T.TS[:, a + 15:a + 64:16], "TS%d" % h, "BL%d%d" % (4 * t, h))
         yield
 
     def zrep(t, h):
-        a = 128 * t + 64 * h
+        zz = T.LND[:, 136 * t - 132 + 64 * h:136 * t - 68 + 64 * h] if t else T.Z0[:, 64 * h:64 * h + 64]
         for k in range(16):
-            act(T.ZR[:, 1024 * h + k:1024 * h + 1024:16], T.ZL[:, a:a + 64], AF.Copy, "Z%d%d" % (t, h), "+ZR%d" % h)
+            act(T.ZR[:, 1024 * h + k:1024 * h + 1024:16], zz, AF.Copy, "Z%d%d" % (t, h), "+ZR%d" % h)
 
     def far(t):
         act(T.XW[:, lo[t]:lo[t] + 128], T.ONB[:], AF.Copy, "ONB", "XWp", scale=4096.0)
@@ -472,7 +480,7 @@ def rank_program(g, core, T, topo):
     def sums(t, s, h, other):
         q, a, k, pk = 4 * t + s, 64 * h, kk[h], "k%d" % h
         bl, bk = T.BL[:, 16 * q + 4 * h:16 * q + 4 * h + 4], "BL%d%d" % (q, h)
-        bf, fk = (T.TS[:, a + 15:a + 64:16], "TS") if s == 0 else (T.SC[:, 68 * h + 16:68 * h + 68:17], "SC%d" % h)
+        bf, fk = (T.TS[:, a + 15:a + 64:16], "TS%d" % h) if s == 0 else (T.SC[:, 68 * h + 16:68 * h + 68:17], "SC%d" % h)
 
         def gather(c):
             u, z = a + CUTS[c], a + CUTS[c + 1]
@@ -486,9 +494,9 @@ def rank_program(g, core, T, topo):
             if c < 4 and next(other, "end") == "end":
                 pull(1)
 
-        def keys(j0, j1):
-            for j in range(j0, j1):
-                mm(k[:, 0, 0:68], T.SW[:, 15 - j:143 - j], T.AB[:, a + j:a + 64:16, :], False, j == 15, "SW AB%d" % h, pk)
+        def keys(js, end):
+            for j in js:
+                mm(k[:, 0, 0:68], T.SW[:, 15 - j:143 - j], T.AB[:, a + j:a + 64:16, :], False, end and j == js[-1], "SW AB%d" % h, pk)
 
         cp(T.KL[:, a:a + 64], kwin().indirect(bl), "KN " + bk, "KL%d" % h)
         act(T.N0[:, 68 * h:68 * h + 68:17], bf, AF.Copy, fk, "N0%d" % h)
@@ -517,9 +525,9 @@ def rank_program(g, core, T, topo):
             if c == len(CUTS) - 2:
                 mm(k[:, 0, 0:68], T.ONB[:], T.CK[:], False, False, "ONB CK", pk)
                 seat_begin(t, 2 * s + h)
-                keys(0, 8)
+                keys([j for j in range(16) if j not in LAST], False)
             gather(c)
-        keys(8, 16)
+        keys(LAST, True)
         if s or h:
             if len(CUTS) < 6:
                 pull()
@@ -544,16 +552,13 @@ def rank_program(g, core, T, topo):
         bl, bk = T.BL[:, 16 * q + 4 * h:16 * q + 4 * h + 4], "BL%d%d" % (q, h)
         bf, fk = T.SC[:, 68 * h + 16:68 * h + 68:17], "SC%d" % h
         cnt, pk, c4 = kk[h][:, 3, 0:12], "k%d" % h, slice(4 * h, 4 * h + 4)
-
-        def zsum():
-            mm(dz[:, 128 + a:192 + a], T.IB[:], T.XB[:, a:a + 64], True, False, "IB XB%d" % h, "dz")
-            mm(dz[:, 128 + a:192 + a], T.IB[:], T.ZR[:, 16 * a:16 * a + 1024:16], False, True, "IB ZR%d" % h, "dz")
-
         if h == 0:
             act(T.CDE[:, 0:64], T.BT[:].indirect(bl), AF.Copy, "BT EV " + bk, "CDE0", scale=EV)
         else:
             ts(T.CDE[:, 64:128], T.BT[:].indirect(bl), EV, A.mult, rd="BT EV " + bk, wr="CDE1")
         act(T.CDO[:, a:a + 64], T.BT[:].indirect(bl), AF.Copy, "BT OD " + bk, "CDO%d" % h, scale=OD)
+        if t == VIS - 1 and h:
+            seat_kin_of(t, 1)
         act(L["sq3"][:, c4], bf, AF.Square, fk, "sq3%d" % h, bias=-lo[t] - 63.5)
         for i in (0, 8):
             act(T.BN[:, h, i:i + 4], bf, AF.Copy, fk, "+BN%d" % h)
@@ -562,33 +567,39 @@ def rank_program(g, core, T, topo):
         for gr in range(8):
             r = 32 * (gr // 2)
             cd, ck = (T.CDE, "CDE") if gr % 2 == 0 else (T.CDO, "CDO")
-            if h == 0:
-                if gr == 4:
-                    zsum()
-                if gr in (2, 4, 6):
-                    need("P", "P", tot["P"])
-                mm(eA[0:64, :, 16 * gr:16 * gr + 16], cd[r:r + 32, 0:64], cd[r:r + 32, 0:64], False, gr == 7, ck + "0", "eA")
-            else:
-                o = 16 * (gr % 2)
-                mm(eq[gr // 2][:, 0:4, o:o + 16], cd[r:r + 32, :], cd[r:r + 32, 64:128], False, gr % 2 == 1, "%s0 %s1" % (ck, ck), "e%d" % (gr // 2))
+            o = 16 * (gr % 2)
+            mm(eq[gr // 2][:, c4, o:o + 16], cd[r:r + 32, :], cd[r:r + 32, a:a + 64], False, gr % 2 == 1,
+               "%s0 %s1" % (ck, ck), "e%d" % (gr // 2))
+        if t == VIS - 1 and h:
+            parents(t)
         mm(cnt, T.IF[:], T.BN[:, h, 0:12], True, False, "IF BN%d" % h, pk)
         for i in (0, 4):
             mm(cnt[:, i:i + 4], T.IB[:], T.NL[:, c4], False, False, "IB NL", pk)
             mm(cnt[:, i:i + 4], T.IB[:], T.PO[:, c4], False, False, "IB PO%d" % h, pk)
+        for i in ((2, 3) if h else range(4)):
+            act(T.EQ[:, c4, 32 * i:32 * i + 32], eq[i][:, c4, :], AF.Relu, "", "EQ%d%d" % (h, i), "e%d" % i, bias=-12.0 + EPS)
         if h == 0:
-            seat_kin_of(t, 0)
+            zsum(0)
+            for i in range(4):
+                order(1, i)
+            seat_count(0)
             seat_z(t, 0)
-        else:
-            zsum()
-            if t == VIS - 1:
-                seat_kin_of(t, 1)
-            for i in (2, 3):
-                act(T.EQ[:, 4:8, 32 * i:32 * i + 32], eq[i][:, 0:4, :], AF.Relu, "", "EQ%d" % i, "e%d" % i, bias=-12.0 + EPS)
+            seat_kin_of(t, 0)
 
     def seat_kin_of(t, h):
         bl, bk = T.BL[:, 64 * t + 48 + 4 * h:64 * t + 52 + 4 * h], "BL%d%d" % (4 * t + 3, h)
         act(T.VK[:, h, 64:128], kwin().indirect(bl), AF.Copy, "KN " + bk, "VKb%d" % h)
         act(T.VK[:, h, 0:64], kwin().indirect(bl), AF.Copy, "KN NM0 " + bk, "VKa%d" % h, scale=NM0)
+
+    def translate(t, h):
+        if t in (1, 2):
+            a = 256 * t + 64 * h
+            cp(T.TT[:].indirect(T.L8[:, 4 * h:4 * h + 4]), T.VF[:, a:a + 64], "L8 VF%d" % h, "TT TTd")
+
+    def zsum(h):
+        a = 64 * h
+        mm(dz[:, 128 + a:192 + a], T.IB[:], T.XB[:, a:a + 64], True, False, "IB XB%d" % h, "dz")
+        mm(dz[:, 128 + a:192 + a], T.IB[:], T.ZR[:, 16 * a:16 * a + 1024:16], False, True, "IB ZR%d" % h, "dz")
 
     def parents(t):
         mm(eA[:, 0, :], T.B0[:], T.VK[:, :, 64:128], True, True, "B0 VKb0 VKb1", "eA")
@@ -598,14 +609,18 @@ def rank_program(g, core, T, topo):
         act(T.ZQ[:, 64 * h:64 * h + 64], dz[:, 128 + 64 * h:192 + 64 * h], AF.Identity, "", "ZQ%d" % h, "dz", scale=0.4999, bias=M0C)
         act(T.VF[:, 128 * t + a:128 * t + a + 64], T.ID[:].indirect(T.BL[:, 64 * t + 48 + 4 * h:64 * t + 52 + 4 * h]), AF.Copy,
             "ID BL%d%d" % (4 * t + 3, h), "VF%d" % h)
-        act(T.ZN[:, a:a + 64], T.ZQ[:, 64 * h:64 * h + 64], AF.Identity, "ZQ%d" % h, "ZN%d" % h, bias=-M0C)
-        if t < VIS - 1:
-            send(nxt, T.ZL[:, 128 + a:192 + a], T.ZN[:, a:a + 64], "aZ%d%d" % (h, t), "ZN%d" % h)
+        if t == VIS - 1:
+            act(T.ZN[:, 64 * h:64 * h + 64], T.ZQ[:, 64 * h:64 * h + 64], AF.Identity, "ZQ%d" % h, "ZN%d" % h, bias=-M0C)
+        else:
+            m = 136 * t
+            act(T.SND[:, m + 132 * h:m + 132 * h + 4], T.SC[:, 68 * h + 16:68 * h + 68:17], AF.Copy, "SC%d" % h, "SB%d" % h)
+            act(T.SND[:, m + 4 + 64 * h:m + 68 + 64 * h], T.ZQ[:, 64 * h:64 * h + 64], AF.Identity, "ZQ%d" % h, "ZN%d" % h, bias=-M0C)
+            send(nxt, T.LND[:, m + 68 * h:m + 68 * h + 68], T.SND[:, m + 68 * h:m + 68 * h + 68], "aZ%d%d" % (h, t), "ZN%d SB%d" % (h, h))
             arrives("aZ%d%d" % (h, t), "Z%d%d" % (t + 1, h))
 
     def seat_count(h):
         for c in range(4):
-            mm(kk[h][:, 3, c:12:4], T.EQ[:, 4 * h + c, :], T.CW[:, 0:3], False, c == 3, "CW EQ0 EQ1 EQ2 EQ3" if h else "CW EQA EQz", "k%d" % h)
+            mm(kk[h][:, 3, c:12:4], T.EQ[:, 4 * h + c, :], T.CW[:, 0:3], False, c == 3, "CW EQ%d0 EQ%d1 EQ%d2 EQ%d3" % (h, h, h, h), "k%d" % h)
 
     def seat_kin(t, h):
         tt(T.OF[:, h, 0:12], kk[h][:, 3, 0:12], T.DUM[:, h, 0:12], A.min, "DUM", "OF%d" % h, "k%d" % h)
@@ -617,8 +632,14 @@ def rank_program(g, core, T, topo):
         yield
 
     def seat_feet(t):
-        v = T.MS3[:, 15::16]
+        v, a = T.MS3[:, 15::16], lo[t]
+
+        def spread():
+            tt(T.FB[:], T.LB[:].indirect(T.C8[:]), D, A.mult, "LB C8 D", "FB")
+            mm(eA[:, 3, :], T.BLK[:], T.FB[:], True, True, "BLK FB", "eA")
+
         if t < VIS - 1:
+            spread()
             yield
         tt(T.MV[:], eA[:, 0, :], D, A.mult, "D", "MV", "eA")
         yield
@@ -633,15 +654,12 @@ def rank_program(g, core, T, topo):
             yield
         scan(T.MS2[:], RS, T.MU2[:], 0.0, A.mult, A.add, "RS MU2", "MS2")
         tt(T.PK1[:, 0::2], L["bov"], T.SN[:], A.mult, "bov SN", "PK1a")
-        yield
         if t == VIS - 1:
-            cp(fwin().indirect(T.LN[:, 0:8]), T.VF[:, 256 * t:256 * t + 128], "LNa VF0 VF1", "FX")
-        for _ in place(T.BN[:, :, 0:4], "BN0 BN1", T.LN[:, 8:16], "LNb"):
-            yield
-        if t < VIS - 1:
-            while "walk%d" % (t + 1) not in read:
-                yield
-            cp(fwin().indirect(T.LN[:, 0:8]), T.VF[:, 256 * t:256 * t + 128], "LNa VF0 VF1", "FX")
+            spread()
+        yield
+        for i, _ in enumerate(place(T.BN[:, :, 0:4], "BN0 BN1", T.LN[:, 8:16], "LNb")):
+            if i == 1:
+                tt(T.FX[:, a:a + 128], eA[:, 3, :], T.FX[:, a:a + 128], A.min, "FX", "FX", "eA")
             yield
         cp(fwin().indirect(T.LN[:, 8:16]), T.VF[:, 256 * t + 128:256 * t + 256], "LNb VFr", "FX")
         yield
@@ -649,10 +667,11 @@ def rank_program(g, core, T, topo):
     def seat_rest(t):
         fin = t == VIS - 1
         a, m0 = lo[t], 16 * t
-        zn, znk = T.ZN[:, 128 * t:128 * t + 128], "ZN0 ZN1"
+        zn, znk = T.ZN[:] if fin else T.SND[:, 136 * t + 4:136 * t + 132], "ZN0 ZN1"
         seated[0] = t
         ts(T.SN[:], T.OF[:, :, 0:4], float(NW), A.is_lt, -1.0, A.mult, rd="OF0 OF1", wr="SN")
         cp(T.LN[:, 0:8], T.OF[:, :, 4:8], "OF0 OF1", "LNa")
+        ts(T.LB[:], T.OF[:, :, 0:4], M0C, A.add, M0C, A.subtract, rd="OF0 OF1", wr="LB")
         if not fin:
             mm(dz[:, 80:88], T.ONB[:], T.LIVE[:, 0:8], True, False, "ONB LIVE", "dz")
             mm(dz[:, 80:88], T.ONB[:], T.SN[:], False, True, "ONB SN", "dz")
@@ -660,22 +679,22 @@ def rank_program(g, core, T, topo):
             act(L["aq"], dz[:, 80:88], AF.Copy, "", "AQ AS", "dz", accum_out=AS)
             act(T.MS[:, m0 + 8:m0 + 12], T.ONB[:, 0:4], AF.Copy, "ONB AS", "MSa", scale=AS)
             send(nxt, T.ML[:, m0:m0 + 16], T.MS[:, m0:m0 + 16], "aM%d" % t, "MS MSa")
-            arrives("aM%d" % t, "M%d" % t)
-            zrep(t + 1, 0)
+            arrives("aM%d" % t, "ML%d" % t)
         yield
-        if t in (1, 2):
-            cp(T.TT[:].indirect(T.L8[:]), T.VF[:, 256 * t:256 * t + 128], "L8 VF0 VF1", "TT TTd")
+        translate(t, 1)
         if fin:
-            act(T.OR[:], T.ID[:].indirect(T.CL[:, 24:32]), AF.Copy, "ID C4", "OR")
+            act(T.OR[:], T.ID[:].indirect(T.CL[:, 8:16]), AF.Copy, "ID CB", "OR")
         yield
         yield
         cp(T.X[:].indirect(T.LN[:, 0:8]), zn, "LNa " + znk, "X XL Xt")
         if not fin:
+            zrep(t + 1, 0)
             act(T.XW[:, a:a + 128], T.X[:, a:a + 128], AF.Copy, "X", "XW")
         yield
-        yield
+        if fin:
+            yield
         if not fin:
-            for _ in start(t + 1):
+            for _ in start(t + 1, 0):
                 yield
             if t == 2:
                 cp(T.L8[:], T.OF[:, :, 8:12], "OF0 OF1", "L8")
@@ -687,13 +706,13 @@ def rank_program(g, core, T, topo):
         cp(T.KN[:, a:z], T.KI[:, a:z], "KI%d" % i, "+KN")
 
     def converts():
-        for i in range(1, len(KCH)):
+        for i in range(1, len(KCH) - 1):
             yield
             yield
             convert(i)
 
     convert(0)
-    lines[:] = [[out_before(0)], [converts()], [late()], [start(0)]]
+    lines[:] = [[out_before(0)], [converts()], [late()], [start(0, 0), start(0, 1)]]
     while lines[0] or lines[1]:
         pull()
     zrep(0, 0)
@@ -711,7 +730,7 @@ def rank_program(g, core, T, topo):
             dma("Y", "early", T.yk[:], T.KN[:, NB:NW], rd="KN", wr="yk")
             dma("Y", "early", T.yx[:], T.X[:, NB:NW], rd="X", wr="yx")
         read.append("walk%d" % t)
-        lines[:] = [[feet3 if t else later()] + [out_feet(t)] + ([] if fin else [out_before(t + 1)]), [alive]]
+        lines[:] = [([feet3] if t else []) + [out_feet(t)] + ([] if fin else [out_before(t + 1)]), [alive]]
         other = iter(())
         for i in range(2 * ST):
             sums(t, i // 2, i % 2, other)
@@ -721,32 +740,30 @@ def rank_program(g, core, T, topo):
                 for h in range(2):
                     act(T.BN[:, h, 4:8], T.J8[:, 4 * h:4 * h + 4], AF.Identity, "J8", "+BN%d" % h, bias=float(lo[t]))
         seat_sums(t, 0)
-        read.append("end%d" % t)
         if t in (1, 2):
-            cp(T.L8[:], T.ML[:, 16 * (t - 1):16 * (t - 1) + 8], "M%d" % (t - 1), "L8")
-        pull()
-        act(T.EQ[0:64, 0:4, :], eA[0:64], AF.Relu, "", "EQA", "eA", bias=-12.0 + EPS)
-        seat_count(0)
+            cp(T.L8[:], T.ML[:, 16 * (t - 1):16 * (t - 1) + 8], "ML%d" % (t - 1), "L8")
+        first, second = seat_kin(t, 0), seat_kin(t, 1)
         for _ in other:
             pull()
         while fin and lines[0]:
             pull()
-        send(prv if fin else nxt, T.CL[:, 8 * t:8 * t + 8], T.BL[:, 64 * t + 48:64 * t + 56], "aB" if fin else "aC%d" % t,
-             "BL%d0 BL%d1" % (4 * t + 3, 4 * t + 3))
-        arrives("aB" if fin else "aC%d" % t, "C%d" % (t + 1))
+        if fin:
+            send(prv, T.CL[:, 8:16], T.BL[:, 64 * t + 48:64 * t + 56], "aB", "BL%d0 BL%d1" % (4 * t + 3, 4 * t + 3))
+            arrives("aB", "CB")
         seat_sums(t, 1)
-        first, second = seat_kin(t, 0), seat_kin(t, 1)
+        translate(t, 0)
         next(first)
         pull()
         next(first)
         pull()
         while not fin and lines[0] and t + 1 not in read:
             pull()
-        for i in (0, 1):
-            ts(T.EQ[:, 4:8, 32 * i:32 * i + 32], eq[i][:, 0:4, :], -12.0 + EPS, A.add, 0.0, A.max, wr="EQ%d" % i, ps="e%d" % i)
         if fin:
-            parents(t)
             lines[:] = [[seat_feet(t)]]
+        zsum(1)
+        seat_z(t, 1)
+        for i in (0, 1):
+            ts(T.EQ[:, 4:8, 32 * i:32 * i + 32], eq[i][:, 4:8, :], -12.0 + EPS, A.add, 0.0, A.max, wr="EQ1%d" % i, ps="e%d" % i)
         seat_count(1)
         if fin:
             pull()
@@ -754,7 +771,6 @@ def rank_program(g, core, T, topo):
         if not fin:
             seat_kin_of(t, 1)
             parents(t)
-        seat_z(t, 1)
         pull()
         next(second)
         if fin:
@@ -773,7 +789,7 @@ def rank_program(g, core, T, topo):
             arrives("aTB", "TBL")
             dma("Y", "ot", T.OT[0::16, 0:NW], T.TBL[:], rd="TBL", wr="OT")
     a = lo[VIS - 1]
-    dma("Y", "out", T.yz[:], T.ZN[:, 384:512], rd="ZN0 ZN1")
+    dma("Y", "out", T.yz[:], T.ZN[:], rd="ZN0 ZN1")
     dma("Y", "out", T.yp[:], T.KN[0::16, 0:NB], rd="KN")
     dma("S", "out", T.yk[:, a - NB:a - NB + 128], T.KN[:, a:a + 128], rd="KN", wr="yk")
     for u, z in ((NB, a), (a + 128, NW)):

from concourse.mybir import AluOpType as A, ActivationFunctionType as AF

NW, NB, NJ, VIS, ST = 3584, 2560, 1024, 4, 3
WN = 3856
DA, DB = 3600, 3728
WT, SL = 131072.0, 4096
BIG = 4096.0
OFS = 1792.0
SAT = 2
M0C = 1.5 * 2.0 ** 23
EPS = 2.0 ** -20
CUTS = (0, 24, 32, 40, 48)
ABS = {0: 0, 2: 1, 3: 3}
LAST = [j % 16 for j in range(CUTS[-2], CUTS[-1])]
LISTS = "d0 d1 e0 c0 cn ch ny bov bou held dum ndum sq3 aq".split()
BUFS = {
    "float32": "KN:3856 FX:3856 TT:3856 OT:3856 ID:3584 TRF:224 ML:48 MS:48 COLF:16 CF:160 C15F:128 CGF:128 D:128 B0:128 IF:128 RG8:128 "
               "R0:68 RS:128 I8:8 J8:8 NN:32 NR:1024 VF:1024 FVO:128 TM:128 TS:128 MU:128 MS1:128 GZ:128 UM:128 "
               "MU2:128 MS2:128 MS3:128 MV:128 SM:112 OR:128 VM:136 GG:136 BB:136 SC:136 N0:136 ZQ:128 "
               "SND:408 LND:408 BF8:128 BLK:128 FB:128 LB:8 BIT:8 RPI:128 CMP:16 E2:32 A1:32 OO:32 SQ:16 NO:16 PK0:16 PK1:16 PKO:16",
    "bfloat16": "X:3856 XW:3584 BT:4096 Z0:128 ZN:128 ZR:2048 IB:128 NIB:128 ONB:128 BON:128 SW:144 CK:68 CW:4 BCB:1024 DIFF:2048 "
                "XB:128 CDE:128 CDO:128 LIVE:16 LX:128 SN:8 NL:8 PO:8 NU:256 RP:128",
    "float16": "C16:128 C2:256 IE:160 IO:160 RH8:128 F16:1024",
    "int32": "KI:3592 FI:1024 BI:128 TRI:224 COLI:4 BC:8 AI:8 C8I:8",
    "uint16": "CL:16 BL:256 KL:128 YL:16 LO:16 VL:8 LS:16 LN:16 L8:8 C8:8",
}
SCRATCH = {"TD": ("dram", [128, 224], "float32"), "TB": ("dram", [128, 224], "float32"), "TBL": ("dram", [128, 224], "float32"),
           "BTD": ("dram", [16, 64, 64], "bfloat16"),
           "AB": ("sbuf", [128, 128, 17], "bfloat16"), "EQ": ("sbuf", [128, 8, 128], "bfloat16"), "CT": ("sbuf", [128, 4, 32], "float16"),
           "CT2": ("sbuf", [128, 8, 32], "float16"), "VK": ("sbuf", [128, 2, 128], "float32"), "BN": ("sbuf", [128, 2, 16], "float32"),
           "OF": ("sbuf", [128, 2, 16], "float32"), "DUM": ("sbuf", [128, 2, 16], "float32")}
for _d in BUFS:
    for _b in BUFS[_d].split():
        SCRATCH[_b.split(":")[0]] = ("sbuf", [128, int(_b.split(":")[1])], _d)
SCRATCH["dz"] = ("psum", [128, 512], "float32")
SCRATCH["eA"] = ("psum", [128, 4, 128], "float32")
for _i in range(4):
    SCRATCH["e%d" % _i] = ("psum", [128, 16, 32], "float32")
for _i in range(2):
    SCRATCH["k%d" % _i] = ("psum", [128, 4, 128], "float32")
KCH = [(NB, NW), (0, 1024), (1024, 2048), (2048, NB)]
SEMAPHORES = (["V", "S", "P", "G", "lx", "lw", "lf", "lb", "lz", "lt", "btd", "bt", "tt", "tb", "ot", "out", "early", "aT", "aB", "aTB", "loc"]
              + ["kn%d" % i for i in range(len(KCH))] + ["a%s%d" % (k, t) for k in ("Z0", "Z1", "M") for t in range(3)])


def rank_program(g, core, T, topo):
    rank = T.rank_of(core)
    if rank is None:
        return
    cores = T.cores
    n = len(cores)
    Q = {"V": g.vector, "S": g.scalar, "P": g.tensor, "G": g, "Y": g.sync}
    tot, waited, last, readers, excl = {}, {}, {}, {}, {}

    def need(eng, sem, val):
        val = tot[sem] if val is None else val
        if waited.get((eng, sem), 0) < val:
            Q[eng].wait_ge(T.sem[sem], val)
            waited[(eng, sem)] = val

    def before(eng, rd, wr, ps):
        for k in rd:
            if k in last:
                need(eng, last[k][0], last[k][1])
        for w in wr:
            k = w.lstrip("+")
            if k in last and (k == w or last[k][0] != eng):
                need(eng, last[k][0], last[k][1])
            for s, v in readers.get(k, {}).items():
                if s != eng:
                    need(eng, s, v)
        for k in ps:
            for s, v in excl.get(k, {}).items():
                if s != eng:
                    need(eng, s, v)

    def after(sem, val, rd, wr, ps):
        for k in rd:
            readers.setdefault(k, {})[sem] = val
        for w in wr:
            last[w.lstrip("+")] = (sem, val)
            readers[w.lstrip("+")] = {}
        for k in ps:
            excl.setdefault(k, {})[sem] = val

    def op(eng, fn, rd, wr, ps):
        rd, wr, ps = rd.split(), wr.split(), ps.split()
        before(eng, rd, wr, ps)
        fn().then_inc(T.sem[eng], 1)
        tot[eng] = tot.get(eng, 0) + 1
        after(eng, tot[eng], rd, wr, ps)

    def ts(out, in0, s1, op0, s2=None, op1=None, rd="", wr="", ps=""):
        if op1 is None:
            op("V", lambda: g.vector.tensor_scalar(out=out, in0=in0, scalar1=s1, scalar2=None, op0=op0), rd, wr, ps)
        else:
            op("V", lambda: g.vector.tensor_scalar(out=out, in0=in0, scalar1=s1, scalar2=s2, op0=op0, op1=op1), rd, wr, ps)

    def tt(out, in0, in1, o, rd="", wr="", ps=""):
        op("V", lambda: g.vector.tensor_tensor(out=out, in0=in0, in1=in1, op=o), rd, wr, ps)

    def cp(out, in_, rd="", wr="", ps=""):
        op("V", lambda: g.vector.tensor_copy(out=out, in_=in_), rd, wr, ps)

    def scan(out, d0, d1, init, o0, o1, rd="", wr="", ps=""):
        op("V", lambda: g.vector.tensor_tensor_scan(out=out, data0=d0, data1=d1, initial=init, op0=o0, op1=o1), rd, wr, ps)

    def turn32(out, in_, rd, wr):
        op("V", lambda: g.vector.transpose(out=out, in_=in_), rd, wr, "")

    def fill(ap, c, wr):
        op("V", lambda: g.vector.memset(ap, c), "", wr, "")

    def act(out, in_, f, rd="", wr="", ps="", **kw):
        op("S", lambda: g.scalar.activation(out=out, in_=in_, func=f, **kw), rd, wr, ps)

    def mm(out, l, r, a, z, rd="", ps=""):
        op("P", lambda: g.tensor.matmul(out=out, lhsT=l, rhs=r, start=a, stop=z), rd, "", ps)

    def iota(out, pat, base, cm, wr, flag=True):
        if flag:
            op("G", lambda: g.iota(out=out, pattern=pat, base=base, channel_multiplier=cm, allow_small_or_imprecise_dtypes=True), "", wr, "")
        else:
            op("G", lambda: g.iota(out=out, pattern=pat, base=base, channel_multiplier=cm), "", wr, "")

    def keep(ap, pat, base, cm, key):
        op("G", lambda: g.affine_select(out=ap, in_=ap, pattern=pat, compare_op=A.is_ge, fill=0.0, base=base, channel_multiplier=cm), key, key, "")

    def dma(eng, grp, out, in_, rd="", wr=""):
        rd, wr = rd.split(), wr.split()
        for k in rd:
            if k in last:
                need(eng, last[k][0], last[k][1])
        for k in wr:
            if k in last and last[k][0] != grp:
                need(eng, last[k][0], last[k][1])
            for s, v in readers.get(k, {}).items():
                need(eng, s, v)
        Q[eng].dma_start(out=out, in_=in_).then_inc(T.sem[grp], 16)
        tot[grp] = tot.get(grp, 0) + 16
        after(grp, None, rd, wr, [])

    def send(dst, out, in_, sem, rd):
        before("G", rd.split(), [], [])
        rid, pid, _ = topo.addr(dst)
        m = 0
        for e in topo.engines(core, dst)[:8]:
            m |= 1 << e
        g.remote_dma(out, in_, T.sem[sem], T.sem.loc, pid, rid, m)
        tot["loc"] = tot.get("loc", 0) + 8

    def arrives(sem, key):
        tot[sem] = 8
        last[key] = (sem, 8)
        readers[key] = {}

    nxt, prv = cores[(rank + 1) % n], cores[(rank - 1) % n]
    lo = [NB + 128 * ((rank - t) % n) for t in range(VIS)]
    D, RS, dz, eA = T.D[:], T.RS[:], T.dz, T.eA
    eq, kk = [T["e%d" % i] for i in range(4)], [T.k0, T.k1]
    PF, P15, PG, OD, EV, M0, NM0, PW, P16, AS = [T.COLF[:, i:i + 1] for i in range(10)]
    PI, P15I, PGI, PEI = [T.COLI[:, i:i + 1] for i in range(4)]
    L = {k: T.SM[:, 8 * i:8 * i + 8] for i, k in enumerate(LISTS)}

    def t3(out, a, o, b):
        tt(L[out], L[a], L[b], o, a + " " + b, out)

    dma("Y", "lf", T.FI[0:8, :], T.ft[:], wr="FI")
    dma("Y", "lb", T.BI[0:8, :], T.bs[:], wr="BI")
    dma("S", "lz", T.Z0[:], T.z0[:], wr="Z00 Z01")
    dma("S", "lt", T.TRI[:], T.tr[:], wr="TRI")
    for i, (a, z) in enumerate(KCH):
        dma("Y", "kn%d" % i, T.KI[:, a:z], T.kn[:, a:z], wr="KI%d" % i)
    dma("Y", "lw", T.XW[:], T.x0[:], wr="XW")
    dma("Y", "lx", T.X[:, 0:NW], T.x0[:], wr="XL")

    iota(PI, [[0, 1]], 0, 1, "PI", False)
    iota(PF, [[0, 1]], 0, 1, "PF")
    iota(T.CGF[:], [[1, 8], [0, 16]], 0, 0, "CGF")
    iota(T.I8[:], [[16, 8]], 0, 0, "I8")
    iota(T.C15F[:], [[0, 8], [1, 16]], 0, 0, "C15F")
    iota(T.CF[:], [[1, 160]], 0, 0, "CF")
    fill(T.CK[:], 0.0, "CK")
    fill(RS, 1.0, "RS")
    fill(T.R0[:], -1.0e9, "R0")
    fill(T.ONB[:], 1.0, "ONB")
    fill(T.E2[:, 0::4], 0.0, "E2")
    fill(T.E2[:, 2::4], 1.0, "+E2")
    fill(T.A1[:, 2::4], 0.0, "A1c")
    fill(T.N0[:], OFS, "N00 N01")
    fill(T.RS[:, 0::16], 0.0, "RS")
    fill(T.R0[:, 0::17], 1.0e9, "R0")
    fill(L["c0"], 0.0, "c0")
    fill(T.KI[:, NW:], -1, "KIt")
    iota(T.CK[0:1, 0:68], [[0, 4], [SL, 17]], 0, 0, "CK")
    iota(T.KN[:, NW:WN], [[0, WN - NW]], -1, 0, "KNt")
    ts(P15I, PI, 15, A.bitwise_and, rd="PI", wr="P15I")
    ts(PGI, PI, 4, A.arith_shift_right, rd="PI", wr="PGI")
    ts(PEI, PI, 4, A.arith_shift_right, 1, A.bitwise_and, rd="PI", wr="PEI")
    for b in range(6):
        ts(T.BC[0:64, b:b + 1], PI[0:64, :], b, A.arith_shift_right, 1, A.bitwise_and, rd="PI", wr="+BC")
    cp(P15, P15I, "P15I", "P15")
    cp(PG, PGI, "PGI", "PG")
    cp(OD, PEI, "PEI", "OD")
    ts(P16, PF, 16.0, A.add, rd="PF", wr="P16")
    ts(T.BIT[0:64, 0:6], T.BC[0:64, 0:6], 2.0, A.mult, rd="BC", wr="BIT")
    ts(T.RH8[:], T.CGF[:], PF, A.is_equal, rd="CGF PF", wr="RH8")
    ts(T.RG8[:], T.CGF[:], PF, A.is_equal, rd="CGF PF", wr="RG8")
    ts(M0, P15, 0.0, A.is_equal, rd="P15", wr="M0")
    ts(NM0, P15, 0.0, A.not_equal, rd="P15", wr="NM0")
    ts(EV, OD, 0.0, A.is_equal, rd="OD", wr="EV")
    ts(PW, PG, 16.0, A.mult, 15.0, A.add, rd="PG", wr="PW")
    act(T.J8[:], T.I8[:], AF.Identity, "I8 P15", "J8", bias=P15)
    ts(D, T.C15F[:], P15, A.is_equal, rd="C15F P15", wr="D")
    cp(T.BF8[0:8, :], T.BI[0:8, :], "BI", "BF8")
    mm(eq[2][:, 4:8, :], T.RG8[0:8, :], T.BF8[0:8, :], True, True, "RG8 BF8", "e2")

    def feet(h):
        ps, pk = eq[1 + 2 * h][:], "e%d" % (1 + 2 * h)
        ts(T.F16[0:8, 512 * h:512 * h + 512], T.FI[0:8, 512 * h:512 * h + 512], -OFS, A.add, rd="FI", wr="F16%d" % h)
        mm(ps, T.RH8[0:8, :], T.F16[0:8, 512 * h:512 * h + 512], True, True, "RH8 F16%d" % h, pk)
        act(T.FX[:, NB + 512 * h:NB + 512 * h + 512], ps, AF.Identity, "", "+FX", pk, bias=OFS)

    feet(rank // 4)
    ts(T.IE[:], T.CF[:], P16, A.is_equal, EV, A.mult, rd="CF P16 EV", wr="IE")
    ts(T.IO[:], T.CF[:], P16, A.is_equal, OD, A.mult, rd="CF P16 OD", wr="IO")
    ts(T.IF[:], T.CF[:, 0:128], PF, A.is_equal, rd="CF PF", wr="IF")
    ts(T.SW[:], T.CF[:, 0:144], PW, A.is_equal, WT, A.mult, rd="CF PW", wr="SW")
    feet(1 - rank // 4)
    act(L["ndum"], T.J8[:], AF.Identity, "J8", "ndum", scale=-1.0, bias=OFS - DA)
    for out, d, key in ((L["dum"], DA, "dum"), (T.A1[:, 3::4], DA, "A1d"), (T.PK1[:, 1::2], DA, "PK1b"),
                        (T.DUM[:, :, 0:4], DA, "DUM"), (T.DUM[:, :, 4:8], DB, "+DUM"), (T.DUM[:, :, 8:12], DA, "+DUM")):
        act(out, T.J8[:], AF.Identity, "J8", key, bias=float(d))
    for t in range(VIS):
        act(T.NN[:, 8 * t:8 * t + 8], T.J8[:], AF.Identity, "J8", "+NN", bias=float(lo[t]))
    act(T.IB[:], T.IF[:], AF.Copy, "IF", "IB")
    act(T.NIB[:], T.IF[:], AF.Copy, "IF", "NIB", scale=-1.0)
    last["XWp"] = last["XW"]

    iota(T.RPI[:], [[0, 4], [1, 2], [0, 16]], 0, 0, "RPI")
    iota(T.C8I[:], [[1, 8]], 0, 0, "C8I", False)
    for b in range(6):
        iota(T.BCB[0:64, 64 * b:64 * b + 64], [[0, 32 >> b], [2, 2], [0, 1 << b]], -1, 0, "+BCa")
        act(T.BCB[0:64, 384 + 64 * b:448 + 64 * b], T.ONB[0:64, 0:64], AF.Identity, "ONB BIT", "+BCb", scale=T.BIT[0:64, b:b + 1], bias=-1.0)
    iota(T.BCB[0:64, 768:1024], [[0, 256]], 0, 0, "+BCa")
    iota(T.FX[:, 0:NB], [[0, NB]], -1, 0, "FXa")

    def constants_g():
        iota(T.NU[:], [[0, 256]], -32, 0, "NU")
        iota(T.FX[:, NW:WN], [[0, WN - NW]], -1, 0, "FXb")
        keep(T.NU[:], [[-16, 8], [0, 2], [-1, 16]], 0, 1, "NU")
        iota(T.ID[:], [[1, NW]], 0, 0, "ID")
        iota(T.X[:, NW:WN], [[0, WN - NW]], 0, 0, "Xt")
        iota(T.TT[:, NW:WN], [[0, WN - NW]], 0, 0, "TT")

    def kwin():
        return T.KN[:, 0:WN]

    def fwin():
        return T.FX[:, 0:WN]

    lines, read, seated = [], [], [-1]

    def pull(first=0):
        for line in lines[first:]:
            while line and next(line[0], "end") == "end":
                line.pop(0)

    def late():
        for _ in range(4):
            yield
        cp(T.TRF[:], T.TRI[:], "TRI", "TRF")
        send(nxt, T.TD[:], T.TRF[:], "aT", "TRF")
        arrives("aT", "TD")
        constants_g()
        for b in range(16):
            dma("Y", "btd", T.BTD[b], T.BCB[0:64, 64 * b:64 * b + 64], rd="BCa BCb", wr="BTD")
        for i in range(8):
            dma("Y", "bt", T.BT[16 * i:16 * i + 16, :], T.BTD[:], rd="BTD", wr="BT")
        for p in range(16):
            dma("Y", "tt", T.TT[p::16, 0:NW], T.TD[:], rd="TD", wr="TTd")
        yield
        yield
        yield
        ts(T.BON[:], T.CGF[:], PG, A.is_equal, float(NW), A.mult, rd="CGF PG", wr="BON")
        act(T.BLK[:], T.BON[:], AF.Sign, "BON", "BLK")
        act(T.CDE[:, 64:128], T.ONB[:, 0:64], AF.Copy, "ONB", "CDE1")
        act(T.CDO[:, 64:128], T.ONB[:, 0:64], AF.Copy, "ONB", "CDO1")
        act(T.B0[:], T.BLK[:], AF.Copy, "BLK M0", "B0", scale=M0)
        yield
        fill(T.LIVE[:], 0.0, "LIVE")
        cp(T.C8[:], T.C8I[:], "C8I", "C8")
        fill(T.PK0[:], 0.0, "PK0")
        yield
        ts(T.RP[:], T.RPI[:], OD, A.is_equal, rd="RPI OD", wr="RP")
        yield
        fill(T.CW[:, 0:2], BIG, "CW")
        fill(T.CW[:, 2:4], BIG / EPS, "+CW")
        fill(T.MS[:], 0.0, "MS")
        yield

    def rows(t):
        act(T.VF[:, 256 * t + 128:256 * t + 256], T.CF[:, 0:128], AF.Identity, "CF", "VFr", bias=float(lo[t]))
        for h in range(2):
            a = 256 * t + 128 * h
            act(T.NR[:, a + 64:a + 128], T.CF[:, 0:64], AF.Copy, "CF", "+NR", scale=0.0)
            act(T.NR[:, a:a + 64], T.VF[:, 256 * t + 128 + 64 * h:256 * t + 192 + 64 * h], AF.Copy, "VFr M0", "+NR", scale=M0)

    def to_list(out, b0, b1, pk):
        for c, (m, mk) in enumerate(((T.IE, "IE"), (T.IO, "IO"))):
            for gp in range(2):
                w = 16 + 16 * (c - gp)
                mm(out[:, 2 * b0 + c:2 * b1:2], m[:, w:w + 128], T.CT2[:, b0:b1, 16 * gp], gp == 0, gp == 1, mk + " CT2", pk)

    def out_before(t):
        a, z = lo[t], lo[t] + 128
        y0, pl = T.MS1[:, 15::16], eA[:, 1, 0:16]
        tt(T.MU[:], T.FX[:, a:z], D, A.mult, "FX D", "MU")
        act(T.CMP[:, 0:8], T.J8[:], AF.Identity, "J8", "CMPa", bias=a - OFS)
        yield
        scan(T.MS1[:], RS, T.MU[:], 0.0, A.mult, A.add, "RS MU", "MS1")
        ts(T.C2[:, 128:256], T.KN[:, a:z], -OFS, A.add, rd="KN", wr="C2b")
        yield
        cp(T.YL[:, 0:8], y0, "MS1", "YLa")
        tt(L["d0"], y0, L["dum"], A.subtract, "MS1 dum", "d0")
        act(T.SQ[:, 0:8], y0, AF.Square, "MS1", "SQ", bias=-a - 63.5)
        act(T.SQ[:, 8:16], y0, AF.Square, "MS1", "+SQ", bias=-lo[t - 1] - 63.5)
        if t:
            yield
            ts(T.C2[:, 0:128], kwin().indirect(T.YL[:, 0:8]), -OFS, A.add, rd="KN YLa", wr="C2a")
            read.append(t)
        yield
        b0 = 0 if t else 4
        turn32(T.CT2[:, b0:8, :], T.C2[:, 32 * b0:256], "C2a C2b", "CT2")
        to_list(pl, b0, 8, "eA")
        yield
        ts(T.NO[:], T.SQ[:], 4096.0, A.is_ge, rd="SQ", wr="NO")
        yield
        if t == 1:
            yield
        if t:
            tt(L["e0"], pl[:, 0:8], T.CMP[:, 0:8], A.is_equal, "CMPa", "e0l", "eA")
        ts(T.CMP[:, 8:16], pl[:, 8:16], a - OFS - 0.5, A.max, z - OFS - 0.5, A.min, wr="CMPb", ps="eA")
        tt(L["d1"] if t else T.A1[:, 0::4], L["d0"], T.NO[:, 0:8], A.mult, "d0 NO", "d1 A1a")
        yield
        if t:
            tt(L["c0"], L["e0"], T.NO[:, 8:16], A.mult, "e0l NO", "c0")
            yield
            ts(L["cn"], L["c0"], float(a - DA), A.mult, rd="c0", wr="cn")
            tt(T.A1[:, 2::4], L["c0"], L["ndum"], A.mult, "c0 ndum", "A1c")
            yield
            tt(T.A1[:, 0::4], L["d1"], L["cn"], A.subtract, "d1 cn", "A1a")
            yield

    def out(t):
        a, z = lo[t], lo[t] + 128
        pl = eq[0][:, 8, 0:16]
        while t and lines[0]:
            yield
        if t:
            ts(T.C2[:, 0:128], kwin().indirect(T.YL[:, 0:8]), -OFS, A.add, rd="KN YLa", wr="C2a")
            ts(T.C2[:, 128:256], T.KN[:, a:z], -OFS, A.add, rd="KN", wr="C2b")
        else:
            ts(T.C2[:, 0:128], T.KI[:].indirect(T.YL[:, 0:8]), -OFS, A.add, rd="KI0 KI1 KI2 KI3 KIt YLa", wr="C2a")
        yield
        turn32(T.CT2[:], T.C2[:], "C2a C2b", "CT2")
        to_list(pl, 0, 8, "e0")
        if t == 0:
            convert(len(KCH) - 1)
        act(T.GZ[:], kwin().indirect(T.YL[:, 0:8]), AF.Copy, "KN KNt YLa NM0", "GZ", scale=NM0)
        act(T.UM[:], T.KN[:, a:z], AF.Copy, "KN M0", "UM", scale=M0)
        if t:
            yield
        yield
        tt(T.E2[:, 1::4], pl[:, 0:8], T.CMP[:, 0:8], A.is_equal, "CMPa", "E2a", "e0")
        tt(T.A1[:, 1::4], pl[:, 0:8], L["c0"], A.mult, "c0", "A1b", "e0")
        tt(T.E2[:, 3::4], pl[:, 8:16], T.CMP[:, 8:16], A.not_equal, "CMPb", "E2b", "e0")
        read.append("met%d" % t)
        yield
        scan(T.OO[:], T.E2[:], T.A1[:], 0.0, A.mult, A.add, "E2 E2a E2b A1a A1b A1c A1d", "OO")
        yield
        cp(T.LO[:, 0:8], T.OO[:, 3::4], "OO", "LOa")
        yield
        tt(kwin().indirect(T.LO[:, 0:8]), T.GZ[:], T.UM[:], A.add, "LOa GZ UM", "KN")
        yield

    def live(t):
        pl = eq[0][:, 8, 0:16]
        while "met%d" % t not in read:
            yield
        yield
        tt(L["ch"], L["c0"], T.E2[:, 1::4], A.is_gt, "c0 E2a", "ch")
        yield
        tt(L["ny"], L["ch"], T.NO[:, 0:8], A.max, "ch NO", "ny")
        ts(T.YL[:, 8:16], pl[:, 8:16], OFS, A.add, wr="YLb", ps="e0")
        yield
        tt(T.LIVE[:, 0:8], L["ny"], T.E2[:, 3::4], A.mult, "ny E2b", "LIVE")
        ts(L["held"], T.OO[:, 3::4], float(NW), A.is_lt, rd="OO", wr="held")
        tt(L["bou"], pl[:, 8:16], L["ndum"], A.add, "ndum", "bou", "e0")
        yield
        while "walk%d" % t not in read:
            yield
        act(T.NL[:], T.LIVE[:, 0:8], AF.Identity, "LIVE", "NL", scale=-BIG, bias=BIG)
        if t:
            second = start(t, 1)
            next(second)
            yield
            next(second)
            cp(T.AI[:, 0:4], T.ML[:, 16 * t - 8:16 * t - 4], "ML%d" % (t - 1), "AI0")
            yield
            next(second)
            ts(T.AI[:, 4:8], T.AI[:, 0:4], 31, A.bitwise_and, rd="AI0", wr="AI1")
            yield
            next(second)
            ts(T.CK[0:1, 0::17], T.AI[0:1, 4:8], WT, A.mult, rd="AI1", wr="CK")
        yield
        yield
        tt(T.LX[:], T.LIVE[:].indirect(T.C8[:]), D, A.mult, "LIVE C8 D", "LX")
        yield
        mm(eA[:, 2, :], T.BON[:], T.LX[:], True, True, "BON LX", "eA")
        yield

    def place(met, rd, out, key):
        tt(T.PK0[:, 1::2], T.MS2[:, 15::16], met, A.is_equal, "MS2 " + rd, "PK0")
        yield
        scan(T.PKO[:], T.PK0[:], T.PK1[:], 0.0, A.mult, A.add, "PK0 PK1a PK1b", "PKO")
        yield
        cp(out, T.PKO[:, 1::2], "PKO", key)
        yield

    def out_feet(t):
        a, z = lo[t], lo[t] + 128
        while lines[1]:
            yield
        tt(T.MU2[:], fwin().indirect(T.YL[:, 8:16]), D, A.mult, "FX FXa FXb YLb D", "MU2")
        act(T.FVO[:], T.FX[:, a:z], AF.Copy, "FX", "FVO")
        yield
        scan(T.MS2[:], RS, T.MU2[:], 0.0, A.mult, A.add, "RS MU2", "MS2")
        tt(T.PK1[:, 0::2], L["held"], L["bou"], A.mult, "held bou", "PK1a")
        yield
        tt(T.FX[:, a:z], eA[:, 2, :], T.FX[:, a:z], A.max, "FX", "FX", "eA")
        for _ in place(T.NN[:, 8 * t:8 * t + 8], "NN", T.LO[:, 8:16], "LOb"):
            yield
        cp(fwin().indirect(T.LO[:, 8:16]), T.FVO[:], "LOb FVO", "FX")
        yield

    def seat_begin(t, i):
        while i == 2 and lines[1]:
            pull(1)
        if i >= 2:
            order(0, i - 2)

    def order(h, q):
        out = eq[q][:, 4 * h:4 * h + 4, :]
        mm(out, T.IB[:], T.NU[:, 128 * h:128 * h + 128], True, False, "IB NU", "e%d" % q)
        mm(out, T.LX[32 * q:32 * q + 32, :], T.RP[32 * q:32 * q + 32, :], False, False, "LX RP", "e%d" % q)

    def start(t, h):
        a, c = 64 * h, T.CL[:, 4 * h:4 * h + 4]
        if t == 0:
            tt(T.TM[:, a:a + 64], eq[2][:, 4 + 2 * h:6 + 2 * h, :], T.D[:, 0:64], A.mult, "D", "TM%d" % h, "e2")
        else:
            cp(c, T.LND[:, 136 * t - 136 + 132 * h:136 * t - 132 + 132 * h], "Z%d%d" % (t, h), "CL%d" % h)
            yield
            tt(T.TM[:, a:a + 64], T.TT[:].indirect(c), T.D[:, 0:64], A.mult, "TT TTd D CL%d" % h, "TM%d" % h)
        yield
        scan(T.TS[:, a:a + 64], T.RS[:, 0:64], T.TM[:, a:a + 64], 0.0, A.mult, A.add, "RS TM%d" % h, "TS%d" % h)
        yield
        cp(T.BL[:, 64 * t + 4 * h:64 * t + 4 * h + 4], T.TS[:, a + 15:a + 64:16], "TS%d" % h, "BL%d%d" % (4 * t, h))
        yield

    def zrep(t, h):
        zz = T.LND[:, 136 * t - 132 + 64 * h:136 * t - 68 + 64 * h] if t else T.Z0[:, 64 * h:64 * h + 64]
        for k in range(16):
            act(T.ZR[:, 1024 * h + k:1024 * h + 1024:16], zz, AF.Copy, "Z%d%d" % (t, h), "+ZR%d" % h)

    def far(t):
        act(T.XW[:, lo[t]:lo[t] + 128], T.ONB[:], AF.Copy, "ONB", "XWp", scale=4096.0)

    def sums(t, s, h, other):
        q, a, k, pk = 4 * t + s, 64 * h, kk[h], "k%d" % h
        bl, bk = T.BL[:, 16 * q + 4 * h:16 * q + 4 * h + 4], "BL%d%d" % (q, h)
        bf, fk = (T.TS[:, a + 15:a + 64:16], "TS%d" % h) if s == 0 else (T.SC[:, 68 * h + 16:68 * h + 68:17], "SC%d" % h)

        def gather(c):
            u, z = a + CUTS[c], a + CUTS[c + 1]
            tt(T.DIFF[:, 16 * u:16 * z], T.XW[:].indirect(T.KL[:, u:z]), T.ZR[:, 16 * u:16 * z], A.subtract,
               "XW XWp KL%d ZR%d" % (h, h), "DF%d%d" % (h, c))
            if c in ABS:
                u = a + CUTS[ABS[c]]
                if c == len(CUTS) - 2:
                    readers["AB%d" % h] = {}
                act(T.AB[:, u:z, 1:17], T.DIFF[:, 16 * u:16 * z], AF.Abs, "DF%d%d" % (h, c), "+AB%d" % h)
            if c < 4 and next(other, "end") == "end":
                pull(1)

        def keys(js, end):
            for j in js:
                mm(k[:, 0, 0:68], T.SW[:, 15 - j:143 - j], T.AB[:, a + j:a + 64:16, :], False, end and j == js[-1], "SW AB%d" % h, pk)

        cp(T.KL[:, a:a + 64], kwin().indirect(bl), "KN " + bk, "KL%d" % h)
        act(T.N0[:, 68 * h:68 * h + 68:17], bf, AF.Copy, fk, "N0%d" % h)
        if q:
            act(T.XB[:, a:a + 64], T.X[:, 0:NW].indirect(bl), AF.Copy, "X XL " + bk, "XB%d" % h)
        u, z, w = a + CUTS[-1], a + 64, 16 * (64 - CUTS[-1])
        act(T.DIFF[:, 16 * u:16 * z], T.XW[:].indirect(T.KL[:, u:z]), AF.Copy, "XW XWp KL%d" % h, "DF%ds" % h)
        mm(dz[:, 128:128 + w], T.NIB[:], T.ZR[:, 16 * u:16 * z], True, False, "NIB ZR%d" % h, "dz")
        mm(dz[:, 0:64], T.NIB[:], T.ZR[:, 16 * a:16 * a + 1024:16], False, False, "NIB ZR%d" % h, "dz")
        mm(dz[:, 0:64], T.IB[:], T.XB[:, a:a + 64], False, False, "IB XB%d" % h, "dz")
        mm(dz[:, 128:128 + w], T.IB[:], T.DIFF[:, 16 * u:16 * z], False, True, "IB DF%ds" % h, "dz")
        mm(k[:, 1:3, 0:34], T.IF[:], T.N0[:, 68 * h:68 * h + 68], True, False, "IF N0%d" % h, pk)
        pull()
        gather(0)
        ts(T.C16[:, a:a + 64], T.KL[:, a:a + 64], -OFS, A.add, rd="KL%d" % h, wr="C16%d" % h)
        gather(1)
        turn32(T.CT[:, 2 * h:2 * h + 2, :], T.C16[:, a:a + 64], "C16%d" % h, "CT%d" % h)
        for c, (m, mk) in enumerate(((T.IE, "IE"), (T.IO, "IO"))):
            for gp in range(2):
                mm(k[:, 1:3, 17 * c + 1:17 * c + 17], m[:, 16 + 16 * (c - gp):144 + 16 * (c - gp)],
                   T.CT[:, 2 * h:2 * h + 2, 16 * gp:16 * gp + 16], False, False, mk + " CT%d" % h, pk)
        for c in range(2, len(CUTS) - 1):
            if c == SAT:
                act(T.AB[:, u:z, 1:17], dz[:, 128:128 + w], AF.Abs, "", "+AB%d" % h, "dz")
                act(T.AB[:, a:a + 64, 0], dz[:, 0:64], AF.Abs, "", "+AB%d" % h, "dz")
            if c == len(CUTS) - 2:
                mm(k[:, 0, 0:68], T.ONB[:], T.CK[:], False, False, "ONB CK", pk)
                seat_begin(t, 2 * s + h)
                keys([j for j in range(16) if j not in LAST], False)
            gather(c)
        keys(LAST, True)
        if s or h:
            if len(CUTS) < 6:
                pull()
            next(other)
            pull()

    def least(t, s, h):
        q, k, pk, a = 4 * t + s + 1, kk[h], "k%d" % h, 68 * h
        scan(T.VM[:, a:a + 68], T.R0[:], k[:, 0, 0:68], 1.0e9, A.max, A.min, "R0", "VM%d" % h, pk)
        yield
        tt(T.GG[:, a:a + 68], k[:, 0, 0:68], T.VM[:, a:a + 68], A.subtract, "VM%d" % h, "GG%d" % h, pk)
        yield
        tt(T.BB[:, a:a + 68], k[:, 1:3, 0:34], T.GG[:, a:a + 68], A.subtract, "GG%d" % h, "BB%d" % h, pk)
        yield
        scan(T.SC[:, a:a + 68], T.GG[:, a:a + 68], T.BB[:, a:a + 68], 0.0, A.min, A.max, "GG%d BB%d" % (h, h), "SC%d" % h)
        yield
        cp(T.BL[:, 16 * q + 4 * h:16 * q + 4 * h + 4], T.SC[:, a + 16:a + 68:17], "SC%d" % h, "BL%d%d" % (q, h))
        yield

    def seat_sums(t, h):
        q, a = 4 * t + 3, 64 * h
        bl, bk = T.BL[:, 16 * q + 4 * h:16 * q + 4 * h + 4], "BL%d%d" % (q, h)
        bf, fk = T.SC[:, 68 * h + 16:68 * h + 68:17], "SC%d" % h
        cnt, pk, c4 = kk[h][:, 3, 0:12], "k%d" % h, slice(4 * h, 4 * h + 4)
        if h == 0:
            act(T.CDE[:, 0:64], T.BT[:].indirect(bl), AF.Copy, "BT EV " + bk, "CDE0", scale=EV)
        else:
            ts(T.CDE[:, 64:128], T.BT[:].indirect(bl), EV, A.mult, rd="BT EV " + bk, wr="CDE1")
        act(T.CDO[:, a:a + 64], T.BT[:].indirect(bl), AF.Copy, "BT OD " + bk, "CDO%d" % h, scale=OD)
        if t == VIS - 1 and h:
            seat_kin_of(t, 1)
        act(L["sq3"][:, c4], bf, AF.Square, fk, "sq3%d" % h, bias=-lo[t] - 63.5)
        for i in (0, 8):
            act(T.BN[:, h, i:i + 4], bf, AF.Copy, fk, "+BN%d" % h)
        act(T.PO[:, c4], L["sq3"][:, c4], AF.Relu, "sq3%d" % h, "PO%d" % h, scale=-64.0, bias=262144.0)
        act(T.XB[:, a:a + 64], T.X[:, 0:NW].indirect(bl), AF.Copy, "X XL " + bk, "XB%d" % h)
        for gr in range(8):
            r = 32 * (gr // 2)
            cd, ck = (T.CDE, "CDE") if gr % 2 == 0 else (T.CDO, "CDO")
            o = 16 * (gr % 2)
            mm(eq[gr // 2][:, c4, o:o + 16], cd[r:r + 32, :], cd[r:r + 32, a:a + 64], False, gr % 2 == 1,
               "%s0 %s1" % (ck, ck), "e%d" % (gr // 2))
        if t == VIS - 1 and h:
            parents(t)
        mm(cnt, T.IF[:], T.BN[:, h, 0:12], True, False, "IF BN%d" % h, pk)
        for i in (0, 4):
            mm(cnt[:, i:i + 4], T.IB[:], T.NL[:, c4], False, False, "IB NL", pk)
            mm(cnt[:, i:i + 4], T.IB[:], T.PO[:, c4], False, False, "IB PO%d" % h, pk)
        for i in ((2, 3) if h else range(4)):
            act(T.EQ[:, c4, 32 * i:32 * i + 32], eq[i][:, c4, :], AF.Relu, "", "EQ%d%d" % (h, i), "e%d" % i, bias=-12.0 + EPS)
        if h == 0:
            zsum(0)
            for i in range(4):
                order(1, i)
            seat_count(0)
            seat_z(t, 0)
            seat_kin_of(t, 0)

    def seat_kin_of(t, h):
        bl, bk = T.BL[:, 64 * t + 48 + 4 * h:64 * t + 52 + 4 * h], "BL%d%d" % (4 * t + 3, h)
        act(T.VK[:, h, 64:128], kwin().indirect(bl), AF.Copy, "KN " + bk, "VKb%d" % h)
        act(T.VK[:, h, 0:64], kwin().indirect(bl), AF.Copy, "KN NM0 " + bk, "VKa%d" % h, scale=NM0)

    def translate(t, h):
        if t in (1, 2):
            a = 256 * t + 64 * h
            cp(T.TT[:].indirect(T.L8[:, 4 * h:4 * h + 4]), T.VF[:, a:a + 64], "L8 VF%d" % h, "TT TTd")

    def zsum(h):
        a = 64 * h
        mm(dz[:, 128 + a:192 + a], T.IB[:], T.XB[:, a:a + 64], True, False, "IB XB%d" % h, "dz")
        mm(dz[:, 128 + a:192 + a], T.IB[:], T.ZR[:, 16 * a:16 * a + 1024:16], False, True, "IB ZR%d" % h, "dz")

    def parents(t):
        mm(eA[:, 0, :], T.B0[:], T.VK[:, :, 64:128], True, True, "B0 VKb0 VKb1", "eA")

    def seat_z(t, h):
        a = 128 * t + 64 * h
        act(T.ZQ[:, 64 * h:64 * h + 64], dz[:, 128 + 64 * h:192 + 64 * h], AF.Identity, "", "ZQ%d" % h, "dz", scale=0.4999, bias=M0C)
        act(T.VF[:, 128 * t + a:128 * t + a + 64], T.ID[:].indirect(T.BL[:, 64 * t + 48 + 4 * h:64 * t + 52 + 4 * h]), AF.Copy,
            "ID BL%d%d" % (4 * t + 3, h), "VF%d" % h)
        if t == VIS - 1:
            act(T.ZN[:, 64 * h:64 * h + 64], T.ZQ[:, 64 * h:64 * h + 64], AF.Identity, "ZQ%d" % h, "ZN%d" % h, bias=-M0C)
        else:
            m = 136 * t
            act(T.SND[:, m + 132 * h:m + 132 * h + 4], T.SC[:, 68 * h + 16:68 * h + 68:17], AF.Copy, "SC%d" % h, "SB%d" % h)
            act(T.SND[:, m + 4 + 64 * h:m + 68 + 64 * h], T.ZQ[:, 64 * h:64 * h + 64], AF.Identity, "ZQ%d" % h, "ZN%d" % h, bias=-M0C)
            send(nxt, T.LND[:, m + 68 * h:m + 68 * h + 68], T.SND[:, m + 68 * h:m + 68 * h + 68], "aZ%d%d" % (h, t), "ZN%d SB%d" % (h, h))
            arrives("aZ%d%d" % (h, t), "Z%d%d" % (t + 1, h))

    def seat_count(h):
        for c in range(4):
            mm(kk[h][:, 3, c:12:4], T.EQ[:, 4 * h + c, :], T.CW[:, 0:3], False, c == 3, "CW EQ%d0 EQ%d1 EQ%d2 EQ%d3" % (h, h, h, h), "k%d" % h)

    def seat_kin(t, h):
        tt(T.OF[:, h, 0:12], kk[h][:, 3, 0:12], T.DUM[:, h, 0:12], A.min, "DUM", "OF%d" % h, "k%d" % h)
        yield
        cp(T.LS[:, 8 * h:8 * h + 8], T.OF[:, h, 0:8], "OF%d" % h, "LS%d" % h)
        yield
        tt(kwin().indirect(T.LS[:, 8 * h:8 * h + 8]), T.VK[:, h, :], T.NR[:, 256 * t + 128 * h:256 * t + 128 * h + 128], A.add,
           "LS%d VKa%d VKb%d NR" % (h, h, h), "KN")
        yield

    def seat_feet(t):
        v, a = T.MS3[:, 15::16], lo[t]

        def spread():
            tt(T.FB[:], T.LB[:].indirect(T.C8[:]), D, A.mult, "LB C8 D", "FB")
            mm(eA[:, 3, :], T.BLK[:], T.FB[:], True, True, "BLK FB", "eA")

        if t < VIS - 1:
            spread()
            yield
        tt(T.MV[:], eA[:, 0, :], D, A.mult, "D", "MV", "eA")
        yield
        scan(T.MS3[:], RS, T.MV[:], 0.0, A.mult, A.add, "RS MV", "MS3")
        yield
        cp(T.VL[:], v, "MS3", "VL")
        tt(L["bov"], L["dum"], v, A.subtract, "MS3 dum", "bov")
        yield
        tt(T.MU2[:], fwin().indirect(T.VL[:]), D, A.mult, "FX FXa FXb VL D", "MU2")
        yield
        while seated[0] < t:
            yield
        scan(T.MS2[:], RS, T.MU2[:], 0.0, A.mult, A.add, "RS MU2", "MS2")
        tt(T.PK1[:, 0::2], L["bov"], T.SN[:], A.mult, "bov SN", "PK1a")
        if t == VIS - 1:
            spread()
        yield
        for i, _ in enumerate(place(T.BN[:, :, 0:4], "BN0 BN1", T.LN[:, 8:16], "LNb")):
            if i == 1:
                tt(T.FX[:, a:a + 128], eA[:, 3, :], T.FX[:, a:a + 128], A.min, "FX", "FX", "eA")
            yield
        cp(fwin().indirect(T.LN[:, 8:16]), T.VF[:, 256 * t + 128:256 * t + 256], "LNb VFr", "FX")
        yield

    def seat_rest(t):
        fin = t == VIS - 1
        a, m0 = lo[t], 16 * t
        zn, znk = T.ZN[:] if fin else T.SND[:, 136 * t + 4:136 * t + 132], "ZN0 ZN1"
        seated[0] = t
        ts(T.SN[:], T.OF[:, :, 0:4], float(NW), A.is_lt, -1.0, A.mult, rd="OF0 OF1", wr="SN")
        cp(T.LN[:, 0:8], T.OF[:, :, 4:8], "OF0 OF1", "LNa")
        ts(T.LB[:], T.OF[:, :, 0:4], M0C, A.add, M0C, A.subtract, rd="OF0 OF1", wr="LB")
        if not fin:
            mm(dz[:, 80:88], T.ONB[:], T.LIVE[:, 0:8], True, False, "ONB LIVE", "dz")
            mm(dz[:, 80:88], T.ONB[:], T.SN[:], False, True, "ONB SN", "dz")
            act(T.MS[:, m0:m0 + 8], T.OF[:, :, 8:12], AF.Copy, "OF0 OF1", "MS")
            act(L["aq"], dz[:, 80:88], AF.Copy, "", "AQ AS", "dz", accum_out=AS)
            act(T.MS[:, m0 + 8:m0 + 12], T.ONB[:, 0:4], AF.Copy, "ONB AS", "MSa", scale=AS)
            send(nxt, T.ML[:, m0:m0 + 16], T.MS[:, m0:m0 + 16], "aM%d" % t, "MS MSa")
            arrives("aM%d" % t, "ML%d" % t)
        yield
        translate(t, 1)
        if fin:
            act(T.OR[:], T.ID[:].indirect(T.CL[:, 8:16]), AF.Copy, "ID CB", "OR")
        yield
        yield
        cp(T.X[:].indirect(T.LN[:, 0:8]), zn, "LNa " + znk, "X XL Xt")
        if not fin:
            zrep(t + 1, 0)
            act(T.XW[:, a:a + 128], T.X[:, a:a + 128], AF.Copy, "X", "XW")
        yield
        if fin:
            yield
        if not fin:
            for _ in start(t + 1, 0):
                yield
            if t == 2:
                cp(T.L8[:], T.OF[:, :, 8:12], "OF0 OF1", "L8")
        else:
            cp(T.OT[:].indirect(T.L8[:]), T.OR[:], "L8 OR", "OT")

    def convert(i):
        a, z = KCH[i]
        cp(T.KN[:, a:z], T.KI[:, a:z], "KI%d" % i, "+KN")

    def converts():
        for i in range(1, len(KCH) - 1):
            yield
            yield
            convert(i)

    convert(0)
    lines[:] = [[out_before(0)], [converts()], [late()], [start(0, 0), start(0, 1)]]
    while lines[0] or lines[1]:
        pull()
    zrep(0, 0)
    zrep(0, 1)
    alive = live(0)
    lines[0:2] = [[out(0)], []]
    lines.append([alive])
    while any(lines[0:4]):
        pull()
    act(T.XB[:], T.XW[:].indirect(T.BL[:, 0:8]), AF.Copy, "XW BL00 BL01", "XB0 XB1 XWp")
    far(0)
    for t in range(VIS):
        fin = t == VIS - 1
        if fin:
            dma("Y", "early", T.yk[:], T.KN[:, NB:NW], rd="KN", wr="yk")
            dma("Y", "early", T.yx[:], T.X[:, NB:NW], rd="X", wr="yx")
        read.append("walk%d" % t)
        lines[:] = [([feet3] if t else []) + [out_feet(t)] + ([] if fin else [out_before(t + 1)]), [alive]]
        other = iter(())
        for i in range(2 * ST):
            sums(t, i // 2, i % 2, other)
            other = least(t, i // 2, i % 2)
            if i == 1:
                rows(t)
                for h in range(2):
                    act(T.BN[:, h, 4:8], T.J8[:, 4 * h:4 * h + 4], AF.Identity, "J8", "+BN%d" % h, bias=float(lo[t]))
        seat_sums(t, 0)
        if t in (1, 2):
            cp(T.L8[:], T.ML[:, 16 * (t - 1):16 * (t - 1) + 8], "ML%d" % (t - 1), "L8")
        first, second = seat_kin(t, 0), seat_kin(t, 1)
        for _ in other:
            pull()
        while fin and lines[0]:
            pull()
        if fin:
            send(prv, T.CL[:, 8:16], T.BL[:, 64 * t + 48:64 * t + 56], "aB", "BL%d0 BL%d1" % (4 * t + 3, 4 * t + 3))
            arrives("aB", "CB")
        seat_sums(t, 1)
        translate(t, 0)
        next(first)
        pull()
        next(first)
        pull()
        while not fin and lines[0] and t + 1 not in read:
            pull()
        if fin:
            lines[:] = [[seat_feet(t)]]
        zsum(1)
        seat_z(t, 1)
        for i in (0, 1):
            ts(T.EQ[:, 4:8, 32 * i:32 * i + 32], eq[i][:, 4:8, :], -12.0 + EPS, A.add, 0.0, A.max, wr="EQ1%d" % i, ps="e%d" % i)
        seat_count(1)
        if fin:
            pull()
        next(first)
        if not fin:
            seat_kin_of(t, 1)
            parents(t)
        pull()
        next(second)
        if fin:
            lines[1:] = [[second], [seat_rest(t)]]
        else:
            far(t + 1)
            feet3, alive = seat_feet(t), live(t + 1)
            lines[1:] = [[second, out(t + 1)], [seat_rest(t)], [alive]]
        while any(lines[0:3]):
            pull()
        if not fin:
            zrep(t + 1, 1)
        if t == 2:
            dma("Y", "tb", T.TB[:], T.TT[0::16, 0:NW], rd="TT", wr="TB")
            send(prv, T.TBL[:], T.TB[:], "aTB", "TB")
            arrives("aTB", "TBL")
            dma("Y", "ot", T.OT[0::16, 0:NW], T.TBL[:], rd="TBL", wr="OT")
    a = lo[VIS - 1]
    dma("Y", "out", T.yz[:], T.ZN[:], rd="ZN0 ZN1")
    dma("Y", "out", T.yp[:], T.KN[0::16, 0:NB], rd="KN")
    dma("S", "out", T.yk[:, a - NB:a - NB + 128], T.KN[:, a:a + 128], rd="KN", wr="yk")
    for u, z in ((NB, a), (a + 128, NW)):
        if z > u:
            dma("Y", "out", T.yk[0::16, u - NB:z - NB], T.KN[0::16, u:z], rd="KN", wr="yk")
    dma("Y", "out", T.yx[:, a - NB:a - NB + 128], T.X[:, a:a + 128], rd="X", wr="yx")
    dma("Y", "out", T.yt[:], T.OT[0::16, 0:NW], rd="OT")
    dma("S", "out", T.yf[:], T.FX[0::16, NB:NW], rd="FX")
    for s in list(tot):
        need("G", s, tot[s])
